import numpy as np, ml_dtypes
CORES = [6,15,38,47]
N = 4
import mx_ref
BF = ml_dtypes.bfloat16
def pick(q, e):
    c = np.concatenate([q[0].reshape(128, -1, 4), np.zeros((128, 1, 4), np.uint8)], axis=1); s = np.concatenate([q[1], np.ones((16, 1), np.uint8)], axis=1)
    return (np.ascontiguousarray(c[:, e].reshape(128, -1)), np.ascontiguousarray(s[:, e]))
def join(*qs):
    return (np.concatenate([q[0] for q in qs], axis=1), np.concatenate([q[1] for q in qs], axis=1))
def put(q, e, v):
    c, s = q[0].reshape(128, -1, 4).copy(), q[1].copy(); c[:, e] = v[0].reshape(128, -1, 4); s[:, e] = v[1]
    return (c.reshape(128, -1), s)
def pk(c, s):
    return (np.ascontiguousarray(c), mx_ref.live(s))
def emit(q):
    return q[0], q[1]
def cut(t, i, w=512):
    return t[:, w * i:w * i + w]
def f(rng, *shape):
    return mx_ref.flush((rng.standard_normal(shape, dtype=np.float32) * np.exp2(rng.integers(-2, 3, shape[:-1] + (1,)))).astype(BF))
def wide(rng, *shape, cols=0):
    v = rng.standard_normal(shape, dtype=np.float32) * np.exp2(rng.integers(-12, 13, shape)).astype(np.float32)
    if cols: v *= np.repeat(np.exp2(rng.integers(-cols, cols + 1, shape[:-2] + (1, shape[-1] // 4))) * (rng.random(shape[:-2] + (1, shape[-1] // 4)) > 0.0625), 4, axis=-1).astype(np.float32)
    return mx_ref.flush(v.astype(BF))
P, CAPP, O, L, S = 256, 80, 1, 2, 256
def plain(rng):
    v = np.array(f(rng, 128, 512))
    v[:, 4 * L:] = 0
    return {"x": f(rng, N, 128, 4 * P), "pl": np.stack([v] * N), "w": f(rng, N, 128, 512 * O)}
def sized(rng, *shape):
    return (1 + rng.random(shape)) * rng.choice([-1.0, 1.0], shape)
def planes(rng):
    v = np.zeros((128, 128, 4))
    for b in range(L): v[8 * b:8 * b + 8, b] = sized(rng, 8, 4)
    return np.stack([v.reshape(128, 512)] * N).astype(np.float32).astype(BF)
def aim(v, t, pl):
    for b in range(L):
        g = np.sign(pl[0].astype(np.float32).reshape(128, 128, 4)[8 * b:8 * b + 8, b])
        v[:, 8 * b:8 * b + 8] = np.abs(v[:, 8 * b:8 * b + 8]) * g[None, :, None, :] * (1 - 2 * (t >> b & 1))[:, None, :, None]
    return v.reshape(N, 128, 4 * P).astype(np.float32).astype(BF)
def setup_inputs(rng):
    d = plain(rng)
    v = d["x"].astype(np.float32).reshape(N, 128, P, 4).transpose(1, 0, 2, 3).reshape(128, N * P, 4)
    e, n = rng.permutation(N * P), N * P // 4
    near, of = e[:n], rng.choice(e[n:], n)
    size, change = np.exp2(rng.integers(-1, 2, (n, 1))), rng.choice([0.0, 0.0625, 0.25, 0.5], (n, 1))
    v[:, near] = v[:, of] * size * (1 + change * rng.standard_normal((128, n, 4)))
    d["x"] = mx_ref.flush(v.reshape(128, N, P, 4).transpose(1, 0, 2, 3).reshape(N, 128, 4 * P).astype(BF))
    return d
def setup_inputs_same(rng):
    d, first = plain(rng), rng.permutation(N)
    if first[0] == 0: first[0], first[1] = int(first[1]), int(first[0])
    d["pl"], u = planes(rng), sized(rng, 128, N, 4)
    t = np.stack([rng.permutation(np.flatnonzero(first <= s)[np.arange(P) % (s + 1)]) for s in range(N)])
    v = np.stack([u[:, t[s]] for s in range(N)])
    v[first[0]][:, np.flatnonzero(t[first[0]] == 0)[::2]] = 0
    d["x"] = aim(v, t, d["pl"])
    return d
def setup_inputs_full(rng):
    d, h, r = plain(rng), rng.permutation(N), rng.permutation(N)
    n = rng.integers(CAPP + 1, 2 * CAPP + 1, N)
    n[r[0]] = CAPP
    n[r[1]] = P
    t = np.stack([rng.permutation(np.concatenate([np.full(n[s], h[0]), rng.choice(h[2:], P - n[s])])) for s in range(N)])
    d["pl"] = planes(rng)
    d["x"] = aim(sized(rng, N, 128, P, 4), t, d["pl"])
    return d
def setup_inputs_edge(rng):
    d, n = plain(rng), N * P // 4
    o = np.stack([s * P + rng.permutation(P) for s in range(N)]).reshape(N, P // 4, 4)
    m = np.sort(np.concatenate([rng.permutation(o[:, k].reshape(-1)).reshape(N, 4) for k in range(P // 4)]), axis=1)
    v = np.repeat(rng.choice([-1.0, 1.0], (n, 1, 512)), 4, axis=1)
    e, k = 32 * L + np.argsort(rng.random((n, 512 - 32 * L)), axis=1)[:, :49], np.arange(n)[:, None]
    v[k, 1, e[:, :16]] *= -1
    v[k, 2, e[:, :32]] *= -1
    v[k, 3, e[:, 32:]] *= -1
    x, t = np.zeros((N * P, 512)), np.zeros(N * P, int)
    x[m] = v * np.exp2(rng.integers(0, 2, (n, 1, 1)))
    x[m[0, 3]] = 0
    t[m] = np.repeat(np.arange(P // 4) % N, N)[:, None]
    d["pl"] = planes(rng)
    d["x"] = aim(np.ascontiguousarray(x.reshape(N, P, 128, 4).transpose(0, 2, 1, 3)), t.reshape(N, P), d["pl"])
    return d
def setup_inputs_deal(rng):
    d, t = plain(rng), []
    c = np.ones(N, int)
    c[0], c[N - 1] = 2, 0
    for s in range(N):
        a = np.bincount(rng.permutation(np.repeat(np.arange(N), (CAPP - c[s]) // N))[:P // N - c[s]], minlength=N)
        t.append(rng.permutation(np.repeat(np.arange(N), N * a + c[s])))
    d["pl"] = planes(rng)
    d["x"] = aim(sized(rng, N, 128, P, 4), np.stack(t), d["pl"])
    return d
def setup_inputs_spread(rng):
    d, x = plain(rng), np.array(wide(rng, N, 128, 4 * P, cols=6))
    x[0, :, :4] = -0.0
    d["pl"][:, :, :4] = np.abs(d["pl"][:, :, :4])
    return {**d, "x": x}
def check_inputs(d):
    b = []
    for k in ("x", "pl", "w"):
        v = np.abs(d[k].astype(np.float32))
        if not (np.isfinite(v).all() and ((v == 0) | (v >= 2.0 ** -30) & (v <= 2.0 ** 30)).all()): b.append("a value of " + k)
    v = d["pl"].astype(np.float32)
    if (v[:, :, 4 * L:] != 0).any(): b.append("pl has numbers behind its first L columns")
    if (v != v[:1]).any(): b.append("pl differs between ranks")
    return b
def reference(x, pl, w):
    q = [mx_ref.quantize(np.ascontiguousarray(x[s])) for s in range(N)]
    every = join(*q)
    bucket = []
    for s in range(N):
        z = mx_ref.matmul(mx_ref.quantize(np.ascontiguousarray(pl[s])), q[s])
        bucket.append(sum((z[b] < 0) * 2 ** b for b in range(L)))
    alive = []
    for d in range(N):
        e = np.concatenate([P * s + np.flatnonzero(bucket[s] == d)[:CAPP] for s in range(N)])
        if e.size == 0: continue
        at = np.concatenate([e, np.full(-e.size % 128, -1)])
        m = np.concatenate([mx_ref.matmul(pick(every, at[i:i + 128]), pick(every, at)) for i in range(0, at.size, 128)])
        falls = np.triu(m >= np.float32(0.9375) * np.diagonal(m), 1).any(axis=0)
        alive.append(e[~falls[:e.size]])
    alive = np.concatenate(alive)
    oc, osc = np.zeros((N, 128, 4 * S), np.uint8), np.zeros((N, 16, S), np.uint8)
    num, y = np.zeros((N, 1, S), np.float32), np.zeros((N, 128, O * S), np.float32)
    for r in range(N):
        e = alive[r::N]
        e = np.concatenate([e, np.full(S - e.size, -1)])
        v = pick(every, e)
        oc[r], osc[r] = emit(v)
        num[r, 0] = e
        for o in range(O): y[r, :, o * S:o * S + S] = mx_ref.matmul(mx_ref.quantize(np.ascontiguousarray(cut(w[r], o))), v)
    return {"oc": oc, "osc": osc, "num": num, "y": y}

@@ -1,0 +1,376 @@
+from concourse.bass import DstId, RemoteDMATransfer
+from concourse.mybir import dt, AluOpType, AxisListType, ActivationFunctionType
+
+N, P, CAPP = 4, 256, 80
+S1 = N * CAPP
+C5 = CAPP // 16
+BIG = 1.0e29
+TINY = 1.0e-36
+
+CODE = "float8_e4m3fn_x4"
+SCRATCH = {
+    "xt": ("sbuf", [128, 4 * P + 8], "bfloat16"),
+    "plt": ("sbuf", [128, 512], "bfloat16"),
+    "wt": ("sbuf", [128, 512], "bfloat16"),
+    "xq": ("sbuf", [128, P + 2], CODE), "xs": ("sbuf", [128, P + 2], "uint8"),
+    "plq": ("sbuf", [128, 128], CODE), "pls": ("sbuf", [128, 128], "uint8"),
+    "prq": ("sbuf", [128, 256], CODE), "prs": ("sbuf", [128, 256], "uint8"),
+    "wq": ("sbuf", [128, 128], CODE), "ws": ("sbuf", [128, 128], "uint8"),
+    "s1q": ("sbuf", [128, 272], CODE), "s1s": ("sbuf", [128, 272], "uint8"),
+    "l1q": ("sbuf", [128, S1 + 8], CODE), "l1s": ("sbuf", [128, S1 + 8], "uint8"),
+    "s2q": ("sbuf", [128, 240], CODE), "s2s": ("sbuf", [128, 240], "uint8"),
+    "l2q": ("sbuf", [128, S1 + 8], CODE), "l2s": ("sbuf", [128, S1 + 8], "uint8"),
+    "oq": ("sbuf", [128, P], CODE), "os_": ("sbuf", [128, P], "uint8"),
+    "ploff": ("sbuf", [128, 16], "uint16"),
+    "pn": ("sbuf", [128, 1], "int32"), "pm16": ("sbuf", [128, 1], "int32"), "ph5": ("sbuf", [128, 1], "int32"),
+    "r16": ("sbuf", [128, 1], "float32"), "q5": ("sbuf", [128, 1], "float32"),
+    "io16": ("sbuf", [128, 16], "float32"), "b16": ("sbuf", [128, 16], "float32"), "b16h": ("sbuf", [128, 8], "float32"),
+    "qb2": ("sbuf", [128, 5], "float32"), "qb2h": ("sbuf", [128, 5], "float32"), "sb8": ("sbuf", [128, 2], "float32"),
+    "sg": ("sbuf", [128, 4], "float32"),
+    "neg1": ("sbuf", [128, 128], "float32"), "idm": ("sbuf", [128, 128], "float32"),
+    "zf": ("sbuf", [128, S1], "float32"), "negw": ("sbuf", [128, S1], "float32"),
+    "nega": ("sbuf", [128, 128], "float32"), "neg0": ("sbuf", [128, 128], "float32"),
+    "one": ("sbuf", [128, 24], "float32"), "mka": ("sbuf", [128, 24], "float32"), "mk": ("sbuf", [128, 24], "float32"),
+    "mo": ("sbuf", [128, 4], "float32"),
+    "zb": ("sbuf", [128, S1], "bfloat16"),
+    "s0": ("sbuf", [128, P], "bfloat16"), "t1": ("sbuf", [128, P], "bfloat16"), "ind": ("sbuf", [128, P], "bfloat16"),
+    "c1": ("sbuf", [128, P], "bfloat16"), "jv": ("sbuf", [128, 2 * P], "bfloat16"), "ja": ("sbuf", [128, 3 * P], "bfloat16"),
+    "ac": ("sbuf", [128, 4], "float32"), "lq": ("sbuf", [128, 8], "float32"), "lw": ("sbuf", [128, 24], "float32"),
+    "off1": ("sbuf", [128, 24], "uint16"),
+    "tm": ("sbuf", [128, 24], "float32"), "rn": ("sbuf", [128, 4], "float32"),
+    "m1s": ("sbuf", [128, 8], "uint16"), "m1l": ("sbuf", [128, 32], "uint16"),
+    "db": ("sbuf", [128, 384], "float32"), "mb0": ("sbuf", [128, 128], "float32"), "mb1": ("sbuf", [128, 256], "float32"),
+    "mb2": ("sbuf", [128, S1], "float32"), "nt": ("sbuf", [128, 4], "float32"), "acc": ("sbuf", [128, 4], "float32"),
+    "jf": ("sbuf", [128, 704], "bfloat16"),
+    "cn1": ("sbuf", [128, 4], "float32"), "ce": ("sbuf", [128, 8], "float32"), "fi": ("sbuf", [128, 4], "float32"),
+    "fo": ("sbuf", [128, 4], "float32"), "ov": ("sbuf", [128, 2], "float32"), "ev": ("sbuf", [128, 4], "float32"),
+    "bb": ("sbuf", [128, 32], "bfloat16"), "bt": ("sbuf", [128, 32], "bfloat16"), "rw": ("sbuf", [128, 128], "bfloat16"),
+    "uu": ("sbuf", [128, 128], "bfloat16"), "d0": ("sbuf", [128, S1], "bfloat16"), "d1": ("sbuf", [128, S1], "bfloat16"),
+    "c2": ("sbuf", [128, S1], "float32"), "cn2": ("sbuf", [128, 16], "float32"),
+    "jv2": ("sbuf", [128, 2 * S1], "bfloat16"), "ja2": ("sbuf", [128, 3 * S1], "bfloat16"),
+    "ac2": ("sbuf", [128, 4], "float32"), "l2": ("sbuf", [128, 8], "float32"), "lst": ("sbuf", [128, 32], "float32"),
+    "gs": ("sbuf", [128, 8], "float32"), "ei": ("sbuf", [128, 2], "int32"), "seli": ("sbuf", [128, 2], "int32"),
+    "sel": ("sbuf", [128, 2], "uint16"), "off2": ("sbuf", [128, 32], "uint16"),
+    "ai": ("sbuf", [128, 4], "int32"), "aj": ("sbuf", [128, 4], "int32"), "a5": ("sbuf", [128, 8], "float32"),
+    "wd": ("sbuf", [128, 4], "float32"), "we": ("sbuf", [128, 4], "float32"), "tp": ("sbuf", [128, 64], "float32"),
+    "ta": ("sbuf", [128, 64], "float32"), "fin": ("sbuf", [128, 16], "uint16"),
+    "yb": ("sbuf", [128, P], "float32"),
+    "nr16": ("sbuf", [1, S1], "uint16"), "nr": ("sbuf", [128, S1 + 8], "float32"), "ng": ("sbuf", [128, 384], "float32"),
+    "ngt": ("sbuf", [32, 384], "float32"), "v2s": ("sbuf", [128, 4], "uint16"), "v2l": ("sbuf", [128, 32], "uint16"),
+    "xn": ("sbuf", [128, 128], "float32"), "xnt": ("sbuf", [128, 128], "float32"), "nw": ("sbuf", [128, S1 + 8], "float32"),
+    "nout": ("sbuf", [128, P], "float32"),
+    "pz": ("psum", [128, 1024], "float32"), "pmm": ("psum", [128, 1536], "float32"), "py": ("psum", [128, 1024], "float32"),
+}
+SEMAPHORES = ["vs", "sa", "ts", "gc", "dpl", "dx0", "dx1", "dw", "dz", "dn", "so", "sp", "ls", "a1", "m1r", "a2", "a3", "m2r"]
+
+
+def share(topo, src, dsts):
+    el = topo.engines(src, dsts[0])
+    for d in dsts[1:]:
+        el = [e for e in el if e in topo.engines(src, d)]
+    q = len(el) // 4
+    part = [el[i * q:(i + 1) * q] for i in range(4)]
+
+    def far(d):
+        a, b = topo.chip(src), topo.chip(d)
+        return not topo.mates(a, b) and not topo.same_plane(a, b)
+    lead = [d for d in dsts if far(d)] or [dsts[-1]]
+    lead = lead[0]
+    rest = [d for d in dsts if d != lead]
+    return {lead: (part[2] + part[3], part[0] + part[1]), rest[0]: (part[0], part[2]), rest[1]: (part[1], part[3])}
+
+
+def bits(es):
+    m = 0
+    for e in es:
+        m |= 1 << e
+    return m
+
+
+def rank_program(g, core, T, topo):
+    me = T.rank_of(core)
+    if me is None:
+        return
+    A, F, X = AluOpType, ActivationFunctionType, AxisListType.X
+    u8, u32 = dt.uint8, dt.uint32
+    eng = {"v": g.vector, "a": g.scalar, "t": g.tensor, "g": g, "s": g.sync}
+    own_sem = {"v": "vs", "a": "sa", "t": "ts", "g": "gc"}
+    count, seen = {}, {}
+
+    def wait(q, deps):
+        need = {}
+        for s, v in deps:
+            need[s] = max(v, need.get(s, 0))
+        for s, v in need.items():
+            if seen.get((q, s), 0) < v:
+                eng[q].wait_ge(T.sem[s], v)
+                seen[(q, s)] = v
+
+    def op(q, deps, name, *args, **kw):
+        wait(q, deps)
+        e = eng[q]
+        calls = {"copy": g.vector.tensor_copy, "tt": g.vector.tensor_tensor, "ts": g.vector.tensor_scalar,
+                 "red": g.vector.tensor_reduce, "scan": g.vector.tensor_tensor_scan, "tr": g.vector.transpose,
+                 "set": g.vector.memset, "qmx": g.vector.quantize_mx, "act": g.scalar.activation,
+                 "mm": g.tensor.matmul_mx, "iota": g.iota, "aff": g.affine_select, "bc": g.partition_broadcast}
+        s = own_sem[q]
+        calls[name](*args, **kw).then_inc(T.sem[s], 1)
+        count[s] = count.get(s, 0) + 1
+        return (s, count[s])
+
+    def dma(q, deps, s, out, in_):
+        wait(q, deps)
+        eng[q].dma_start(out, in_).then_inc(T.sem[s], 16)
+        count[s] = count.get(s, 0) + 16
+        return (s, count[s])
+
+    order = [(me + 1 + x) % N for x in range(N)]
+    peers = [T.cores[r] for r in order[:3]]
+    mine = share(topo, core, peers)
+    into = {"c": 0, "p": 0}
+    for r in range(N):
+        if r != me:
+            sh = share(topo, T.cores[r], [T.cores[(r + 1 + x) % N] for x in range(3)])[core]
+            into["c"] += len(sh[0])
+            into["p"] += len(sh[1])
+
+    def send(deps, sem, kind, pieces):
+        wait("g", deps)
+        tr = []
+        for d, (src, dst) in zip(peers, pieces):
+            rid, pid = topo.addr(d)[:2]
+            es = mine[d][0 if kind == "c" else 1]
+            tr.append(RemoteDMATransfer(dst_ids=[DstId(rid=rid, pnc=pid)], dma_engine_mask=bits(es),
+                                        remote_sem=T.sem[sem], src=src, dst=dst))
+            count["ls"] = count.get("ls", 0) + len(es)
+        g.remote_dma_fused(tr, local_sem=T.sem.ls)
+
+    tpl = dma("s", [], "dpl", T.plt[:], T.pl[:])
+    tx1 = dma("a", [], "dx1", T.xt[:, 512:1024], T.x[:, 512:1024])
+    tx0 = dma("s", [], "dx0", T.xt[:, 0:512], T.x[:, 0:512])
+    tw = dma("s", [], "dw", T.wt[:], T.w[:])
+
+    k = op("v", [], "set", T.ploff[:, 0:8], 0)
+    tpo = op("v", [], "set", T.ploff[:, 8:16], 1)
+    tz4 = op("v", [], "set", T.xt[:, 4 * P:4 * P + 8], 0.0)
+    for qd in range(4):
+        b = qd & 1
+        op("v", [], "set", T.sg[32 * qd:32 * qd + 32, 0:1], -1.0 if b else 1.0)
+        op("v", [], "set", T.sg[32 * qd:32 * qd + 32, 1:2], -TINY if b else TINY)
+    op("v", [], "set", T.sg[0:64, 2:3], 0.0)
+    tsg = op("v", [], "set", T.sg[64:128, 2:3], 1.0)
+    tzb = op("v", [], "set", T.zb[:], 0.0)
+    tpn = op("g", [], "iota", T.pn[:], [[0, 1]], 0, 1)
+    tio = op("g", [], "iota", T.io16[:], [[16, 16]], 0, 1, allow_small_or_imprecise_dtypes=True)
+    tzf = op("v", [], "set", T.zf[:], 0.0)
+    tn1 = op("v", [], "set", T.neg1[:], -0.9375)
+    ton = op("v", [], "set", T.one[:], 1.0)
+    a = op("v", [tpn], "ts", T.pm16[:], T.pn[:], 112, None, A.bitwise_and)
+    b = op("v", [tpn], "ts", T.ph5[:], T.pn[:], 5, None, A.logical_shift_right)
+    a = op("v", [a], "copy", T.r16[:], T.pm16[:])
+    tq5 = op("v", [b], "copy", T.q5[:], T.ph5[:])
+    tb16 = op("v", [a, tio], "ts", T.b16[:], T.io16[:], T.r16[:, 0:1], None, A.subtract)
+    tb16h = op("v", [tb16], "ts", T.b16h[:], T.b16[:, 0:8], 0.5, None, A.add)
+    tid = op("g", [tn1], "aff", T.idm[:], T.neg1[:], [[-1, 128]], A.is_equal, 0.0, 0, 1)
+    tnw = op("g", [tzf], "aff", T.negw[:], T.zf[:], [[-1, S1]], A.is_gt, -BIG, 192, 1)
+    a = op("g", [tzf], "aff", T.nega[:], T.zf[:, 0:128], [[-1, 128]], A.is_gt, -BIG, 0, 1)
+    tn0 = op("g", [a], "aff", T.neg0[:], T.nega[:], [[1, 128]], A.is_gt, BIG, 0, 1)
+    a = op("g", [ton], "aff", T.mka[:], T.one[:], [[0, 4], [-16, 6]], A.is_ge, 0.0, 0, 1)
+    tmk = op("g", [a], "aff", T.mk[:], T.mka[:], [[0, 4], [16, 6]], A.is_ge, 0.0, 15, -1)
+    op("g", [ton], "aff", T.mo[:, 0:2], T.one[:, 0:2], [[-CAPP, 2]], A.is_equal, 0.0, 0, 1)
+    tmo = op("g", [ton], "aff", T.mo[:, 2:4], T.one[:, 0:2], [[-CAPP, 2]], A.is_equal, 0.0, 128 - 2 * CAPP, 1)
+
+    tplq = op("v", [tpl], "qmx", T.plq[:], T.pls[:], T.plt[:])
+    tprq = op("v", [tplq, tpo], "copy", T.prq[:].bitcast(u32), T.plq[:].bitcast(u32).indirect(T.ploff[:]))
+    tprs = op("a", [tplq, tpo], "act", T.prs[:], T.pls[:].indirect(T.ploff[:]), F.Copy)
+    tq0 = op("v", [tx0], "qmx", T.xq[:, 0:128], T.xs[:, 0:128], T.xt[:, 0:512])
+    tq1 = op("v", [tx1, tz4], "qmx", T.xq[:, 128:P + 2], T.xs[:, 128:P + 2], T.xt[:, 512:4 * P + 8])
+    tq = [tq0, tq1]
+    for d in ("l1", "l2"):
+        dma("s", tq, "dz", T[d + "q"][:, S1:S1 + 2].bitcast(u8), T.xq[:, P:P + 2].bitcast(u8))
+        tdz = dma("s", tq, "dz", T[d + "s"][:, S1:S1 + 2], T.xs[:, P:P + 2])
+    tz0 = op("t", [tprq, tprs] + tq, "mm", T.pz[:, 0:P], T.prq[:, 0:128], T.prs[:, 0:128], T.xq[:, 0:P], T.xs[:, 0:P], True, True)
+    tz1 = op("t", [], "mm", T.pz[:, 512:512 + P], T.prq[:, 128:256], T.prs[:, 128:256], T.xq[:, 0:P], T.xs[:, 0:P], True, True)
+
+    ts0 = op("a", [tz0, tsg], "act", T.s0[:], T.pz[:, 0:P], F.Sign, bias=T.sg[:, 1:2], scale=T.sg[:, 0:1])
+    tt1 = op("v", [tz1, tsg], "ts", T.t1[:], T.pz[:, 512:512 + P], 0.0, T.sg[:, 2:3], A.is_lt, A.is_equal)
+    a = op("v", [ts0, tt1], "tt", T.ind[:], T.s0[:], T.t1[:], A.is_equal)
+    tc = op("v", [a, tzb], "scan", T.c1[:], T.ind[:], T.zb[:, 0:P], 0.0, A.add, A.add)
+    for m in range(3):
+        tac = op("a", [tc, tb16h], "act", T.ja[:, P * m:P * m + P], T.c1[:], F.Sign, bias=T.b16h[:, m:m + 1], scale=-1.0,
+                 accum_out=T.ac[:, m:m + 1])
+    j3 = op("v", [tc, tb16], "ts", T.jv[:, 0:P], T.c1[:], T.b16[:, 3:4], None, A.is_le)
+    j4 = op("v", [tc], "ts", T.jv[:, P:2 * P], T.c1[:], T.b16[:, 4:5], None, A.is_le)
+    op("v", [tc], "ts", T.lq[:, 5:6], T.c1[:, P - 1:P], 0.5, None, A.is_gt)
+    op("v", [j3], "red", T.lq[:, 3:4], T.jv[:, 0:P], X, A.add)
+    op("v", [j4], "red", T.lq[:, 4:5], T.jv[:, P:2 * P], X, A.add)
+    tl = op("v", [tac], "ts", T.lq[:, 0:3], T.ac[:, 0:3], 0.5, P / 2.0, A.mult, A.add)
+    for x in range(4):
+        d = order[x]
+        for qd in range(4):
+            out, src = T.lw[32 * qd:32 * qd + 32, 6 * x:6 * x + 6], T.lq[32 * d:32 * d + 32, 0:6]
+            if qd < 2:
+                tv = op("v", [tl], "copy", out, src)
+            else:
+                ta = op("a", [tl], "act", out, src, F.Copy)
+    tlw = [tv, ta]
+    toff = op("v", tlw, "copy", T.off1[:], T.lw[:])
+    tpc = op("v", [toff] + tq, "copy", T.s1q[:, 0:272].bitcast(u32), T.xq[:, 0:P + 2].bitcast(u32).indirect(T.off1[:, 0:17]))
+    tps = op("a", [toff] + tq, "act", T.s1s[:, 0:272], T.xs[:, 0:P + 2].indirect(T.off1[:, 0:17]), F.Copy)
+    o0 = CAPP * me
+    toc = op("v", [], "copy", T.l1q[:, o0:o0 + CAPP].bitcast(u32), T.xq[:, 0:P + 2].bitcast(u32).indirect(T.off1[:, 18:18 + C5]))
+    tos = op("a", [], "act", T.l1s[:, o0:o0 + CAPP], T.xs[:, 0:P + 2].indirect(T.off1[:, 18:18 + C5]), F.Copy)
+    send([tpc], "a1", "c", [(T.s1q[:, 96 * x:96 * x + CAPP].bitcast(u8), T.l1q[:, o0:o0 + CAPP].bitcast(u8)) for x in range(3)])
+    send([tps], "a1", "p", [(T.s1s[:, 96 * x:96 * x + CAPP], T.l1s[:, o0:o0 + CAPP]) for x in range(3)])
+    a = op("v", [tmk], "tt", T.tm[:], T.lw[:], T.mk[:], A.mult)
+    for x in range(4):
+        b = op("v", [a], "red", T.rn[:, x:x + 1], T.tm[:, 6 * x:6 * x + 6], X, A.add)
+    op("v", [b], "ts", T.m1s[:, 0:8:2], T.rn[:], float(P * me), None, A.add)
+    tm1 = op("v", [], "copy", T.m1s[:, 1:8:2], T.lw[:, 5:24:6])
+    send([tm1], "m1r", "c", [(T.m1s[:, 2 * x:2 * x + 2], T.m1l[:, 8 * me:8 * me + 2]) for x in range(3)])
+    tm1o = op("v", [tm1], "copy", T.m1l[:, 8 * me:8 * me + 2], T.m1s[:, 6:8])
+    am1 = ("m1r", into["c"])
+    for s in range(N):
+        tdn = dma("s", [am1, tm1o], "dn", T.nr16[0:1, CAPP * s:CAPP * s + CAPP], T.m1l[0:CAPP, 8 * s:8 * s + 1])
+
+    twq = op("v", [tw], "qmx", T.wq[:], T.ws[:], T.wt[:])
+    op("v", [tb16, tq5], "ts", T.qb2[:], T.b16[:, 0:5], 4.0, T.q5[:, 0:1], A.mult, A.add)
+    a = ("vs", count["vs"])
+    tq2 = op("v", [a], "ts", T.qb2h[:], T.qb2[:], 0.5, None, A.add)
+    tsb8 = op("v", [], "ts", T.sb8[:], T.b16[:, 0:2], float(8 * (me + 1) + 8192), 0.125, A.add, A.mult)
+    td1 = op("v", [], "set", T.d1[:, 128:S1], 0.0)
+    op("v", [], "set", T.ce[:], 0.0)
+    op("v", [], "set", T.gs[:], 0.0)
+    op("v", [], "set", T.a5[:], 0.0)
+    op("v", [], "set", T.l2[:, 5:8], 0.0)
+    op("v", [], "set", T.v2s[:], 0)
+    op("v", [], "set", T.v2l[:, 8 * me:8 * me + 8], 0)
+    op("v", [], "set", T.xn[:], 0.0)
+    op("v", [], "set", T.nr[:], 0.0)
+    tset = op("v", [], "set", T.nw[:], -1.0)
+
+    aa1 = ("a1", into["c"] + into["p"])
+    blocks = {0: (0, 128, T.mb0, T.neg0[:], 0, 0), 1: (128, 256, T.mb1, T.negw[:, 64:S1], 512, 128), 2: (192, S1, T.mb2, T.negw[:], 1024, 384)}
+    tmm = {}
+    for b in (1, 2, 0):
+        k0, n, mb, ng, c0, jc = blocks[b]
+        tmm[b] = op("t", [aa1, toc, tos], "mm", T.pmm[:, c0:c0 + n], T.l1q[:, k0:k0 + 128], T.l1s[:, k0:k0 + 128],
+                    T.l1q[:, 0:n], T.l1s[:, 0:n], True, True)
+    tacc = {}
+    for b in (1, 2, 0):
+        k0, n, mb, ng, c0, jc = blocks[b]
+        a = op("v", [tmm[b], tid], "tt", T.db[:, 128 * b:128 * b + 128], T.pmm[:, c0 + k0:c0 + k0 + 128], T.idm[:], A.mult)
+        c = op("v", [tnw, tn0], "tt", mb[:], T.pmm[:, c0:c0 + n], ng, A.add)
+        a = op("v", [a], "red", T.nt[:, b:b + 1], T.db[:, 128 * b:128 * b + 128], X, A.add)
+        tacc[b] = op("a", [a, c], "act", T.jf[:, jc:jc + n], mb[:], F.Sign, bias=T.nt[:, b:b + 1], accum_out=T.acc[:, b:b + 1])
+    a = op("v", [am1, tm1o], "copy", T.cn1[:], T.m1l[:, 1:32:8])
+    a = op("v", [a, tset], "scan", T.ce[:, 1:5], T.cn1[:], T.zf[:, 0:4], 0.0, A.add, A.add)
+    a = op("v", [a], "tt", T.fi[:], T.cn1[:], T.ce[:, 0:4], A.is_gt)
+    a = op("v", [a, tmo], "tt", T.fo[:], T.fi[:], T.mo[:], A.mult)
+    tov = op("v", [a], "tt", T.ov[:], T.fo[:, 0:4:2], T.fo[:, 1:4:2], A.add)
+    op("v", [tacc[2]], "ts", T.ev[:, 2:3], T.acc[:, 2:3], 0.5 - S1, 4.0, A.is_le, A.mult)
+    a = op("v", [tacc[1], tov], "ts", T.ev[:, 1:2], T.acc[:, 1:2], 0.5 - 256, T.ov[:, 1:2], A.is_le, A.max)
+    b = op("v", [tacc[0], tov], "ts", T.ev[:, 0:1], T.acc[:, 0:1], 0.5 - 128, T.ov[:, 0:1], A.is_le, A.max)
+    a = op("v", [a], "ts", T.ev[:, 3:4], T.ev[:, 1:2], 2.0, T.ev[:, 2:3], A.mult, A.add)
+    a = op("v", [a, b], "ts", T.bb[:], T.zb[:, 0:32], T.ev[:, 0:1], T.ev[:, 3:4], A.add, A.add)
+    tbt = op("v", [a], "tr", T.bt[:], T.bb[:])
+    tb = op("g", [tbt], "bc", T.rw[:, 96:128], T.bt[96:97, 0:32], 128)
+    for i in range(3):
+        for qd in range(4):
+            out, src = T.rw[32 * qd:32 * qd + 32, 32 * i:32 * i + 32], T.bt[32 * i:32 * i + 32, 0:32]
+            if qd < 2:
+                tv = op("v", [tbt], "copy", out, src)
+            else:
+                ta = op("a", [tbt], "act", out, src, F.Copy)
+    trw = [tb, tv, ta]
+    a = op("v", trw, "ts", T.uu[:], T.rw[:], 4.0, -4.0, A.is_ge, A.mult)
+    op("v", [], "ts", T.d0[:, 256:S1], T.rw[:, 64:128], 4.0, None, A.is_ge)
+    a = op("v", [a], "tt", T.d0[:, 0:128], T.rw[:], T.uu[:], A.add)
+    op("v", [a], "ts", T.d0[:, 128:256], T.d0[:, 0:128], 2.0, None, A.is_ge)
+    a = op("v", [a], "ts", T.d1[:, 0:128], T.d0[:, 0:128], 2.0, -2.0, A.is_ge, A.mult)
+    tc2 = op("v", [a, td1], "scan", T.c2[:], T.d0[:], T.d1[:], 0.0, A.add, A.add)
+    send([tc2], "a2", "c", [(T.c2[:, S1 - 1:S1], T.cn2[:, 4 * me:4 * me + 1])] * 3)
+    aa2 = ("a2", into["c"])
+
+    for m in range(3):
+        tac = op("a", [tc2, tq2], "act", T.ja2[:, S1 * m:S1 * m + S1], T.c2[:], F.Sign, bias=T.qb2h[:, m:m + 1], scale=-1.0,
+                 accum_out=T.ac2[:, m:m + 1])
+    j3 = op("v", [tc2, tq2], "ts", T.jv2[:, 0:S1], T.c2[:], T.qb2[:, 3:4], None, A.is_le)
+    j4 = op("v", [], "ts", T.jv2[:, S1:2 * S1], T.c2[:], T.qb2[:, 4:5], None, A.is_le)
+    tcn = op("v", [], "copy", T.cn2[:, 4 * me:4 * me + 1], T.c2[:, S1 - 1:S1])
+    op("v", [j3], "red", T.l2[:, 3:4], T.jv2[:, 0:S1], X, A.add)
+    op("v", [j4], "red", T.l2[:, 4:5], T.jv2[:, S1:2 * S1], X, A.add)
+    tl = op("v", [tac], "ts", T.l2[:, 0:3], T.ac2[:, 0:3], 0.5, S1 / 2.0, A.mult, A.add)
+    for e in range(4):
+        for qd in range(4):
+            out, src = T.lst[32 * qd:32 * qd + 32, 8 * e:8 * e + 8], T.l2[32 * e:32 * e + 32, 0:8]
+            if qd < 2:
+                tv = op("v", [tl], "copy", out, src)
+            else:
+                ta = op("a", [tl], "act", out, src, F.Copy)
+    tlst = [tv, ta]
+    tnr = op("v", [tdn, tset], "copy", T.nr[0:1, 0:S1], T.nr16[0:1, 0:S1])
+
+    def places():
+        return op("v", [aa2, tcn], "scan", T.gs[:, 1:5], T.cn2[:, 0:16:4], T.zf[:, 0:4], 0.0, A.add, A.add)
+    if me == 0:
+        a = op("v", [tsb8], "ts", T.ei[:], T.sb8[:], 0.0, 8.0, A.subtract, A.mult)
+    else:
+        tgs = places()
+        a = op("v", [tgs, tsb8], "ts", T.ei[:], T.sb8[:], T.gs[:, me:me + 1], 8.0, A.subtract, A.mult)
+    a = op("v", [a], "ts", T.seli[:], T.ei[:], 31, None, A.bitwise_and)
+    a = op("v", [a], "copy", T.sel[:], T.seli[:])
+    to2 = op("v", [a] + tlst, "copy", T.off2[:], T.lst[:, 0:32].indirect(T.sel[:]))
+    for x in range(3):
+        tpc = op("v", [to2, tdz], "copy", T.s2q[:, 80 * x:80 * x + 80].bitcast(u32), T.l1q[:, 0:S1 + 2].bitcast(u32).indirect(T.off2[:, 8 * x:8 * x + C5]))
+        tps = op("a", [to2, tdz, aa1], "act", T.s2s[:, 80 * x:80 * x + 80], T.l1s[:, 0:S1 + 2].indirect(T.off2[:, 8 * x:8 * x + C5]), F.Copy)
+    send([tpc], "a3", "c", [(T.s2q[:, 80 * x:80 * x + 80].bitcast(u8), T.l2q[:, o0:o0 + CAPP].bitcast(u8)) for x in range(3)])
+    send([tps], "a3", "p", [(T.s2s[:, 80 * x:80 * x + 80], T.l2s[:, o0:o0 + CAPP]) for x in range(3)])
+    tng = op("a", [tnr], "act", T.ng[:], T.nr[:].indirect(T.off2[:, 0:24]), F.Copy)
+    toc = op("v", [], "copy", T.l2q[:, o0:o0 + CAPP].bitcast(u32), T.l1q[:, 0:S1 + 2].bitcast(u32).indirect(T.off2[:, 24:24 + C5]))
+    tos = op("a", [], "act", T.l2s[:, o0:o0 + CAPP], T.l1s[:, 0:S1 + 2].indirect(T.off2[:, 24:24 + C5]), F.Copy)
+    tno = op("a", [tset], "act", T.nw[:, o0:o0 + CAPP], T.nr[:].indirect(T.off2[:, 24:24 + C5]), F.Copy)
+    a = op("v", [tng], "tr", T.ngt[:], T.ng[0:32, :])
+    for i in range(3):
+        tv2 = op("v", [a, tset], "copy", T.v2s[32 * i:32 * i + 32, 0:3], T.ngt[0:32, 32 * i:384:128])
+    send([tv2], "m2r", "c", [(T.v2s[:, x:x + 1], T.v2l[:, 8 * me:8 * me + 1]) for x in range(3)])
+
+    if me == 0:
+        tgs = places()
+    a = op("v", [tgs], "ts", T.ai[:], T.gs[:, 1:5], float(3 - me), None, A.add)
+    a = op("v", [a], "ts", T.aj[:], T.ai[:], 2, None, A.logical_shift_right)
+    a = op("v", [a, tset], "copy", T.a5[:, 1:5], T.aj[:])
+    a = op("v", [a], "tt", T.wd[:], T.a5[:, 0:4], T.a5[:, 1:5], A.subtract)
+    a = op("v", [a], "ts", T.we[:], T.wd[:], float(CAPP), None, A.add)
+    for d in range(4):
+        b = op("v", [a], "ts", T.tp[:, 16 * d:16 * d + 16], T.b16[:], T.a5[:, d + 1:d + 2], T.we[:, d:d + 1], A.is_ge, A.mult)
+    a = op("v", [b], "tt", T.ta[:, 0:32], T.tp[:, 0:32], T.tp[:, 32:64], A.add)
+    b = op("v", [a], "tt", T.ta[:, 32:48], T.ta[:, 0:16], T.ta[:, 16:32], A.add)
+    a = op("v", [b], "tt", T.ta[:, 48:64], T.ta[:, 32:48], T.b16[:], A.add)
+    tfin = op("v", [a], "ts", T.fin[:], T.ta[:, 48:64], float(S1), None, A.min)
+
+    aa3 = ("a3", into["c"] + into["p"])
+    tfc, tfs, ty = [], [], []
+    for h in range(2):
+        tfc.append(op("v", [aa3, tfin, toc, tdz], "copy", T.oq[:, 128 * h:128 * h + 128].bitcast(u32), T.l2q[:, 0:S1 + 2].bitcast(u32).indirect(T.fin[:, 8 * h:8 * h + 8])))
+        tfs.append(op("a", [aa3, tfin, tos, tdz], "act", T.os_[:, 128 * h:128 * h + 128], T.l2s[:, 0:S1 + 2].indirect(T.fin[:, 8 * h:8 * h + 8]), F.Copy))
+        ty.append(op("t", [tfc[h], tfs[h], twq], "mm", T.py[:, 512 * h:512 * h + 128], T.wq[:], T.ws[:], T.oq[:, 128 * h:128 * h + 128], T.os_[:, 128 * h:128 * h + 128], True, True))
+    dma("s", tfc, "so", T.oc[:], T.oq[:].bitcast(u8))
+    for i in range(4):
+        dma("s", tfs, "so", T.osc[4 * i:4 * i + 4, :], T.os_[32 * i:32 * i + 4, :])
+    b0 = op("v", [ty[0]], "copy", T.yb[:, 0:128], T.py[:, 0:128])
+    b1 = op("a", [ty[1]], "act", T.yb[:, 128:256], T.py[:, 512:640], F.Copy)
+    dma("s", [b0], "so", T.y[:, 0:128], T.yb[:, 0:128])
+    dma("a", [b1], "sp", T.y[:, 128:256], T.yb[:, 128:256])
+    a = op("v", [("m2r", into["c"]), tset], "copy", T.xn[:, 0:128:32], T.v2l[:, 0:32:8])
+    a = op("v", [a], "tr", T.xnt[:], T.xn[:])
+    for d in range(4):
+        if d != me:
+            for i in range(3):
+                w = min(32, CAPP - 32 * i)
+                tnw_ = op("v", [a, tset], "copy", T.nw[0:1, CAPP * d + 32 * i:CAPP * d + 32 * i + w], T.xnt[32 * i:32 * i + 1, 32 * d:32 * d + w])
+    a = op("v", [tnw_, tno, tfin], "copy", T.nout[:], T.nw[:].indirect(T.fin[:]))
+    dma("s", [a], "so", T.num[:], T.nout[0:1, :])
+
+    wait("g", [(s, v) for s, v in count.items()])
+    wait("g", [am1, aa1, aa2, aa3, ("m2r", into["c"])])

@@ -26,26 +26,27 @@ SCRATCH = {
     "r16": ("sbuf", [128, 1], "float32"), "q5": ("sbuf", [128, 1], "float32"),
     "io16": ("sbuf", [128, 16], "float32"), "b16": ("sbuf", [128, 16], "float32"), "b16h": ("sbuf", [128, 8], "float32"),
     "qb2": ("sbuf", [128, 5], "float32"), "qb2h": ("sbuf", [128, 5], "float32"), "sb8": ("sbuf", [128, 2], "float32"),
-    "sg": ("sbuf", [128, 4], "float32"),
+    "bd": ("sbuf", [128, 4], "float32"),
     "neg1": ("sbuf", [128, 128], "float32"), "idm": ("sbuf", [128, 128], "float32"),
-    "zf": ("sbuf", [128, S1], "float32"), "negw": ("sbuf", [128, S1], "float32"),
+    "zf": ("sbuf", [128, 128], "float32"),
     "nega": ("sbuf", [128, 128], "float32"), "neg0": ("sbuf", [128, 128], "float32"),
     "one": ("sbuf", [128, 24], "float32"), "mka": ("sbuf", [128, 24], "float32"), "mk": ("sbuf", [128, 24], "float32"),
     "mo": ("sbuf", [128, 4], "float32"),
-    "zb": ("sbuf", [128, S1], "bfloat16"),
-    "s0": ("sbuf", [128, P], "bfloat16"), "t1": ("sbuf", [128, P], "bfloat16"), "ind": ("sbuf", [128, P], "bfloat16"),
+    "zb": ("sbuf", [128, P], "bfloat16"), "two": ("sbuf", [128, 32], "bfloat16"),
+    "t0": ("sbuf", [128, P], "bfloat16"), "th": ("sbuf", [128, P], "float32"), "ind": ("sbuf", [128, P], "bfloat16"),
     "c1": ("sbuf", [128, P], "bfloat16"), "jv": ("sbuf", [128, 2 * P], "bfloat16"), "ja": ("sbuf", [128, 3 * P], "bfloat16"),
     "ac": ("sbuf", [128, 4], "float32"), "lq": ("sbuf", [128, 8], "float32"), "lw": ("sbuf", [128, 24], "float32"),
     "off1": ("sbuf", [128, 24], "uint16"),
     "tm": ("sbuf", [128, 24], "float32"), "rn": ("sbuf", [128, 4], "float32"),
-    "m1s": ("sbuf", [128, 8], "uint16"), "m1l": ("sbuf", [128, 32], "uint16"),
-    "db": ("sbuf", [128, 384], "float32"), "mb0": ("sbuf", [128, 128], "float32"), "mb1": ("sbuf", [128, 256], "float32"),
-    "mb2": ("sbuf", [128, S1], "float32"), "nt": ("sbuf", [128, 4], "float32"), "acc": ("sbuf", [128, 4], "float32"),
+    "hl": ("sbuf", [128, 32], "bfloat16"), "m1s": ("sbuf", [128, 4], "uint16"), "m1l": ("sbuf", [128, 32], "uint16"),
+    "db": ("sbuf", [128, 384], "float32"), "mb0": ("sbuf", [128, 128], "float32"), "mb1": ("sbuf", [128, 128], "float32"),
+    "mb2": ("sbuf", [128, 128], "float32"), "nt": ("sbuf", [128, 4], "float32"), "acc": ("sbuf", [128, 8], "float32"),
     "jf": ("sbuf", [128, 704], "bfloat16"),
     "cn1": ("sbuf", [128, 4], "float32"), "ce": ("sbuf", [128, 8], "float32"), "fi": ("sbuf", [128, 4], "float32"),
-    "fo": ("sbuf", [128, 4], "float32"), "ov": ("sbuf", [128, 2], "float32"), "ev": ("sbuf", [128, 4], "float32"),
-    "bb": ("sbuf", [128, 32], "bfloat16"), "bt": ("sbuf", [128, 32], "bfloat16"), "rw": ("sbuf", [128, 128], "bfloat16"),
-    "uu": ("sbuf", [128, 128], "bfloat16"), "d0": ("sbuf", [128, S1], "bfloat16"), "d1": ("sbuf", [128, S1], "bfloat16"),
+    "fo": ("sbuf", [128, 4], "float32"), "ov": ("sbuf", [128, 2], "float32"), "th1": ("sbuf", [128, 1], "float32"),
+    "ev": ("sbuf", [128, 4], "float32"), "bb": ("sbuf", [128, 32], "bfloat16"), "bt": ("sbuf", [128, 32], "bfloat16"),
+    "bb2": ("sbuf", [128, 32], "bfloat16"), "bt2": ("sbuf", [128, 32], "bfloat16"),
+    "d0": ("sbuf", [128, S1], "bfloat16"), "d1": ("sbuf", [128, S1], "bfloat16"),
     "c2": ("sbuf", [128, S1], "float32"), "cn2": ("sbuf", [128, 16], "float32"),
     "jv2": ("sbuf", [128, 2 * S1], "bfloat16"), "ja2": ("sbuf", [128, 3 * S1], "bfloat16"),
     "ac2": ("sbuf", [128, 4], "float32"), "l2": ("sbuf", [128, 8], "float32"), "lst": ("sbuf", [128, 32], "float32"),
@@ -61,7 +62,7 @@ SCRATCH = {
     "nout": ("sbuf", [128, P], "float32"),
     "pz": ("psum", [128, 1024], "float32"), "pmm": ("psum", [128, 1536], "float32"), "py": ("psum", [128, 1024], "float32"),
 }
-SEMAPHORES = ["vs", "sa", "ts", "gc", "dpl", "dx0", "dx1", "dw", "dz", "dn", "so", "sp", "ls", "a1", "m1r", "a2", "a3", "m2r"]
+SEMAPHORES = ["vs", "sa", "ts", "gc", "dpl", "dx0", "dx1", "dw", "dz", "dn", "so", "sp", "ls", "a0", "a1", "m1r", "a2", "a3", "m2r"]
 
 
 def share(topo, src, dsts):
@@ -74,8 +75,7 @@ def share(topo, src, dsts):
     def far(d):
         a, b = topo.chip(src), topo.chip(d)
         return not topo.mates(a, b) and not topo.same_plane(a, b)
-    lead = [d for d in dsts if far(d)] or [dsts[-1]]
-    lead = lead[0]
+    lead = ([d for d in dsts if far(d)] or [dsts[-1]])[0]
     rest = [d for d in dsts if d != lead]
     return {lead: (part[2] + part[3], part[0] + part[1]), rest[0]: (part[0], part[2]), rest[1]: (part[1], part[3])}
 
@@ -95,6 +95,10 @@ def rank_program(g, core, T, topo):
     u8, u32 = dt.uint8, dt.uint32
     eng = {"v": g.vector, "a": g.scalar, "t": g.tensor, "g": g, "s": g.sync}
     own_sem = {"v": "vs", "a": "sa", "t": "ts", "g": "gc"}
+    calls = {"copy": g.vector.tensor_copy, "tt": g.vector.tensor_tensor, "ts": g.vector.tensor_scalar,
+             "red": g.vector.tensor_reduce, "scan": g.vector.tensor_tensor_scan, "tr": g.vector.transpose,
+             "set": g.vector.memset, "qmx": g.vector.quantize_mx, "act": g.scalar.activation,
+             "mm": g.tensor.matmul_mx, "iota": g.iota, "aff": g.affine_select, "bc": g.partition_broadcast}
     count, seen = {}, {}
 
     def wait(q, deps):
@@ -108,11 +112,6 @@ def rank_program(g, core, T, topo):
 
     def op(q, deps, name, *args, **kw):
         wait(q, deps)
-        e = eng[q]
-        calls = {"copy": g.vector.tensor_copy, "tt": g.vector.tensor_tensor, "ts": g.vector.tensor_scalar,
-                 "red": g.vector.tensor_reduce, "scan": g.vector.tensor_tensor_scan, "tr": g.vector.transpose,
-                 "set": g.vector.memset, "qmx": g.vector.quantize_mx, "act": g.scalar.activation,
-                 "mm": g.tensor.matmul_mx, "iota": g.iota, "aff": g.affine_select, "bc": g.partition_broadcast}
         s = own_sem[q]
         calls[name](*args, **kw).then_inc(T.sem[s], 1)
         count[s] = count.get(s, 0) + 1
@@ -150,21 +149,20 @@ def rank_program(g, core, T, topo):
     tx0 = dma("s", [], "dx0", T.xt[:, 0:512], T.x[:, 0:512])
     tw = dma("s", [], "dw", T.wt[:], T.w[:])
 
-    k = op("v", [], "set", T.ploff[:, 0:8], 0)
-    tpo = op("v", [], "set", T.ploff[:, 8:16], 1)
+    op("v", [], "set", T.ploff[:, 0:8], 0)
+    op("v", [], "set", T.ploff[:, 8:12], 1)
+    tpo = op("v", [], "set", T.ploff[:, 12:16], 2)
     tz4 = op("v", [], "set", T.xt[:, 4 * P:4 * P + 8], 0.0)
     for qd in range(4):
-        b = qd & 1
-        op("v", [], "set", T.sg[32 * qd:32 * qd + 32, 0:1], -1.0 if b else 1.0)
-        op("v", [], "set", T.sg[32 * qd:32 * qd + 32, 1:2], -TINY if b else TINY)
-    op("v", [], "set", T.sg[0:64, 2:3], 0.0)
-    tsg = op("v", [], "set", T.sg[64:128, 2:3], 1.0)
+        op("v", [], "set", T.bd[32 * qd:32 * qd + 32, 0:1], float(qd & 1))
+        tbd = op("v", [], "set", T.bd[32 * qd:32 * qd + 32, 1:2], TINY if qd & 2 else 0.0)
     tzb = op("v", [], "set", T.zb[:], 0.0)
     tpn = op("g", [], "iota", T.pn[:], [[0, 1]], 0, 1)
     tio = op("g", [], "iota", T.io16[:], [[16, 16]], 0, 1, allow_small_or_imprecise_dtypes=True)
     tzf = op("v", [], "set", T.zf[:], 0.0)
     tn1 = op("v", [], "set", T.neg1[:], -0.9375)
     ton = op("v", [], "set", T.one[:], 1.0)
+    tlz = op("v", [], "set", T.lq[:, 5:6], 0.0)
     a = op("v", [tpn], "ts", T.pm16[:], T.pn[:], 112, None, A.bitwise_and)
     b = op("v", [tpn], "ts", T.ph5[:], T.pn[:], 5, None, A.logical_shift_right)
     a = op("v", [a], "copy", T.r16[:], T.pm16[:])
@@ -172,15 +170,15 @@ def rank_program(g, core, T, topo):
     tb16 = op("v", [a, tio], "ts", T.b16[:], T.io16[:], T.r16[:, 0:1], None, A.subtract)
     tb16h = op("v", [tb16], "ts", T.b16h[:], T.b16[:, 0:8], 0.5, None, A.add)
     tid = op("g", [tn1], "aff", T.idm[:], T.neg1[:], [[-1, 128]], A.is_equal, 0.0, 0, 1)
-    tnw = op("g", [tzf], "aff", T.negw[:], T.zf[:], [[-1, S1]], A.is_gt, -BIG, 192, 1)
-    a = op("g", [tzf], "aff", T.nega[:], T.zf[:, 0:128], [[-1, 128]], A.is_gt, -BIG, 0, 1)
-    tn0 = op("g", [a], "aff", T.neg0[:], T.nega[:], [[1, 128]], A.is_gt, BIG, 0, 1)
+    tng = op("g", [tzf], "aff", T.nega[:], T.zf[:], [[-1, 128]], A.is_gt, -BIG, 0, 1)
+    tn0 = op("g", [tng], "aff", T.neg0[:], T.nega[:], [[1, 128]], A.is_gt, BIG, 0, 1)
     a = op("g", [ton], "aff", T.mka[:], T.one[:], [[0, 4], [-16, 6]], A.is_ge, 0.0, 0, 1)
     tmk = op("g", [a], "aff", T.mk[:], T.mka[:], [[0, 4], [16, 6]], A.is_ge, 0.0, 15, -1)
     op("g", [ton], "aff", T.mo[:, 0:2], T.one[:, 0:2], [[-CAPP, 2]], A.is_equal, 0.0, 0, 1)
     tmo = op("g", [ton], "aff", T.mo[:, 2:4], T.one[:, 0:2], [[-CAPP, 2]], A.is_equal, 0.0, 128 - 2 * CAPP, 1)
 
-    tplq = op("v", [tpl], "qmx", T.plq[:], T.pls[:], T.plt[:])
+    a = op("v", [tpl], "ts", T.plt[:, 8:12], T.plt[:, 4:8], -1.0, None, A.mult)
+    tplq = op("v", [a], "qmx", T.plq[:], T.pls[:], T.plt[:])
     tprq = op("v", [tplq, tpo], "copy", T.prq[:].bitcast(u32), T.plq[:].bitcast(u32).indirect(T.ploff[:]))
     tprs = op("a", [tplq, tpo], "act", T.prs[:], T.pls[:].indirect(T.ploff[:]), F.Copy)
     tq0 = op("v", [tx0], "qmx", T.xq[:, 0:128], T.xs[:, 0:128], T.xt[:, 0:512])
@@ -192,20 +190,21 @@ def rank_program(g, core, T, topo):
     tz0 = op("t", [tprq, tprs] + tq, "mm", T.pz[:, 0:P], T.prq[:, 0:128], T.prs[:, 0:128], T.xq[:, 0:P], T.xs[:, 0:P], True, True)
     tz1 = op("t", [], "mm", T.pz[:, 512:512 + P], T.prq[:, 128:256], T.prs[:, 128:256], T.xq[:, 0:P], T.xs[:, 0:P], True, True)
 
-    ts0 = op("a", [tz0, tsg], "act", T.s0[:], T.pz[:, 0:P], F.Sign, bias=T.sg[:, 1:2], scale=T.sg[:, 0:1])
-    tt1 = op("v", [tz1, tsg], "ts", T.t1[:], T.pz[:, 512:512 + P], 0.0, T.sg[:, 2:3], A.is_lt, A.is_equal)
-    a = op("v", [ts0, tt1], "tt", T.ind[:], T.s0[:], T.t1[:], A.is_equal)
-    tc = op("v", [a, tzb], "scan", T.c1[:], T.ind[:], T.zb[:, 0:P], 0.0, A.add, A.add)
+    a = op("v", [tz0, tbd], "ts", T.t0[:], T.pz[:, 0:P], 0.0, T.bd[:, 0:1], A.is_lt, A.not_equal)
+    a = op("a", [a, tbd], "act", T.th[:], T.t0[:], F.Identity, bias=T.bd[:, 1:2], scale=BIG)
+    a = op("v", [a, tz1], "tt", T.ind[:], T.pz[:, 512:512 + P], T.th[:], A.is_ge)
+    tc = op("v", [a, tzb], "scan", T.c1[:], T.ind[:], T.zb[:], 0.0, A.add, A.add)
+    send([tc], "a0", "c", [(T.c1[:, P - 1:P], T.hl[:, 8 * me:8 * me + 1])] * 3)
     for m in range(3):
         tac = op("a", [tc, tb16h], "act", T.ja[:, P * m:P * m + P], T.c1[:], F.Sign, bias=T.b16h[:, m:m + 1], scale=-1.0,
                  accum_out=T.ac[:, m:m + 1])
     j3 = op("v", [tc, tb16], "ts", T.jv[:, 0:P], T.c1[:], T.b16[:, 3:4], None, A.is_le)
     j4 = op("v", [tc], "ts", T.jv[:, P:2 * P], T.c1[:], T.b16[:, 4:5], None, A.is_le)
-    op("v", [tc], "ts", T.lq[:, 5:6], T.c1[:, P - 1:P], 0.5, None, A.is_gt)
+    tho = op("v", [tc], "copy", T.hl[:, 8 * me:8 * me + 1], T.c1[:, P - 1:P])
     op("v", [j3], "red", T.lq[:, 3:4], T.jv[:, 0:P], X, A.add)
     op("v", [j4], "red", T.lq[:, 4:5], T.jv[:, P:2 * P], X, A.add)
-    tl = op("v", [tac], "ts", T.lq[:, 0:3], T.ac[:, 0:3], 0.5, P / 2.0, A.mult, A.add)
-    for x in range(4):
+    tl = op("v", [tac, tlz], "ts", T.lq[:, 0:3], T.ac[:, 0:3], 0.5, P / 2.0, A.mult, A.add)
+    for x in range(3):
         d = order[x]
         for qd in range(4):
             out, src = T.lw[32 * qd:32 * qd + 32, 6 * x:6 * x + 6], T.lq[32 * d:32 * d + 32, 0:6]
@@ -213,29 +212,29 @@ def rank_program(g, core, T, topo):
                 tv = op("v", [tl], "copy", out, src)
             else:
                 ta = op("a", [tl], "act", out, src, F.Copy)
-    tlw = [tv, ta]
-    toff = op("v", tlw, "copy", T.off1[:], T.lw[:])
+    toff = op("v", [tv, ta], "copy", T.off1[:, 0:18], T.lw[:, 0:18])
     tpc = op("v", [toff] + tq, "copy", T.s1q[:, 0:272].bitcast(u32), T.xq[:, 0:P + 2].bitcast(u32).indirect(T.off1[:, 0:17]))
     tps = op("a", [toff] + tq, "act", T.s1s[:, 0:272], T.xs[:, 0:P + 2].indirect(T.off1[:, 0:17]), F.Copy)
     o0 = CAPP * me
-    toc = op("v", [], "copy", T.l1q[:, o0:o0 + CAPP].bitcast(u32), T.xq[:, 0:P + 2].bitcast(u32).indirect(T.off1[:, 18:18 + C5]))
-    tos = op("a", [], "act", T.l1s[:, o0:o0 + CAPP], T.xs[:, 0:P + 2].indirect(T.off1[:, 18:18 + C5]), F.Copy)
+    for qd in range(4):
+        tv = op("v", [tl], "copy", T.lw[32 * qd:32 * qd + 32, 18:24], T.lq[32 * me:32 * me + 32, 0:6])
+    toff = op("v", [tv], "copy", T.off1[:, 18:24], T.lw[:, 18:24])
+    toc = op("v", [toff], "copy", T.l1q[:, o0:o0 + CAPP].bitcast(u32), T.xq[:, 0:P + 2].bitcast(u32).indirect(T.off1[:, 18:18 + C5]))
+    tos = op("a", [toff], "act", T.l1s[:, o0:o0 + CAPP], T.xs[:, 0:P + 2].indirect(T.off1[:, 18:18 + C5]), F.Copy)
     send([tpc], "a1", "c", [(T.s1q[:, 96 * x:96 * x + CAPP].bitcast(u8), T.l1q[:, o0:o0 + CAPP].bitcast(u8)) for x in range(3)])
     send([tps], "a1", "p", [(T.s1s[:, 96 * x:96 * x + CAPP], T.l1s[:, o0:o0 + CAPP]) for x in range(3)])
     a = op("v", [tmk], "tt", T.tm[:], T.lw[:], T.mk[:], A.mult)
     for x in range(4):
         b = op("v", [a], "red", T.rn[:, x:x + 1], T.tm[:, 6 * x:6 * x + 6], X, A.add)
-    op("v", [b], "ts", T.m1s[:, 0:8:2], T.rn[:], float(P * me), None, A.add)
-    tm1 = op("v", [], "copy", T.m1s[:, 1:8:2], T.lw[:, 5:24:6])
-    send([tm1], "m1r", "c", [(T.m1s[:, 2 * x:2 * x + 2], T.m1l[:, 8 * me:8 * me + 2]) for x in range(3)])
-    tm1o = op("v", [tm1], "copy", T.m1l[:, 8 * me:8 * me + 2], T.m1s[:, 6:8])
+    tm1 = op("v", [b], "ts", T.m1s[:], T.rn[:], float(P * me), None, A.add)
+    send([tm1], "m1r", "c", [(T.m1s[:, x:x + 1], T.m1l[:, 8 * me:8 * me + 1]) for x in range(3)])
+    tm1o = op("v", [tm1], "copy", T.m1l[:, 8 * me:8 * me + 1], T.m1s[:, 3:4])
     am1 = ("m1r", into["c"])
     for s in range(N):
         tdn = dma("s", [am1, tm1o], "dn", T.nr16[0:1, CAPP * s:CAPP * s + CAPP], T.m1l[0:CAPP, 8 * s:8 * s + 1])
 
     twq = op("v", [tw], "qmx", T.wq[:], T.ws[:], T.wt[:])
-    op("v", [tb16, tq5], "ts", T.qb2[:], T.b16[:, 0:5], 4.0, T.q5[:, 0:1], A.mult, A.add)
-    a = ("vs", count["vs"])
+    a = op("v", [tb16, tq5], "ts", T.qb2[:], T.b16[:, 0:5], 4.0, T.q5[:, 0:1], A.mult, A.add)
     tq2 = op("v", [a], "ts", T.qb2h[:], T.qb2[:], 0.5, None, A.add)
     tsb8 = op("v", [], "ts", T.sb8[:], T.b16[:, 0:2], float(8 * (me + 1) + 8192), 0.125, A.add, A.mult)
     td1 = op("v", [], "set", T.d1[:, 128:S1], 0.0)
@@ -247,47 +246,53 @@ def rank_program(g, core, T, topo):
     op("v", [], "set", T.v2l[:, 8 * me:8 * me + 8], 0)
     op("v", [], "set", T.xn[:], 0.0)
     op("v", [], "set", T.nr[:], 0.0)
-    tset = op("v", [], "set", T.nw[:], -1.0)
-
-    aa1 = ("a1", into["c"] + into["p"])
-    blocks = {0: (0, 128, T.mb0, T.neg0[:], 0, 0), 1: (128, 256, T.mb1, T.negw[:, 64:S1], 512, 128), 2: (192, S1, T.mb2, T.negw[:], 1024, 384)}
-    tmm = {}
-    for b in (1, 2, 0):
-        k0, n, mb, ng, c0, jc = blocks[b]
-        tmm[b] = op("t", [aa1, toc, tos], "mm", T.pmm[:, c0:c0 + n], T.l1q[:, k0:k0 + 128], T.l1s[:, k0:k0 + 128],
-                    T.l1q[:, 0:n], T.l1s[:, 0:n], True, True)
-    tacc = {}
-    for b in (1, 2, 0):
-        k0, n, mb, ng, c0, jc = blocks[b]
-        a = op("v", [tmm[b], tid], "tt", T.db[:, 128 * b:128 * b + 128], T.pmm[:, c0 + k0:c0 + k0 + 128], T.idm[:], A.mult)
-        c = op("v", [tnw, tn0], "tt", mb[:], T.pmm[:, c0:c0 + n], ng, A.add)
-        a = op("v", [a], "red", T.nt[:, b:b + 1], T.db[:, 128 * b:128 * b + 128], X, A.add)
-        tacc[b] = op("a", [a, c], "act", T.jf[:, jc:jc + n], mb[:], F.Sign, bias=T.nt[:, b:b + 1], accum_out=T.acc[:, b:b + 1])
-    a = op("v", [am1, tm1o], "copy", T.cn1[:], T.m1l[:, 1:32:8])
+    op("v", [], "set", T.nw[:], -1.0)
+    op("v", [], "set", T.bb2[:], 0.0)
+    tset = op("v", [], "set", T.two[:], 2.0)
+    aa0 = ("a0", into["c"])
+    for qd in range(4):
+        a = op("v", [aa0, tho], "ts", T.cn1[32 * qd:32 * qd + 32, :], T.hl[32 * me:32 * me + 32, 0:32:8], 1.0, None, A.min)
     a = op("v", [a, tset], "scan", T.ce[:, 1:5], T.cn1[:], T.zf[:, 0:4], 0.0, A.add, A.add)
     a = op("v", [a], "tt", T.fi[:], T.cn1[:], T.ce[:, 0:4], A.is_gt)
     a = op("v", [a, tmo], "tt", T.fo[:], T.fi[:], T.mo[:], A.mult)
-    tov = op("v", [a], "tt", T.ov[:], T.fo[:, 0:4:2], T.fo[:, 1:4:2], A.add)
-    op("v", [tacc[2]], "ts", T.ev[:, 2:3], T.acc[:, 2:3], 0.5 - S1, 4.0, A.is_le, A.mult)
-    a = op("v", [tacc[1], tov], "ts", T.ev[:, 1:2], T.acc[:, 1:2], 0.5 - 256, T.ov[:, 1:2], A.is_le, A.max)
-    b = op("v", [tacc[0], tov], "ts", T.ev[:, 0:1], T.acc[:, 0:1], 0.5 - 128, T.ov[:, 0:1], A.is_le, A.max)
-    a = op("v", [a], "ts", T.ev[:, 3:4], T.ev[:, 1:2], 2.0, T.ev[:, 2:3], A.mult, A.add)
-    a = op("v", [a, b], "ts", T.bb[:], T.zb[:, 0:32], T.ev[:, 0:1], T.ev[:, 3:4], A.add, A.add)
+    a = op("v", [a], "tt", T.ov[:], T.fo[:, 0:4:2], T.fo[:, 1:4:2], A.add)
+    tov = op("v", [a], "ts", T.th1[:], T.ov[:, 1:2], 4096.0, 0.5 - 256, A.mult, A.add)
+
+    aa1 = ("a1", into["c"] + into["p"])
+    blocks = {0: (0, 128, T.mb0, T.neg0[:], 0, 0), 1: (128, 256, T.mb1, T.nega[:], 512, 128), 2: (192, S1, T.mb2, T.nega[:], 1024, 384)}
+    tmm, tof, tdg = {}, {}, {}
+    for b in (1, 2, 0):
+        k0, n, mb, ng, c0, jc = blocks[b]
+        tmm[b] = op("t", [aa1, toc, tos, tdz], "mm", T.pmm[:, c0:c0 + n], T.l1q[:, k0:k0 + 128], T.l1s[:, k0:k0 + 128],
+                    T.l1q[:, 0:n], T.l1s[:, 0:n], True, True)
+    for b in (1, 2, 0):
+        k0, n, mb, ng, c0, jc = blocks[b]
+        a = op("v", [tmm[b], tid], "tt", T.db[:, 128 * b:128 * b + 128], T.pmm[:, c0 + k0:c0 + k0 + 128], T.idm[:], A.mult)
+        c = op("v", [tng, tn0], "tt", mb[:], T.pmm[:, c0 + k0:c0 + k0 + 128], ng, A.add)
+        a = op("v", [a], "red", T.nt[:, b:b + 1], T.db[:, 128 * b:128 * b + 128], X, A.add)
+        if k0:
+            tof[b] = op("a", [a, c], "act", T.jf[:, jc:jc + k0], T.pmm[:, c0:c0 + k0], F.Sign, bias=T.nt[:, b:b + 1],
+                        accum_out=T.acc[:, 4 + b:5 + b])
+        tdg[b] = op("a", [a, c], "act", T.jf[:, jc + k0:jc + k0 + 128], mb[:], F.Sign, bias=T.nt[:, b:b + 1],
+                    accum_out=T.acc[:, b:b + 1])
+    a = op("v", [tof[2], tdg[2], tset], "ts", T.bb2[:, 0:1], T.acc[:, 2:3], T.acc[:, 6:7], 0.5 - S1, A.add, A.is_le)
+    b = op("v", [tof[1], tdg[1], tov], "ts", T.ev[:, 1:2], T.acc[:, 1:2], T.acc[:, 5:6], T.th1[:, 0:1], A.add, A.is_le)
+    tb2 = op("v", [a], "tr", T.bt2[:], T.bb2[:])
+    for i in (2, 3):
+        op("g", [tb2], "bc", T.d0[:, 192 + 32 * i:224 + 32 * i], T.bt2[32 * i:32 * i + 1, 0:32], 128)
+    a = op("v", [tdg[0], tov], "ts", T.ev[:, 0:1], T.acc[:, 0:1], 0.5 - 128, T.ov[:, 0:1], A.is_le, A.max)
+    a = op("v", [a, b, tset], "ts", T.bb[:], T.two[:], T.ev[:, 1:2], T.ev[:, 0:1], A.mult, A.add)
     tbt = op("v", [a], "tr", T.bt[:], T.bb[:])
-    tb = op("g", [tbt], "bc", T.rw[:, 96:128], T.bt[96:97, 0:32], 128)
+    tb = op("g", [tbt], "bc", T.d0[:, 96:128], T.bt[96:97, 0:32], 128)
     for i in range(3):
         for qd in range(4):
-            out, src = T.rw[32 * qd:32 * qd + 32, 32 * i:32 * i + 32], T.bt[32 * i:32 * i + 32, 0:32]
+            out, src = T.d0[32 * qd:32 * qd + 32, 32 * i:32 * i + 32], T.bt[32 * i:32 * i + 32, 0:32]
             if qd < 2:
                 tv = op("v", [tbt], "copy", out, src)
             else:
                 ta = op("a", [tbt], "act", out, src, F.Copy)
-    trw = [tb, tv, ta]
-    a = op("v", trw, "ts", T.uu[:], T.rw[:], 4.0, -4.0, A.is_ge, A.mult)
-    op("v", [], "ts", T.d0[:, 256:S1], T.rw[:, 64:128], 4.0, None, A.is_ge)
-    a = op("v", [a], "tt", T.d0[:, 0:128], T.rw[:], T.uu[:], A.add)
-    op("v", [a], "ts", T.d0[:, 128:256], T.d0[:, 0:128], 2.0, None, A.is_ge)
-    a = op("v", [a], "ts", T.d1[:, 0:128], T.d0[:, 0:128], 2.0, -2.0, A.is_ge, A.mult)
+    a = op("v", [tb, tv, ta], "ts", T.d1[:, 0:128], T.d0[:, 0:128], 2.0, -2.0, A.is_ge, A.mult)
+    a = op("v", [], "ts", T.d0[:, 128:256], T.d0[:, 0:128], 2.0, None, A.is_ge)
     tc2 = op("v", [a, td1], "scan", T.c2[:], T.d0[:], T.d1[:], 0.0, A.add, A.add)
     send([tc2], "a2", "c", [(T.c2[:, S1 - 1:S1], T.cn2[:, 4 * me:4 * me + 1])] * 3)
     aa2 = ("a2", into["c"])
@@ -355,7 +360,8 @@ def rank_program(g, core, T, topo):
         tfc.append(op("v", [aa3, tfin, toc, tdz], "copy", T.oq[:, 128 * h:128 * h + 128].bitcast(u32), T.l2q[:, 0:S1 + 2].bitcast(u32).indirect(T.fin[:, 8 * h:8 * h + 8])))
         tfs.append(op("a", [aa3, tfin, tos, tdz], "act", T.os_[:, 128 * h:128 * h + 128], T.l2s[:, 0:S1 + 2].indirect(T.fin[:, 8 * h:8 * h + 8]), F.Copy))
         ty.append(op("t", [tfc[h], tfs[h], twq], "mm", T.py[:, 512 * h:512 * h + 128], T.wq[:], T.ws[:], T.oq[:, 128 * h:128 * h + 128], T.os_[:, 128 * h:128 * h + 128], True, True))
-    dma("s", tfc, "so", T.oc[:], T.oq[:].bitcast(u8))
+    for h in range(2):
+        dma("s", [tfc[h]], "so", T.oc[:, 512 * h:512 * h + 512], T.oq[:, 128 * h:128 * h + 128].bitcast(u8))
     for i in range(4):
         dma("s", tfs, "so", T.osc[4 * i:4 * i + 4, :], T.os_[32 * i:32 * i + 4, :])
     b0 = op("v", [ty[0]], "copy", T.yb[:, 0:128], T.py[:, 0:128])
@@ -368,9 +374,9 @@ def rank_program(g, core, T, topo):
         if d != me:
             for i in range(3):
                 w = min(32, CAPP - 32 * i)
-                tnw_ = op("v", [a, tset], "copy", T.nw[0:1, CAPP * d + 32 * i:CAPP * d + 32 * i + w], T.xnt[32 * i:32 * i + 1, 32 * d:32 * d + w])
-    a = op("v", [tnw_, tno, tfin], "copy", T.nout[:], T.nw[:].indirect(T.fin[:]))
+                b = op("v", [a, tset], "copy", T.nw[0:1, CAPP * d + 32 * i:CAPP * d + 32 * i + w], T.xnt[32 * i:32 * i + 1, 32 * d:32 * d + w])
+    a = op("v", [b, tno, tfin], "copy", T.nout[:], T.nw[:].indirect(T.fin[:]))
     dma("s", [a], "so", T.num[:], T.nout[0:1, :])
 
     wait("g", [(s, v) for s, v in count.items()])
-    wait("g", [am1, aa1, aa2, aa3, ("m2r", into["c"])])
+    wait("g", [am1, aa0, aa1, aa2, aa3, ("m2r", into["c"])])

@@ -2,10 +2,13 @@ from concourse.bass import DstId, RemoteDMATransfer
 from concourse.mybir import dt, AluOpType, AxisListType, ActivationFunctionType
 
 N, P, CAPP = 4, 256, 80
+H = P // 2
 S1 = N * CAPP
 C5 = CAPP // 16
 BIG = 1.0e29
 TINY = 1.0e-36
+MARK = 1.0 - 2.0 ** -14
+SHIFT = 64.0
 
 CODE = "float8_e4m3fn_x4"
 SCRATCH = {
@@ -27,27 +30,26 @@ SCRATCH = {
     "io16": ("sbuf", [128, 16], "float32"), "b16": ("sbuf", [128, 16], "float32"), "b16h": ("sbuf", [128, 8], "float32"),
     "qb2": ("sbuf", [128, 5], "float32"), "qb2h": ("sbuf", [128, 5], "float32"), "sb8": ("sbuf", [128, 2], "float32"),
     "bd": ("sbuf", [128, 4], "float32"),
-    "neg1": ("sbuf", [128, 128], "float32"), "idm": ("sbuf", [128, 128], "float32"),
-    "zf": ("sbuf", [128, 128], "float32"),
+    "idm": ("sbuf", [128, 128], "float32"), "zf": ("sbuf", [128, 128], "float32"),
     "nega": ("sbuf", [128, 128], "float32"), "neg0": ("sbuf", [128, 128], "float32"),
     "one": ("sbuf", [128, 24], "float32"), "mka": ("sbuf", [128, 24], "float32"), "mk": ("sbuf", [128, 24], "float32"),
     "mo": ("sbuf", [128, 4], "float32"),
-    "zb": ("sbuf", [128, P], "bfloat16"), "two": ("sbuf", [128, 32], "bfloat16"),
+    "zb": ("sbuf", [128, P], "bfloat16"), "km": ("sbuf", [128, 32], "float32"),
     "t0": ("sbuf", [128, P], "bfloat16"), "th": ("sbuf", [128, P], "float32"), "ind": ("sbuf", [128, P], "bfloat16"),
     "c1": ("sbuf", [128, P], "bfloat16"), "jv": ("sbuf", [128, 2 * P], "bfloat16"), "ja": ("sbuf", [128, 3 * P], "bfloat16"),
     "ac": ("sbuf", [128, 4], "float32"), "lq": ("sbuf", [128, 8], "float32"), "lw": ("sbuf", [128, 24], "float32"),
     "off1": ("sbuf", [128, 24], "uint16"),
     "tm": ("sbuf", [128, 24], "float32"), "rn": ("sbuf", [128, 4], "float32"),
     "hl": ("sbuf", [128, 32], "bfloat16"), "m1s": ("sbuf", [128, 4], "uint16"), "m1l": ("sbuf", [128, 32], "uint16"),
-    "db": ("sbuf", [128, 384], "float32"), "mb0": ("sbuf", [128, 128], "float32"), "mb1": ("sbuf", [128, 128], "float32"),
-    "mb2": ("sbuf", [128, 128], "float32"), "nt": ("sbuf", [128, 4], "float32"), "acc": ("sbuf", [128, 8], "float32"),
-    "jf": ("sbuf", [128, 704], "bfloat16"),
+    "db": ("sbuf", [128, 384], "float32"), "mb": ("sbuf", [128, 384], "float32"), "mx0": ("sbuf", [128, 1], "float32"),
+    "nt": ("sbuf", [128, 4], "float32"), "acc": ("sbuf", [128, 8], "float32"), "jf": ("sbuf", [128, 704], "bfloat16"),
     "cn1": ("sbuf", [128, 4], "float32"), "ce": ("sbuf", [128, 8], "float32"), "fi": ("sbuf", [128, 4], "float32"),
-    "fo": ("sbuf", [128, 4], "float32"), "ov": ("sbuf", [128, 2], "float32"), "th1": ("sbuf", [128, 1], "float32"),
-    "ev": ("sbuf", [128, 4], "float32"), "bb": ("sbuf", [128, 32], "bfloat16"), "bt": ("sbuf", [128, 32], "bfloat16"),
-    "bb2": ("sbuf", [128, 32], "bfloat16"), "bt2": ("sbuf", [128, 32], "bfloat16"),
-    "d0": ("sbuf", [128, S1], "bfloat16"), "d1": ("sbuf", [128, S1], "bfloat16"),
-    "c2": ("sbuf", [128, S1], "float32"), "cn2": ("sbuf", [128, 16], "float32"),
+    "fo": ("sbuf", [128, 4], "float32"), "ov": ("sbuf", [128, 2], "float32"), "th0": ("sbuf", [128, 1], "float32"),
+    "th1": ("sbuf", [128, 1], "float32"),
+    "ev": ("sbuf", [128, 4], "float32"), "bb": ("sbuf", [128, 32], "float32"), "bt": ("sbuf", [128, 32], "float32"),
+    "bb2": ("sbuf", [128, 32], "float32"), "bt2": ("sbuf", [128, 32], "float32"),
+    "rv": ("sbuf", [128, 192], "float32"), "cs": ("sbuf", [128, 1], "float32"), "cn2": ("sbuf", [128, 16], "float32"),
+    "d0": ("sbuf", [128, S1], "float32"), "d1": ("sbuf", [128, S1], "float32"), "c2": ("sbuf", [128, S1], "bfloat16"),
     "jv2": ("sbuf", [128, 2 * S1], "bfloat16"), "ja2": ("sbuf", [128, 3 * S1], "bfloat16"),
     "ac2": ("sbuf", [128, 4], "float32"), "l2": ("sbuf", [128, 8], "float32"), "lst": ("sbuf", [128, 32], "float32"),
     "gs": ("sbuf", [128, 8], "float32"), "ei": ("sbuf", [128, 2], "int32"), "seli": ("sbuf", [128, 2], "int32"),
@@ -56,13 +58,13 @@ SCRATCH = {
     "wd": ("sbuf", [128, 4], "float32"), "we": ("sbuf", [128, 4], "float32"), "tp": ("sbuf", [128, 64], "float32"),
     "ta": ("sbuf", [128, 64], "float32"), "fin": ("sbuf", [128, 16], "uint16"),
     "yb": ("sbuf", [128, P], "float32"),
-    "nr16": ("sbuf", [1, S1], "uint16"), "nr": ("sbuf", [128, S1 + 8], "float32"), "ng": ("sbuf", [128, 384], "float32"),
-    "ngt": ("sbuf", [32, 384], "float32"), "v2s": ("sbuf", [128, 4], "uint16"), "v2l": ("sbuf", [128, 32], "uint16"),
+    "nr16": ("sbuf", [1, S1], "uint16"), "nr": ("sbuf", [128, S1 + 8], "float32"), "ng": ("sbuf", [128, 288], "float32"),
+    "ngt": ("sbuf", [32, 288], "float32"), "v2s": ("sbuf", [128, 4], "uint16"), "v2l": ("sbuf", [128, 32], "uint16"),
     "xn": ("sbuf", [128, 128], "float32"), "xnt": ("sbuf", [128, 128], "float32"), "nw": ("sbuf", [128, S1 + 8], "float32"),
     "nout": ("sbuf", [128, P], "float32"),
-    "pz": ("psum", [128, 1024], "float32"), "pmm": ("psum", [128, 1536], "float32"), "py": ("psum", [128, 1024], "float32"),
+    "pz": ("psum", [128, 2048], "float32"), "pmm": ("psum", [128, 1536], "float32"),
 }
-SEMAPHORES = ["vs", "sa", "ts", "gc", "dpl", "dx0", "dx1", "dw", "dz", "dn", "so", "sp", "ls", "a0", "a1", "m1r", "a2", "a3", "m2r"]
+SEMAPHORES = ["vs", "sa", "ts", "gc", "dpl", "dx0", "dx1", "dw", "dz", "dn", "so", "ls", "a0", "a1", "m1r", "a2", "a3", "m2r"]
 
 
 def share(topo, src, dsts):
@@ -144,63 +146,72 @@ def rank_program(g, core, T, topo):
             count["ls"] = count.get("ls", 0) + len(es)
         g.remote_dma_fused(tr, local_sem=T.sem.ls)
 
-    tpl = dma("s", [], "dpl", T.plt[:], T.pl[:])
-    tx1 = dma("a", [], "dx1", T.xt[:, 512:1024], T.x[:, 512:1024])
-    tx0 = dma("s", [], "dx0", T.xt[:, 0:512], T.x[:, 0:512])
+    tpl = dma("s", [], "dpl", T.plt[:, 0:8], T.pl[:, 0:8])
+    tx1 = dma("a", [], "dx1", T.xt[:, 4 * H:8 * H], T.x[:, 4 * H:8 * H])
+    tx0 = dma("s", [], "dx0", T.xt[:, 0:4 * H], T.x[:, 0:4 * H])
     tw = dma("s", [], "dw", T.wt[:], T.w[:])
 
+    fl = {"allow_small_or_imprecise_dtypes": True}
+    tpn = op("g", [], "iota", T.pn[:], [[0, 1]], 0, 1)
+    tio = op("g", [], "iota", T.io16[:], [[16, 16]], 0, 1, **fl)
+    tzf = op("g", [], "iota", T.zf[:], [[0, 128]], 0, 0, **fl)
+    ton = op("g", [], "iota", T.one[:], [[0, 24]], 1, 0, **fl)
+    tz4 = op("v", [], "set", T.plt[:, 12:512], 0.0)
+    tz5 = op("v", [], "set", T.xt[:, 4 * P:4 * P + 8], 0.0)
+    a = op("v", [tpn], "ts", T.pm16[:], T.pn[:], 112, None, A.bitwise_and)
+    op("v", [], "ts", T.ph5[:], T.pn[:], 5, None, A.logical_shift_right)
     op("v", [], "set", T.ploff[:, 0:8], 0)
     op("v", [], "set", T.ploff[:, 8:12], 1)
     tpo = op("v", [], "set", T.ploff[:, 12:16], 2)
-    tz4 = op("v", [], "set", T.xt[:, 4 * P:4 * P + 8], 0.0)
+    a = op("v", [a], "copy", T.r16[:], T.pm16[:])
     for qd in range(4):
         op("v", [], "set", T.bd[32 * qd:32 * qd + 32, 0:1], float(qd & 1))
-        tbd = op("v", [], "set", T.bd[32 * qd:32 * qd + 32, 1:2], TINY if qd & 2 else 0.0)
-    tzb = op("v", [], "set", T.zb[:], 0.0)
-    tpn = op("g", [], "iota", T.pn[:], [[0, 1]], 0, 1)
-    tio = op("g", [], "iota", T.io16[:], [[16, 16]], 0, 1, allow_small_or_imprecise_dtypes=True)
-    tzf = op("v", [], "set", T.zf[:], 0.0)
-    tn1 = op("v", [], "set", T.neg1[:], -0.9375)
-    ton = op("v", [], "set", T.one[:], 1.0)
-    tlz = op("v", [], "set", T.lq[:, 5:6], 0.0)
-    a = op("v", [tpn], "ts", T.pm16[:], T.pn[:], 112, None, A.bitwise_and)
-    b = op("v", [tpn], "ts", T.ph5[:], T.pn[:], 5, None, A.logical_shift_right)
-    a = op("v", [a], "copy", T.r16[:], T.pm16[:])
-    tq5 = op("v", [b], "copy", T.q5[:], T.ph5[:])
     tb16 = op("v", [a, tio], "ts", T.b16[:], T.io16[:], T.r16[:, 0:1], None, A.subtract)
-    tb16h = op("v", [tb16], "ts", T.b16h[:], T.b16[:, 0:8], 0.5, None, A.add)
-    tid = op("g", [tn1], "aff", T.idm[:], T.neg1[:], [[-1, 128]], A.is_equal, 0.0, 0, 1)
-    tng = op("g", [tzf], "aff", T.nega[:], T.zf[:], [[-1, 128]], A.is_gt, -BIG, 0, 1)
-    tn0 = op("g", [tng], "aff", T.neg0[:], T.nega[:], [[1, 128]], A.is_gt, BIG, 0, 1)
+    op("v", [], "set", T.bd[0:64, 1:2], 0.0)
+    tbd = op("v", [], "set", T.bd[64:128, 1:2], TINY)
+    tzb = op("v", [], "set", T.zb[:], 0.0)
     a = op("g", [ton], "aff", T.mka[:], T.one[:], [[0, 4], [-16, 6]], A.is_ge, 0.0, 0, 1)
     tmk = op("g", [a], "aff", T.mk[:], T.mka[:], [[0, 4], [16, 6]], A.is_ge, 0.0, 15, -1)
-    op("g", [ton], "aff", T.mo[:, 0:2], T.one[:, 0:2], [[-CAPP, 2]], A.is_equal, 0.0, 0, 1)
-    tmo = op("g", [ton], "aff", T.mo[:, 2:4], T.one[:, 0:2], [[-CAPP, 2]], A.is_equal, 0.0, 128 - 2 * CAPP, 1)
+    op("g", [], "aff", T.mo[:, 0:2], T.one[:, 0:2], [[-CAPP, 2]], A.is_equal, 0.0, 0, 1)
+    tmo = op("g", [], "aff", T.mo[:, 2:4], T.one[:, 0:2], [[-CAPP, 2]], A.is_equal, 0.0, 128 - 2 * CAPP, 1)
+    tid = op("g", [tzf], "aff", T.idm[:], T.zf[:], [[-1, 128]], A.not_equal, -0.9375, 0, 1)
+    tng = op("g", [tzf], "aff", T.nega[:], T.zf[:], [[-1, 128]], A.is_gt, -BIG, 0, 1)
+    tn0 = op("g", [tng], "aff", T.neg0[:], T.nega[:], [[1, 128]], A.is_gt, BIG, 0, 1)
 
     a = op("v", [tpl], "ts", T.plt[:, 8:12], T.plt[:, 4:8], -1.0, None, A.mult)
-    tplq = op("v", [a], "qmx", T.plq[:], T.pls[:], T.plt[:])
-    tprq = op("v", [tplq, tpo], "copy", T.prq[:].bitcast(u32), T.plq[:].bitcast(u32).indirect(T.ploff[:]))
-    tprs = op("a", [tplq, tpo], "act", T.prs[:], T.pls[:].indirect(T.ploff[:]), F.Copy)
-    tq0 = op("v", [tx0], "qmx", T.xq[:, 0:128], T.xs[:, 0:128], T.xt[:, 0:512])
-    tq1 = op("v", [tx1, tz4], "qmx", T.xq[:, 128:P + 2], T.xs[:, 128:P + 2], T.xt[:, 512:4 * P + 8])
-    tq = [tq0, tq1]
+    tplq = op("v", [a, tz4], "qmx", T.plq[:], T.pls[:], T.plt[:])
+
+    def plane(b):
+        c = op("v", [tplq, tpo], "copy", T.prq[:, 128 * b:128 * b + 128].bitcast(u32), T.plq[:].bitcast(u32).indirect(T.ploff[:, 8 * b:8 * b + 8]))
+        s = op("a", [tplq, tpo], "act", T.prs[:, 128 * b:128 * b + 128], T.pls[:].indirect(T.ploff[:, 8 * b:8 * b + 8]), F.Copy)
+        return [c, s]
+    tpr = [plane(0)]
+    tq = [op("v", [tx0], "qmx", T.xq[:, 0:H], T.xs[:, 0:H], T.xt[:, 0:4 * H]),
+          op("v", [tx1, tz5], "qmx", T.xq[:, H:P + 2], T.xs[:, H:P + 2], T.xt[:, 4 * H:4 * P + 8])]
+    tpr.append(plane(1))
     for d in ("l1", "l2"):
         dma("s", tq, "dz", T[d + "q"][:, S1:S1 + 2].bitcast(u8), T.xq[:, P:P + 2].bitcast(u8))
         tdz = dma("s", tq, "dz", T[d + "s"][:, S1:S1 + 2], T.xs[:, P:P + 2])
-    tz0 = op("t", [tprq, tprs] + tq, "mm", T.pz[:, 0:P], T.prq[:, 0:128], T.prs[:, 0:128], T.xq[:, 0:P], T.xs[:, 0:P], True, True)
-    tz1 = op("t", [], "mm", T.pz[:, 512:512 + P], T.prq[:, 128:256], T.prs[:, 128:256], T.xq[:, 0:P], T.xs[:, 0:P], True, True)
+    tz = []
+    for b in range(2):
+        for h in range(2):
+            c0 = 512 * (2 * b + h)
+            tz.append(op("t", tpr[b] + [tq[h]], "mm", T.pz[:, c0:c0 + H], T.prq[:, 128 * b:128 * b + 128], T.prs[:, 128 * b:128 * b + 128],
+                         T.xq[:, H * h:H * h + H], T.xs[:, H * h:H * h + H], True, True))
 
-    a = op("v", [tz0, tbd], "ts", T.t0[:], T.pz[:, 0:P], 0.0, T.bd[:, 0:1], A.is_lt, A.not_equal)
-    a = op("a", [a, tbd], "act", T.th[:], T.t0[:], F.Identity, bias=T.bd[:, 1:2], scale=BIG)
-    a = op("v", [a, tz1], "tt", T.ind[:], T.pz[:, 512:512 + P], T.th[:], A.is_ge)
-    tc = op("v", [a, tzb], "scan", T.c1[:], T.ind[:], T.zb[:], 0.0, A.add, A.add)
+    e = [H * h for h in range(2)]
+    a = [op("v", [tz[h], tbd], "ts", T.t0[:, e[h]:e[h] + H], T.pz[:, 512 * h:512 * h + H], 0.0, T.bd[:, 0:1], A.is_lt, A.not_equal) for h in range(2)]
+    tlz = op("v", [], "set", T.lq[:, 5:6], 0.0)
+    tb16h = op("v", [tb16], "ts", T.b16h[:], T.b16[:, 0:8], 0.5, None, A.add)
+    a = [op("a", [a[h], tbd], "act", T.th[:, e[h]:e[h] + H], T.t0[:, e[h]:e[h] + H], F.Identity, bias=T.bd[:, 1:2], scale=BIG) for h in range(2)]
+    a = [op("v", [a[h], tz[2 + h]], "tt", T.ind[:, e[h]:e[h] + H], T.pz[:, 1024 + 512 * h:1024 + 512 * h + H], T.th[:, e[h]:e[h] + H], A.is_ge) for h in range(2)]
+    tc = op("v", [a[1], tzb], "scan", T.c1[:], T.ind[:], T.zb[:], 0.0, A.add, A.add)
     send([tc], "a0", "c", [(T.c1[:, P - 1:P], T.hl[:, 8 * me:8 * me + 1])] * 3)
     for m in range(3):
         tac = op("a", [tc, tb16h], "act", T.ja[:, P * m:P * m + P], T.c1[:], F.Sign, bias=T.b16h[:, m:m + 1], scale=-1.0,
                  accum_out=T.ac[:, m:m + 1])
     j3 = op("v", [tc, tb16], "ts", T.jv[:, 0:P], T.c1[:], T.b16[:, 3:4], None, A.is_le)
     j4 = op("v", [tc], "ts", T.jv[:, P:2 * P], T.c1[:], T.b16[:, 4:5], None, A.is_le)
-    tho = op("v", [tc], "copy", T.hl[:, 8 * me:8 * me + 1], T.c1[:, P - 1:P])
     op("v", [j3], "red", T.lq[:, 3:4], T.jv[:, 0:P], X, A.add)
     op("v", [j4], "red", T.lq[:, 4:5], T.jv[:, P:2 * P], X, A.add)
     tl = op("v", [tac, tlz], "ts", T.lq[:, 0:3], T.ac[:, 0:3], 0.5, P / 2.0, A.mult, A.add)
@@ -218,6 +229,7 @@ def rank_program(g, core, T, topo):
     o0 = CAPP * me
     for qd in range(4):
         tv = op("v", [tl], "copy", T.lw[32 * qd:32 * qd + 32, 18:24], T.lq[32 * me:32 * me + 32, 0:6])
+    tho = op("v", [tc], "copy", T.hl[:, 8 * me:8 * me + 1], T.c1[:, P - 1:P])
     toff = op("v", [tv], "copy", T.off1[:, 18:24], T.lw[:, 18:24])
     toc = op("v", [toff], "copy", T.l1q[:, o0:o0 + CAPP].bitcast(u32), T.xq[:, 0:P + 2].bitcast(u32).indirect(T.off1[:, 18:18 + C5]))
     tos = op("a", [toff], "act", T.l1s[:, o0:o0 + CAPP], T.xs[:, 0:P + 2].indirect(T.off1[:, 18:18 + C5]), F.Copy)
@@ -234,10 +246,11 @@ def rank_program(g, core, T, topo):
         tdn = dma("s", [am1, tm1o], "dn", T.nr16[0:1, CAPP * s:CAPP * s + CAPP], T.m1l[0:CAPP, 8 * s:8 * s + 1])
 
     twq = op("v", [tw], "qmx", T.wq[:], T.ws[:], T.wt[:])
-    a = op("v", [tb16, tq5], "ts", T.qb2[:], T.b16[:, 0:5], 4.0, T.q5[:, 0:1], A.mult, A.add)
-    tq2 = op("v", [a], "ts", T.qb2h[:], T.qb2[:], 0.5, None, A.add)
+    a = op("v", [], "ts", T.q5[:], T.ph5[:], -SHIFT, None, A.add)
     tsb8 = op("v", [], "ts", T.sb8[:], T.b16[:, 0:2], float(8 * (me + 1) + 8192), 0.125, A.add, A.mult)
+    a = op("v", [a, tb16], "ts", T.qb2[:], T.b16[:, 0:5], 4.0, T.q5[:, 0:1], A.mult, A.add)
     td1 = op("v", [], "set", T.d1[:, 128:S1], 0.0)
+    tq2 = op("v", [a], "ts", T.qb2h[:], T.qb2[:], 0.5, None, A.add)
     op("v", [], "set", T.ce[:], 0.0)
     op("v", [], "set", T.gs[:], 0.0)
     op("v", [], "set", T.a5[:], 0.0)
@@ -248,73 +261,92 @@ def rank_program(g, core, T, topo):
     op("v", [], "set", T.nr[:], 0.0)
     op("v", [], "set", T.nw[:], -1.0)
     op("v", [], "set", T.bb2[:], 0.0)
-    tset = op("v", [], "set", T.two[:], 2.0)
+    tset = op("v", [], "set", T.km[:], MARK)
     aa0 = ("a0", into["c"])
     for qd in range(4):
         a = op("v", [aa0, tho], "ts", T.cn1[32 * qd:32 * qd + 32, :], T.hl[32 * me:32 * me + 32, 0:32:8], 1.0, None, A.min)
-    a = op("v", [a, tset], "scan", T.ce[:, 1:5], T.cn1[:], T.zf[:, 0:4], 0.0, A.add, A.add)
+    a = op("v", [a, tset, tzf], "scan", T.ce[:, 1:5], T.cn1[:], T.zf[:, 0:4], 0.0, A.add, A.add)
     a = op("v", [a], "tt", T.fi[:], T.cn1[:], T.ce[:, 0:4], A.is_gt)
     a = op("v", [a, tmo], "tt", T.fo[:], T.fi[:], T.mo[:], A.mult)
     a = op("v", [a], "tt", T.ov[:], T.fo[:, 0:4:2], T.fo[:, 1:4:2], A.add)
-    tov = op("v", [a], "ts", T.th1[:], T.ov[:, 1:2], 4096.0, 0.5 - 256, A.mult, A.add)
+    op("v", [a], "ts", T.th0[:], T.ov[:, 0:1], 4.0 * BIG, None, A.mult)
+    tov = op("v", [], "ts", T.th1[:], T.ov[:, 1:2], 4096.0, 0.5 - 256, A.mult, A.add)
 
     aa1 = ("a1", into["c"] + into["p"])
-    blocks = {0: (0, 128, T.mb0, T.neg0[:], 0, 0), 1: (128, 256, T.mb1, T.nega[:], 512, 128), 2: (192, S1, T.mb2, T.nega[:], 1024, 384)}
-    tmm, tof, tdg = {}, {}, {}
+    first = {0: 0, 1: 128, 2: 192}
+    tmm, tmf, tof, tdg = {}, {}, {}, {}
+
+    def slots(out, b, i0, i1):
+        k0 = first[b]
+        return op("t", [aa1, toc, tos, tdz], "mm", out, T.l1q[:, k0:k0 + 128], T.l1s[:, k0:k0 + 128], T.l1q[:, i0:i1], T.l1s[:, i0:i1], True, True)
     for b in (1, 2, 0):
-        k0, n, mb, ng, c0, jc = blocks[b]
-        tmm[b] = op("t", [aa1, toc, tos, tdz], "mm", T.pmm[:, c0:c0 + n], T.l1q[:, k0:k0 + 128], T.l1s[:, k0:k0 + 128],
-                    T.l1q[:, 0:n], T.l1s[:, 0:n], True, True)
-    for b in (1, 2, 0):
-        k0, n, mb, ng, c0, jc = blocks[b]
-        a = op("v", [tmm[b], tid], "tt", T.db[:, 128 * b:128 * b + 128], T.pmm[:, c0 + k0:c0 + k0 + 128], T.idm[:], A.mult)
-        c = op("v", [tng, tn0], "tt", mb[:], T.pmm[:, c0 + k0:c0 + k0 + 128], ng, A.add)
-        a = op("v", [a], "red", T.nt[:, b:b + 1], T.db[:, 128 * b:128 * b + 128], X, A.add)
-        if k0:
-            tof[b] = op("a", [a, c], "act", T.jf[:, jc:jc + k0], T.pmm[:, c0:c0 + k0], F.Sign, bias=T.nt[:, b:b + 1],
-                        accum_out=T.acc[:, 4 + b:5 + b])
-        tdg[b] = op("a", [a, c], "act", T.jf[:, jc + k0:jc + k0 + 128], mb[:], F.Sign, bias=T.nt[:, b:b + 1],
+        tmm[b] = slots(T.pmm[:, 512 * b:512 * b + 128], b, first[b], first[b] + 128)
+    for b in (1, 2):
+        tmf[b] = slots(T.pz[:, 512 * b + 512:512 * b + 512 + first[b]], b, 0, first[b])
+    tdb, tmb = {}, {}
+
+    def diagonal(b):
+        tdb[b] = op("v", [tmm[b], tid], "tt", T.db[:, 128 * b:128 * b + 128], T.pmm[:, 512 * b:512 * b + 128], T.idm[:], A.mult)
+
+    def signs(b):
+        tmb[b] = op("v", [tmm[b], tng, tn0], "tt", T.mb[:, 128 * b:128 * b + 128], T.pmm[:, 512 * b:512 * b + 128], T.nega[:] if b else T.neg0[:], A.add)
+        a = op("v", [tdb[b]], "red", T.nt[:, b:b + 1], T.db[:, 128 * b:128 * b + 128], X, A.add)
+        if b == 0:
+            tdg[0] = op("v", [tmb[0]], "red", T.mx0[:], T.mb[:, 0:128], X, A.max)
+            return
+        tdg[b] = op("a", [a, tmb[b]], "act", T.jf[:, 128 * b:128 * b + 128], T.mb[:, 128 * b:128 * b + 128], F.Sign, bias=T.nt[:, b:b + 1],
                     accum_out=T.acc[:, b:b + 1])
-    a = op("v", [tof[2], tdg[2], tset], "ts", T.bb2[:, 0:1], T.acc[:, 2:3], T.acc[:, 6:7], 0.5 - S1, A.add, A.is_le)
+        j0 = 256 + 128 * b
+        tof[b] = op("a", [a, tmf[b]], "act", T.jf[:, j0:j0 + first[b]], T.pz[:, 512 * b + 512:512 * b + 512 + first[b]], F.Sign,
+                    bias=T.nt[:, b:b + 1], accum_out=T.acc[:, 4 + b:5 + b])
+    diagonal(1)
+    diagonal(2)
+    signs(1)
+    signs(2)
+    diagonal(0)
+    signs(0)
     b = op("v", [tof[1], tdg[1], tov], "ts", T.ev[:, 1:2], T.acc[:, 1:2], T.acc[:, 5:6], T.th1[:, 0:1], A.add, A.is_le)
-    tb2 = op("v", [a], "tr", T.bt2[:], T.bb2[:])
-    for i in (2, 3):
-        op("g", [tb2], "bc", T.d0[:, 192 + 32 * i:224 + 32 * i], T.bt2[32 * i:32 * i + 1, 0:32], 128)
-    a = op("v", [tdg[0], tov], "ts", T.ev[:, 0:1], T.acc[:, 0:1], 0.5 - 128, T.ov[:, 0:1], A.is_le, A.max)
-    a = op("v", [a, b, tset], "ts", T.bb[:], T.two[:], T.ev[:, 1:2], T.ev[:, 0:1], A.mult, A.add)
+    a = op("v", [tdg[0], tov], "ts", T.ev[:, 0:1], T.mx0[:], T.nt[:, 0:1], T.th0[:, 0:1], A.add, A.is_lt)
+    c = op("v", [tof[2], tdg[2], tset], "ts", T.bb2[:, 0:1], T.acc[:, 2:3], T.acc[:, 6:7], 0.5 - S1, A.add, A.is_le)
+    a = op("v", [a, b, tset], "ts", T.bb[:], T.km[:], T.ev[:, 0:1], T.ev[:, 1:2], A.mult, A.add)
+    tb2 = op("v", [c], "tr", T.bt2[:], T.bb2[:])
     tbt = op("v", [a], "tr", T.bt[:], T.bb[:])
-    tb = op("g", [tbt], "bc", T.d0[:, 96:128], T.bt[96:97, 0:32], 128)
-    for i in range(3):
+    for i in (2, 3):
+        tb = op("g", [tb2], "bc", T.rv[:, 64 + 32 * i:96 + 32 * i], T.bt2[32 * i:32 * i + 1, 0:32], 128)
+    for i in range(4):
         for qd in range(4):
-            out, src = T.d0[32 * qd:32 * qd + 32, 32 * i:32 * i + 32], T.bt[32 * i:32 * i + 32, 0:32]
+            out, src = T.rv[32 * qd:32 * qd + 32, 32 * i:32 * i + 32], T.bt[32 * i:32 * i + 32, 0:32]
             if qd < 2:
                 tv = op("v", [tbt], "copy", out, src)
             else:
                 ta = op("a", [tbt], "act", out, src, F.Copy)
-    a = op("v", [tb, tv, ta], "ts", T.d1[:, 0:128], T.d0[:, 0:128], 2.0, -2.0, A.is_ge, A.mult)
-    a = op("v", [], "ts", T.d0[:, 128:256], T.d0[:, 0:128], 2.0, None, A.is_ge)
-    tc2 = op("v", [a, td1], "scan", T.c2[:], T.d0[:], T.d1[:], 0.0, A.add, A.add)
-    send([tc2], "a2", "c", [(T.c2[:, S1 - 1:S1], T.cn2[:, 4 * me:4 * me + 1])] * 3)
+    trv = [tb, tv, ta]
+    tcs = op("v", trv, "red", T.cs[:], T.rv[:], X, A.add)
+    send([tcs], "a2", "c", [(T.cs[:], T.cn2[:, 4 * me:4 * me + 1])] * 3)
     aa2 = ("a2", into["c"])
 
+    op("a", trv, "act", T.d0[:, 0:128], T.rv[:, 0:128], F.Copy)
+    ta = op("a", [], "act", T.d0[:, 256:S1], T.rv[:, 128:192], F.Copy)
+    op("v", [], "ts", T.d1[:, 0:128], T.rv[:, 0:128], 1.0, -1.0, A.is_ge, A.mult)
+    a = op("v", [], "ts", T.d0[:, 128:256], T.rv[:, 0:128], 1.0, None, A.is_ge)
+    tc2 = op("v", [a, ta, td1], "scan", T.c2[:], T.d0[:], T.d1[:], -SHIFT, A.add, A.add)
     for m in range(3):
         tac = op("a", [tc2, tq2], "act", T.ja2[:, S1 * m:S1 * m + S1], T.c2[:], F.Sign, bias=T.qb2h[:, m:m + 1], scale=-1.0,
                  accum_out=T.ac2[:, m:m + 1])
+    tcn = op("v", [tcs], "copy", T.cn2[:, 4 * me:4 * me + 1], T.cs[:])
     j3 = op("v", [tc2, tq2], "ts", T.jv2[:, 0:S1], T.c2[:], T.qb2[:, 3:4], None, A.is_le)
     j4 = op("v", [], "ts", T.jv2[:, S1:2 * S1], T.c2[:], T.qb2[:, 4:5], None, A.is_le)
-    tcn = op("v", [], "copy", T.cn2[:, 4 * me:4 * me + 1], T.c2[:, S1 - 1:S1])
     op("v", [j3], "red", T.l2[:, 3:4], T.jv2[:, 0:S1], X, A.add)
     op("v", [j4], "red", T.l2[:, 4:5], T.jv2[:, S1:2 * S1], X, A.add)
     tl = op("v", [tac], "ts", T.l2[:, 0:3], T.ac2[:, 0:3], 0.5, S1 / 2.0, A.mult, A.add)
-    for e in range(4):
+    for d in range(4):
         for qd in range(4):
-            out, src = T.lst[32 * qd:32 * qd + 32, 8 * e:8 * e + 8], T.l2[32 * e:32 * e + 32, 0:8]
+            out, src = T.lst[32 * qd:32 * qd + 32, 8 * d:8 * d + 8], T.l2[32 * d:32 * d + 32, 0:8]
             if qd < 2:
                 tv = op("v", [tl], "copy", out, src)
             else:
                 ta = op("a", [tl], "act", out, src, F.Copy)
     tlst = [tv, ta]
-    tnr = op("v", [tdn, tset], "copy", T.nr[0:1, 0:S1], T.nr16[0:1, 0:S1])
 
     def places():
         return op("v", [aa2, tcn], "scan", T.gs[:, 1:5], T.cn2[:, 0:16:4], T.zf[:, 0:4], 0.0, A.add, A.add)
@@ -331,18 +363,20 @@ def rank_program(g, core, T, topo):
         tps = op("a", [to2, tdz, aa1], "act", T.s2s[:, 80 * x:80 * x + 80], T.l1s[:, 0:S1 + 2].indirect(T.off2[:, 8 * x:8 * x + C5]), F.Copy)
     send([tpc], "a3", "c", [(T.s2q[:, 80 * x:80 * x + 80].bitcast(u8), T.l2q[:, o0:o0 + CAPP].bitcast(u8)) for x in range(3)])
     send([tps], "a3", "p", [(T.s2s[:, 80 * x:80 * x + 80], T.l2s[:, o0:o0 + CAPP]) for x in range(3)])
-    tng = op("a", [tnr], "act", T.ng[:], T.nr[:].indirect(T.off2[:, 0:24]), F.Copy)
+    tnr = op("v", [tdn, tset], "copy", T.nr[0:1, 0:S1], T.nr16[0:1, 0:S1])
+    for x in range(3):
+        tgn = op("a", [tnr], "act", T.ng[:, 96 * x:96 * x + 96], T.nr[:].indirect(T.off2[:, 8 * x:8 * x + 6]), F.Copy)
     toc = op("v", [], "copy", T.l2q[:, o0:o0 + CAPP].bitcast(u32), T.l1q[:, 0:S1 + 2].bitcast(u32).indirect(T.off2[:, 24:24 + C5]))
     tos = op("a", [], "act", T.l2s[:, o0:o0 + CAPP], T.l1s[:, 0:S1 + 2].indirect(T.off2[:, 24:24 + C5]), F.Copy)
     tno = op("a", [tset], "act", T.nw[:, o0:o0 + CAPP], T.nr[:].indirect(T.off2[:, 24:24 + C5]), F.Copy)
-    a = op("v", [tng], "tr", T.ngt[:], T.ng[0:32, :])
+    a = op("v", [tgn], "tr", T.ngt[:], T.ng[0:32, :])
     for i in range(3):
-        tv2 = op("v", [a, tset], "copy", T.v2s[32 * i:32 * i + 32, 0:3], T.ngt[0:32, 32 * i:384:128])
+        tv2 = op("v", [a, tset], "copy", T.v2s[32 * i:32 * i + 32, 0:3], T.ngt[0:32, 32 * i:288:96])
     send([tv2], "m2r", "c", [(T.v2s[:, x:x + 1], T.v2l[:, 8 * me:8 * me + 1]) for x in range(3)])
 
     if me == 0:
         tgs = places()
-    a = op("v", [tgs], "ts", T.ai[:], T.gs[:, 1:5], float(3 - me), None, A.add)
+    a = op("v", [tgs], "ts", T.ai[:], T.gs[:, 1:5], 3.25 - me, None, A.add)
     a = op("v", [a], "ts", T.aj[:], T.ai[:], 2, None, A.logical_shift_right)
     a = op("v", [a, tset], "copy", T.a5[:, 1:5], T.aj[:])
     a = op("v", [a], "tt", T.wd[:], T.a5[:, 0:4], T.a5[:, 1:5], A.subtract)
@@ -357,26 +391,30 @@ def rank_program(g, core, T, topo):
     aa3 = ("a3", into["c"] + into["p"])
     tfc, tfs, ty = [], [], []
     for h in range(2):
-        tfc.append(op("v", [aa3, tfin, toc, tdz], "copy", T.oq[:, 128 * h:128 * h + 128].bitcast(u32), T.l2q[:, 0:S1 + 2].bitcast(u32).indirect(T.fin[:, 8 * h:8 * h + 8])))
-        tfs.append(op("a", [aa3, tfin, tos, tdz], "act", T.os_[:, 128 * h:128 * h + 128], T.l2s[:, 0:S1 + 2].indirect(T.fin[:, 8 * h:8 * h + 8]), F.Copy))
-        ty.append(op("t", [tfc[h], tfs[h], twq], "mm", T.py[:, 512 * h:512 * h + 128], T.wq[:], T.ws[:], T.oq[:, 128 * h:128 * h + 128], T.os_[:, 128 * h:128 * h + 128], True, True))
+        tfc.append(op("v", [aa3, tfin, toc, tdz], "copy", T.oq[:, H * h:H * h + H].bitcast(u32), T.l2q[:, 0:S1 + 2].bitcast(u32).indirect(T.fin[:, 8 * h:8 * h + 8])))
+        tfs.append(op("a", [aa3, tfin, tos, tdz], "act", T.os_[:, H * h:H * h + H], T.l2s[:, 0:S1 + 2].indirect(T.fin[:, 8 * h:8 * h + 8]), F.Copy))
+        ty.append(op("t", [tfc[h], tfs[h], twq], "mm", T.pz[:, 512 * h:512 * h + H], T.wq[:], T.ws[:], T.oq[:, H * h:H * h + H], T.os_[:, H * h:H * h + H], True, True))
+    b0 = op("a", [ty[0]], "act", T.yb[:, 0:H], T.pz[:, 0:H], F.Copy)
+    b1 = op("a", [ty[1]], "act", T.yb[:, H:P], T.pz[:, 512:512 + H], F.Copy)
     for h in range(2):
-        dma("s", [tfc[h]], "so", T.oc[:, 512 * h:512 * h + 512], T.oq[:, 128 * h:128 * h + 128].bitcast(u8))
+        dma("s", [tfc[h]], "so", T.oc[:, 4 * H * h:4 * H * h + 4 * H], T.oq[:, H * h:H * h + H].bitcast(u8))
+    dma("s", [b0], "so", T.y[:, 0:H], T.yb[:, 0:H])
+    dma("s", [b1], "so", T.y[:, H:P], T.yb[:, H:P])
     for i in range(4):
         dma("s", tfs, "so", T.osc[4 * i:4 * i + 4, :], T.os_[32 * i:32 * i + 4, :])
-    b0 = op("v", [ty[0]], "copy", T.yb[:, 0:128], T.py[:, 0:128])
-    b1 = op("a", [ty[1]], "act", T.yb[:, 128:256], T.py[:, 512:640], F.Copy)
-    dma("s", [b0], "so", T.y[:, 0:128], T.yb[:, 0:128])
-    dma("a", [b1], "sp", T.y[:, 128:256], T.yb[:, 128:256])
     a = op("v", [("m2r", into["c"]), tset], "copy", T.xn[:, 0:128:32], T.v2l[:, 0:32:8])
     a = op("v", [a], "tr", T.xnt[:], T.xn[:])
-    for d in range(4):
-        if d != me:
-            for i in range(3):
-                w = min(32, CAPP - 32 * i)
-                b = op("v", [a, tset], "copy", T.nw[0:1, CAPP * d + 32 * i:CAPP * d + 32 * i + w], T.xnt[32 * i:32 * i + 1, 32 * d:32 * d + w])
-    a = op("v", [b, tno, tfin], "copy", T.nout[:], T.nw[:].indirect(T.fin[:]))
-    dma("s", [a], "so", T.num[:], T.nout[0:1, :])
+    for d in order[:3]:
+        for i in range(3):
+            w = min(32, CAPP - 32 * i)
+            out, src = T.nw[0:1, CAPP * d + 32 * i:CAPP * d + 32 * i + w], T.xnt[32 * i:32 * i + 1, 32 * d:32 * d + w]
+            if i == 1:
+                ta = op("a", [a, tset], "act", out, src, F.Copy)
+            else:
+                tv = op("v", [a, tset], "copy", out, src)
+    a = op("v", [tv, ta, tno, tfin], "copy", T.nout[:, 0:H], T.nw[:].indirect(T.fin[:, 0:8]))
+    b = op("a", [tv, ta, tno, tfin], "act", T.nout[:, H:P], T.nw[:].indirect(T.fin[:, 8:16]), F.Copy)
+    dma("s", [a, b], "so", T.num[:], T.nout[0:1, :])
 
     wait("g", [(s, v) for s, v in count.items()])
     wait("g", [am1, aa0, aa1, aa2, aa3, ("m2r", into["c"])])

@@ -5,10 +5,13 @@ N, P, CAPP = 4, 256, 80
 H = P // 2
 S1 = N * CAPP
 C5 = CAPP // 16
+RUN = 96
+S2 = N * RUN
 BIG = 1.0e29
 TINY = 1.0e-36
 MARK = 1.0 - 2.0 ** -14
 SHIFT = 64.0
+WHOLE = 3 * 2 ** 22
 
 CODE = "float8_e4m3fn_x4"
 SCRATCH = {
@@ -22,64 +25,72 @@ SCRATCH = {
     "s1q": ("sbuf", [128, 272], CODE), "s1s": ("sbuf", [128, 272], "uint8"),
     "l1q": ("sbuf", [128, S1 + 8], CODE), "l1s": ("sbuf", [128, S1 + 8], "uint8"),
     "s2q": ("sbuf", [128, 240], CODE), "s2s": ("sbuf", [128, 240], "uint8"),
-    "l2q": ("sbuf", [128, S1 + 8], CODE), "l2s": ("sbuf", [128, S1 + 8], "uint8"),
+    "l2q": ("sbuf", [128, S2 + 8], CODE), "l2s": ("sbuf", [128, S2 + 8], "uint8"),
     "oq": ("sbuf", [128, P], CODE), "os_": ("sbuf", [128, P], "uint8"),
     "ploff": ("sbuf", [128, 16], "uint16"),
     "pn": ("sbuf", [128, 1], "int32"), "pm16": ("sbuf", [128, 1], "int32"), "ph5": ("sbuf", [128, 1], "int32"),
     "r16": ("sbuf", [128, 1], "float32"), "q5": ("sbuf", [128, 1], "float32"),
     "io16": ("sbuf", [128, 16], "float32"), "b16": ("sbuf", [128, 16], "float32"), "b16h": ("sbuf", [128, 8], "float32"),
-    "qb2": ("sbuf", [128, 5], "float32"), "qb2h": ("sbuf", [128, 5], "float32"), "sb8": ("sbuf", [128, 2], "float32"),
+    "qb2": ("sbuf", [128, 5], "float32"), "qb2h": ("sbuf", [128, 5], "float32"),
+    "sbx": ("sbuf", [128, 2], "float32"), "qn": ("sbuf", [128, 2], "float32"), "sg8": ("sbuf", [128, 1], "float32"),
+    "rm4": ("sbuf", [128, 1], "float32"), "p7f": ("sbuf", [128, 1], "float32"),
     "bd": ("sbuf", [128, 4], "float32"),
     "idm": ("sbuf", [128, 128], "float32"), "zf": ("sbuf", [128, 128], "float32"),
     "nega": ("sbuf", [128, 128], "float32"), "neg0": ("sbuf", [128, 128], "float32"),
     "one": ("sbuf", [128, 24], "float32"), "mka": ("sbuf", [128, 24], "float32"), "mk": ("sbuf", [128, 24], "float32"),
     "mo": ("sbuf", [128, 4], "float32"),
     "zb": ("sbuf", [128, P], "bfloat16"), "km": ("sbuf", [128, 32], "float32"),
+    "mrun": ("sbuf", [128, 4], "float32"), "io64": ("sbuf", [128, 64], "float32"), "wb": ("sbuf", [128, 1], "float32"),
+    "bw": ("sbuf", [128, 64], "float32"),
     "t0": ("sbuf", [128, P], "bfloat16"), "th": ("sbuf", [128, P], "float32"), "ind": ("sbuf", [128, P], "bfloat16"),
     "c1": ("sbuf", [128, P], "bfloat16"), "jv": ("sbuf", [128, 2 * P], "bfloat16"), "ja": ("sbuf", [128, 3 * P], "bfloat16"),
-    "ac": ("sbuf", [128, 4], "float32"), "lq": ("sbuf", [128, 8], "float32"), "lw": ("sbuf", [128, 24], "float32"),
+    "ac": ("sbuf", [128, 8], "float32"), "lq": ("sbuf", [128, 8], "float32"), "lw": ("sbuf", [128, 24], "float32"),
     "off1": ("sbuf", [128, 24], "uint16"),
     "tm": ("sbuf", [128, 24], "float32"), "rn": ("sbuf", [128, 4], "float32"),
     "hl": ("sbuf", [128, 32], "bfloat16"), "m1s": ("sbuf", [128, 4], "uint16"), "m1l": ("sbuf", [128, 32], "uint16"),
     "db": ("sbuf", [128, 384], "float32"), "mb": ("sbuf", [128, 384], "float32"), "mx0": ("sbuf", [128, 1], "float32"),
-    "nt": ("sbuf", [128, 4], "float32"), "acc": ("sbuf", [128, 8], "float32"), "jf": ("sbuf", [128, 704], "bfloat16"),
+    "nt": ("sbuf", [128, 4], "float32"), "acc": ("sbuf", [128, 8], "float32"), "jf": ("sbuf", [128, 1088], "bfloat16"),
     "cn1": ("sbuf", [128, 4], "float32"), "ce": ("sbuf", [128, 8], "float32"), "fi": ("sbuf", [128, 4], "float32"),
     "fo": ("sbuf", [128, 4], "float32"), "ov": ("sbuf", [128, 2], "float32"), "th0": ("sbuf", [128, 1], "float32"),
     "th1": ("sbuf", [128, 1], "float32"),
     "ev": ("sbuf", [128, 4], "float32"), "bb": ("sbuf", [128, 32], "float32"), "bt": ("sbuf", [128, 32], "float32"),
     "bb2": ("sbuf", [128, 32], "float32"), "bt2": ("sbuf", [128, 32], "float32"),
-    "rv": ("sbuf", [128, 192], "float32"), "cs": ("sbuf", [128, 1], "float32"), "cn2": ("sbuf", [128, 16], "float32"),
-    "d0": ("sbuf", [128, S1], "float32"), "d1": ("sbuf", [128, S1], "float32"), "c2": ("sbuf", [128, S1], "bfloat16"),
+    "rv": ("sbuf", [128, 192], "float32"), "rvj": ("sbuf", [128, 192], "float32"), "cs": ("sbuf", [128, 1], "float32"),
+    "cn2": ("sbuf", [128, 16], "float32"),
+    "d0": ("sbuf", [128, S1], "bfloat16"), "d1": ("sbuf", [128, S1], "bfloat16"), "c2": ("sbuf", [128, S1], "bfloat16"),
     "jv2": ("sbuf", [128, 2 * S1], "bfloat16"), "ja2": ("sbuf", [128, 3 * S1], "bfloat16"),
-    "ac2": ("sbuf", [128, 4], "float32"), "l2": ("sbuf", [128, 8], "float32"), "lst": ("sbuf", [128, 32], "float32"),
-    "gs": ("sbuf", [128, 8], "float32"), "ei": ("sbuf", [128, 2], "int32"), "seli": ("sbuf", [128, 2], "int32"),
-    "sel": ("sbuf", [128, 2], "uint16"), "off2": ("sbuf", [128, 32], "uint16"),
-    "ai": ("sbuf", [128, 4], "int32"), "aj": ("sbuf", [128, 4], "int32"), "a5": ("sbuf", [128, 8], "float32"),
-    "wd": ("sbuf", [128, 4], "float32"), "we": ("sbuf", [128, 4], "float32"), "tp": ("sbuf", [128, 64], "float32"),
+    "ac2": ("sbuf", [128, 8], "float32"), "lst": ("sbuf", [128, 32], "float32"),
+    "ef": ("sbuf", [128, 2], "float32"), "ei": ("sbuf", [128, 2], "int32"),
+    "seli": ("sbuf", [128, 2], "int32"), "sel": ("sbuf", [128, 2], "uint16"), "off2": ("sbuf", [128, 32], "uint16"),
+    "gs": ("sbuf", [128, 8], "float32"), "a5": ("sbuf", [128, 8], "float32"),
+    "we": ("sbuf", [128, 4], "float32"), "tp": ("sbuf", [128, 64], "float32"),
     "ta": ("sbuf", [128, 64], "float32"), "fin": ("sbuf", [128, 16], "uint16"),
     "yb": ("sbuf", [128, P], "float32"),
-    "nr16": ("sbuf", [1, S1], "uint16"), "nr": ("sbuf", [128, S1 + 8], "float32"), "ng": ("sbuf", [128, 288], "float32"),
-    "ngt": ("sbuf", [32, 288], "float32"), "v2s": ("sbuf", [128, 4], "uint16"), "v2l": ("sbuf", [128, 32], "uint16"),
-    "xn": ("sbuf", [128, 128], "float32"), "xnt": ("sbuf", [128, 128], "float32"), "nw": ("sbuf", [128, S1 + 8], "float32"),
+    "nr16": ("sbuf", [1, S1], "uint16"), "nr": ("sbuf", [128, S1 + 8], "float32"), "ng": ("sbuf", [128, S2 - RUN], "float32"),
+    "ngt": ("sbuf", [32, S2 - RUN], "float32"), "v2s": ("sbuf", [128, 4], "uint16"), "v2l": ("sbuf", [128, 32], "uint16"),
+    "xn": ("sbuf", [32, S2], "float32"), "nw": ("sbuf", [128, S2 + 8], "float32"),
     "nout": ("sbuf", [128, P], "float32"),
     "pz": ("psum", [128, 2048], "float32"), "pmm": ("psum", [128, 1536], "float32"),
 }
 SEMAPHORES = ["vs", "sa", "ts", "gc", "dpl", "dx0", "dx1", "dw", "dz", "dn", "so", "ls", "a0", "a1", "m1r", "a2", "a3", "m2r"]
 
 
-def share(topo, src, dsts):
+def far(topo, src, dst):
+    a, b = topo.chip(src), topo.chip(dst)
+    return a != b and not topo.mates(a, b) and not topo.same_plane(a, b)
+
+
+def others(topo, r, cores):
+    o = [(r + 1 + x) % N for x in range(N - 1)]
+    return sorted(o, key=lambda d: not far(topo, cores[r], cores[d]))
+
+
+def split(topo, src, dsts):
     el = topo.engines(src, dsts[0])
     for d in dsts[1:]:
         el = [e for e in el if e in topo.engines(src, d)]
-    q = len(el) // 4
-    part = [el[i * q:(i + 1) * q] for i in range(4)]
-
-    def far(d):
-        a, b = topo.chip(src), topo.chip(d)
-        return not topo.mates(a, b) and not topo.same_plane(a, b)
-    lead = ([d for d in dsts if far(d)] or [dsts[-1]])[0]
-    rest = [d for d in dsts if d != lead]
-    return {lead: (part[2] + part[3], part[0] + part[1]), rest[0]: (part[0], part[2]), rest[1]: (part[1], part[3])}
+    q = len(el) // len(dsts)
+    return [el[i * q:(i + 1) * q] for i in range(len(dsts))]
 
 
 def bits(es):
@@ -125,26 +136,34 @@ def rank_program(g, core, T, topo):
         count[s] = count.get(s, 0) + 16
         return (s, count[s])
 
-    order = [(me + 1 + x) % N for x in range(N)]
-    peers = [T.cores[r] for r in order[:3]]
-    mine = share(topo, core, peers)
-    into = {"c": 0, "p": 0}
+    def move(q, deps, out, src):
+        return op(q, deps, "copy", out, src) if q == "v" else op(q, deps, "act", out, src, F.Copy)
+
+    order = others(topo, me, T.cores) + [me]
+    o0, o2 = CAPP * me, RUN * me
+    into = 0
     for r in range(N):
         if r != me:
-            sh = share(topo, T.cores[r], [T.cores[(r + 1 + x) % N] for x in range(3)])[core]
-            into["c"] += len(sh[0])
-            into["p"] += len(sh[1])
+            o = others(topo, r, T.cores)
+            for grp in (o[:1], o[1:]):
+                if me in grp:
+                    into += len(split(topo, T.cores[r], [T.cores[d] for d in grp])[grp.index(me)])
 
-    def send(deps, sem, kind, pieces):
+    def send(deps, sem, xs, piece):
         wait("g", deps)
+        dst = [T.cores[order[x]] for x in xs]
         tr = []
-        for d, (src, dst) in zip(peers, pieces):
+        for x, d, es in zip(xs, dst, split(topo, core, dst)):
             rid, pid = topo.addr(d)[:2]
-            es = mine[d][0 if kind == "c" else 1]
+            p_src, p_dst = piece(x)
             tr.append(RemoteDMATransfer(dst_ids=[DstId(rid=rid, pnc=pid)], dma_engine_mask=bits(es),
-                                        remote_sem=T.sem[sem], src=src, dst=dst))
+                                        remote_sem=T.sem[sem], src=p_src, dst=p_dst))
             count["ls"] = count.get("ls", 0) + len(es)
         g.remote_dma_fused(tr, local_sem=T.sem.ls)
+
+    def send_all(deps, sem, piece):
+        send(deps, sem, [0], piece)
+        send(deps, sem, [1, 2], piece)
 
     tpl = dma("s", [], "dpl", T.plt[:, 0:8], T.pl[:, 0:8])
     tx1 = dma("a", [], "dx1", T.xt[:, 4 * H:8 * H], T.x[:, 4 * H:8 * H])
@@ -159,17 +178,18 @@ def rank_program(g, core, T, topo):
     tz4 = op("v", [], "set", T.plt[:, 12:512], 0.0)
     tz5 = op("v", [], "set", T.xt[:, 4 * P:4 * P + 8], 0.0)
     a = op("v", [tpn], "ts", T.pm16[:], T.pn[:], 112, None, A.bitwise_and)
-    op("v", [], "ts", T.ph5[:], T.pn[:], 5, None, A.logical_shift_right)
+    tp5 = op("v", [], "ts", T.ph5[:], T.pn[:], 5, None, A.logical_shift_right)
     op("v", [], "set", T.ploff[:, 0:8], 0)
     op("v", [], "set", T.ploff[:, 8:12], 1)
     tpo = op("v", [], "set", T.ploff[:, 12:16], 2)
-    a = op("v", [a], "copy", T.r16[:], T.pm16[:])
+    tr16 = op("v", [a], "copy", T.r16[:], T.pm16[:])
     for qd in range(4):
         op("v", [], "set", T.bd[32 * qd:32 * qd + 32, 0:1], float(qd & 1))
-    tb16 = op("v", [a, tio], "ts", T.b16[:], T.io16[:], T.r16[:, 0:1], None, A.subtract)
+    tb16 = op("v", [tr16, tio], "ts", T.b16[:], T.io16[:], T.r16[:, 0:1], None, A.subtract)
     op("v", [], "set", T.bd[0:64, 1:2], 0.0)
     tbd = op("v", [], "set", T.bd[64:128, 1:2], TINY)
     tzb = op("v", [], "set", T.zb[:], 0.0)
+    op("a", [tzf], "act", T.km[:], T.zf[:, 0:32], F.Identity, bias=MARK)
     a = op("g", [ton], "aff", T.mka[:], T.one[:], [[0, 4], [-16, 6]], A.is_ge, 0.0, 0, 1)
     tmk = op("g", [a], "aff", T.mk[:], T.mka[:], [[0, 4], [16, 6]], A.is_ge, 0.0, 15, -1)
     op("g", [], "aff", T.mo[:, 0:2], T.one[:, 0:2], [[-CAPP, 2]], A.is_equal, 0.0, 0, 1)
@@ -189,9 +209,9 @@ def rank_program(g, core, T, topo):
     tq = [op("v", [tx0], "qmx", T.xq[:, 0:H], T.xs[:, 0:H], T.xt[:, 0:4 * H]),
           op("v", [tx1, tz5], "qmx", T.xq[:, H:P + 2], T.xs[:, H:P + 2], T.xt[:, 4 * H:4 * P + 8])]
     tpr.append(plane(1))
-    for d in ("l1", "l2"):
-        dma("s", tq, "dz", T[d + "q"][:, S1:S1 + 2].bitcast(u8), T.xq[:, P:P + 2].bitcast(u8))
-        tdz = dma("s", tq, "dz", T[d + "s"][:, S1:S1 + 2], T.xs[:, P:P + 2])
+    for d, e in (("l1", S1), ("l2", S2)):
+        dma("s", tq, "dz", T[d + "q"][:, e:e + 2].bitcast(u8), T.xq[:, P:P + 2].bitcast(u8))
+        tdz = dma("s", tq, "dz", T[d + "s"][:, e:e + 2], T.xs[:, P:P + 2])
     tz = []
     for b in range(2):
         for h in range(2):
@@ -199,222 +219,270 @@ def rank_program(g, core, T, topo):
             tz.append(op("t", tpr[b] + [tq[h]], "mm", T.pz[:, c0:c0 + H], T.prq[:, 128 * b:128 * b + 128], T.prs[:, 128 * b:128 * b + 128],
                          T.xq[:, H * h:H * h + H], T.xs[:, H * h:H * h + H], True, True))
 
+    def heads(jv, sz, step):
+        for k, m in enumerate((1, 3)):
+            t = op("v", [], "set", jv[:, sz * k + sz - step * m:sz * k + sz - step * m + 1], float(step * m))
+        return t
+
+    def lists(c, sz, step, off, offh, deps, jv, ja, ac, lq):
+        n = [sz - step * m for m in range(C5)]
+        t, tacc = {}, {}
+        for k, m in enumerate((1, 3)):
+            t[m] = op("v", deps, "ts", jv[:, sz * k:sz * k + n[m]], c[:, sz - n[m]:sz], off[:, m:m + 1], None, A.is_le)
+        for k, m in enumerate((0, 2, 4)):
+            tacc[m] = op("a", deps, "act", ja[:, sz * k:sz * k + n[m]], c[:, sz - n[m]:sz], F.Sign, bias=offh[:, m:m + 1], scale=-1.0,
+                         accum_out=ac[:, m:m + 1])
+        for k, m in enumerate((1, 3)):
+            op("v", [t[m]], "red", lq[:, m:m + 1], jv[:, sz * k:sz * k + n[m] + 1], X, A.add)
+        for m in (0, 2, 4):
+            r = op("v", [tacc[m]], "ts", lq[:, m:m + 1], ac[:, m:m + 1], 0.5, 0.5 * (n[m] + 2 * step * m), A.mult, A.add)
+        return r
+
     e = [H * h for h in range(2)]
     a = [op("v", [tz[h], tbd], "ts", T.t0[:, e[h]:e[h] + H], T.pz[:, 512 * h:512 * h + H], 0.0, T.bd[:, 0:1], A.is_lt, A.not_equal) for h in range(2)]
-    tlz = op("v", [], "set", T.lq[:, 5:6], 0.0)
+    heads(T.jv, P, 16)
+    op("v", [], "set", T.lq[:, 5:6], 0.0)
     tb16h = op("v", [tb16], "ts", T.b16h[:], T.b16[:, 0:8], 0.5, None, A.add)
     a = [op("a", [a[h], tbd], "act", T.th[:, e[h]:e[h] + H], T.t0[:, e[h]:e[h] + H], F.Identity, bias=T.bd[:, 1:2], scale=BIG) for h in range(2)]
     a = [op("v", [a[h], tz[2 + h]], "tt", T.ind[:, e[h]:e[h] + H], T.pz[:, 1024 + 512 * h:1024 + 512 * h + H], T.th[:, e[h]:e[h] + H], A.is_ge) for h in range(2)]
     tc = op("v", [a[1], tzb], "scan", T.c1[:], T.ind[:], T.zb[:], 0.0, A.add, A.add)
-    send([tc], "a0", "c", [(T.c1[:, P - 1:P], T.hl[:, 8 * me:8 * me + 1])] * 3)
-    for m in range(3):
-        tac = op("a", [tc, tb16h], "act", T.ja[:, P * m:P * m + P], T.c1[:], F.Sign, bias=T.b16h[:, m:m + 1], scale=-1.0,
-                 accum_out=T.ac[:, m:m + 1])
-    j3 = op("v", [tc, tb16], "ts", T.jv[:, 0:P], T.c1[:], T.b16[:, 3:4], None, A.is_le)
-    j4 = op("v", [tc], "ts", T.jv[:, P:2 * P], T.c1[:], T.b16[:, 4:5], None, A.is_le)
-    op("v", [j3], "red", T.lq[:, 3:4], T.jv[:, 0:P], X, A.add)
-    op("v", [j4], "red", T.lq[:, 4:5], T.jv[:, P:2 * P], X, A.add)
-    tl = op("v", [tac, tlz], "ts", T.lq[:, 0:3], T.ac[:, 0:3], 0.5, P / 2.0, A.mult, A.add)
-    for x in range(3):
+    send_all([tc], "a0", lambda x: (T.c1[:, P - 1:P], T.hl[:, 8 * me:8 * me + 1]))
+    op("g", [], "iota", T.ce[:, 0:1], [[0, 1]], 0, 0, **fl)
+    op("g", [], "iota", T.bb2[:], [[0, 32]], 0, 0, **fl)
+    op("g", [], "iota", T.lst[:, 5:8], [[0, 3]], 0, 0, **fl)
+    op("g", [], "iota", T.a5[:, 0:1], [[0, 1]], WHOLE, 0, **fl)
+    op("g", [], "iota", T.mrun[:], [[0, 4]], -4 * RUN, 0, **fl)
+    tsg0 = op("g", [], "iota", T.io64[:], [[-RUN, 4], [16, 16]], -RUN, 1, **fl)
+    tl = lists(T.c1, P, 16, T.b16, T.b16h, [tc, tb16h], T.jv, T.ja, T.ac, T.lq)
+
+    def spread(q, x, qd):
         d = order[x]
-        for qd in range(4):
-            out, src = T.lw[32 * qd:32 * qd + 32, 6 * x:6 * x + 6], T.lq[32 * d:32 * d + 32, 0:6]
-            if qd < 2:
-                tv = op("v", [tl], "copy", out, src)
-            else:
-                ta = op("a", [tl], "act", out, src, F.Copy)
-    toff = op("v", [tv, ta], "copy", T.off1[:, 0:18], T.lw[:, 0:18])
-    tpc = op("v", [toff] + tq, "copy", T.s1q[:, 0:272].bitcast(u32), T.xq[:, 0:P + 2].bitcast(u32).indirect(T.off1[:, 0:17]))
-    tps = op("a", [toff] + tq, "act", T.s1s[:, 0:272], T.xs[:, 0:P + 2].indirect(T.off1[:, 0:17]), F.Copy)
-    o0 = CAPP * me
+        return move(q, [tl], T.lw[32 * qd:32 * qd + 32, 6 * x:6 * x + 6], T.lq[32 * d:32 * d + 32, 0:6])
+    for qd in range(3):
+        tv = spread("v", 0, qd)
+    ta = spread("a", 0, 3)
+    spread("v", 1, 0)
+    toff = op("v", [tv, ta], "copy", T.off1[:, 0:6], T.lw[:, 0:6])
+    for x, qd in ((1, 2), (1, 3), (2, 2)):
+        ta = spread("a", x, qd)
+    tpc = op("v", [toff] + tq, "copy", T.s1q[:, 0:CAPP].bitcast(u32), T.xq[:, 0:P + 2].bitcast(u32).indirect(T.off1[:, 0:C5]))
+    tps = op("a", [toff] + tq, "act", T.s1s[:, 0:CAPP], T.xs[:, 0:P + 2].indirect(T.off1[:, 0:C5]), F.Copy)
+    for x, qd in ((1, 1), (2, 0), (2, 1), (2, 3)):
+        tv = spread("v", x, qd)
+    toff = op("v", [tv, ta], "copy", T.off1[:, 6:18], T.lw[:, 6:18])
+    tpc2 = op("v", [toff], "copy", T.s1q[:, 96:272].bitcast(u32), T.xq[:, 0:P + 2].bitcast(u32).indirect(T.off1[:, 6:17]))
+    tps2 = op("a", [toff], "act", T.s1s[:, 96:272], T.xs[:, 0:P + 2].indirect(T.off1[:, 6:17]), F.Copy)
+
+    def codes1(x):
+        return (T.s1q[:, 96 * x:96 * x + CAPP].bitcast(u8), T.l1q[:, o0:o0 + CAPP].bitcast(u8))
+
+    def planes1(x):
+        return (T.s1s[:, 96 * x:96 * x + CAPP], T.l1s[:, o0:o0 + CAPP])
+    send([tpc], "a1", [0], codes1)
+    send([tps], "a1", [0], planes1)
+    send([tpc2], "a1", [1, 2], codes1)
+    send([tps2], "a1", [1, 2], planes1)
     for qd in range(4):
-        tv = op("v", [tl], "copy", T.lw[32 * qd:32 * qd + 32, 18:24], T.lq[32 * me:32 * me + 32, 0:6])
+        tv = spread("v", 3, qd)
     tho = op("v", [tc], "copy", T.hl[:, 8 * me:8 * me + 1], T.c1[:, P - 1:P])
     toff = op("v", [tv], "copy", T.off1[:, 18:24], T.lw[:, 18:24])
     toc = op("v", [toff], "copy", T.l1q[:, o0:o0 + CAPP].bitcast(u32), T.xq[:, 0:P + 2].bitcast(u32).indirect(T.off1[:, 18:18 + C5]))
     tos = op("a", [toff], "act", T.l1s[:, o0:o0 + CAPP], T.xs[:, 0:P + 2].indirect(T.off1[:, 18:18 + C5]), F.Copy)
-    send([tpc], "a1", "c", [(T.s1q[:, 96 * x:96 * x + CAPP].bitcast(u8), T.l1q[:, o0:o0 + CAPP].bitcast(u8)) for x in range(3)])
-    send([tps], "a1", "p", [(T.s1s[:, 96 * x:96 * x + CAPP], T.l1s[:, o0:o0 + CAPP]) for x in range(3)])
     a = op("v", [tmk], "tt", T.tm[:], T.lw[:], T.mk[:], A.mult)
     for x in range(4):
         b = op("v", [a], "red", T.rn[:, x:x + 1], T.tm[:, 6 * x:6 * x + 6], X, A.add)
     tm1 = op("v", [b], "ts", T.m1s[:], T.rn[:], float(P * me), None, A.add)
-    send([tm1], "m1r", "c", [(T.m1s[:, x:x + 1], T.m1l[:, 8 * me:8 * me + 1]) for x in range(3)])
+    send_all([tm1], "m1r", lambda x: (T.m1s[:, x:x + 1], T.m1l[:, 8 * me:8 * me + 1]))
     tm1o = op("v", [tm1], "copy", T.m1l[:, 8 * me:8 * me + 1], T.m1s[:, 3:4])
-    am1 = ("m1r", into["c"])
+    am1 = ("m1r", into)
     for s in range(N):
         tdn = dma("s", [am1, tm1o], "dn", T.nr16[0:1, CAPP * s:CAPP * s + CAPP], T.m1l[0:CAPP, 8 * s:8 * s + 1])
 
-    twq = op("v", [tw], "qmx", T.wq[:], T.ws[:], T.wt[:])
-    a = op("v", [], "ts", T.q5[:], T.ph5[:], -SHIFT, None, A.add)
-    tsb8 = op("v", [], "ts", T.sb8[:], T.b16[:, 0:2], float(8 * (me + 1) + 8192), 0.125, A.add, A.mult)
-    a = op("v", [a, tb16], "ts", T.qb2[:], T.b16[:, 0:5], 4.0, T.q5[:, 0:1], A.mult, A.add)
-    td1 = op("v", [], "set", T.d1[:, 128:S1], 0.0)
-    tq2 = op("v", [a], "ts", T.qb2h[:], T.qb2[:], 0.5, None, A.add)
-    op("v", [], "set", T.ce[:], 0.0)
-    op("v", [], "set", T.gs[:], 0.0)
-    op("v", [], "set", T.a5[:], 0.0)
-    op("v", [], "set", T.l2[:, 5:8], 0.0)
+    op("g", [], "iota", T.d1[:, 128:S1], [[0, S1 - 128]], 0, 0, **fl)
+    op("g", [], "iota", T.nr[:], [[0, S1 + 8]], 0, 0, **fl)
+    op("g", [], "iota", T.xn[:], [[0, S2]], 0, 0, **fl)
+    tsg = op("g", [], "iota", T.nw[:], [[0, S2 + 8]], -1, 0, **fl)
+    a = op("v", [tp5], "ts", T.q5[:], T.ph5[:], -SHIFT, None, A.add)
     op("v", [], "set", T.v2s[:], 0)
     op("v", [], "set", T.v2l[:, 8 * me:8 * me + 8], 0)
-    op("v", [], "set", T.xn[:], 0.0)
-    op("v", [], "set", T.nr[:], 0.0)
-    op("v", [], "set", T.nw[:], -1.0)
-    op("v", [], "set", T.bb2[:], 0.0)
-    tset = op("v", [], "set", T.km[:], MARK)
-    aa0 = ("a0", into["c"])
+    heads(T.jv2, S1, 64)
+    a = op("v", [a], "ts", T.qb2[:], T.b16[:, 0:5], 4.0, T.q5[:, 0:1], A.mult, A.add)
+    tsv = op("v", [a], "ts", T.qb2h[:], T.qb2[:], 0.5, None, A.add)
+    a = op("a", [tb16], "act", T.sg8[:], T.b16[:, 0:1], F.Sign, bias=-7.5)
+    b = op("a", [], "act", T.rm4[:], T.b16[:, 0:1], F.Identity, bias=-4.0)
+    for m in range(2):
+        c = op("a", [tsv], "act", T.qn[:, m:m + 1], T.q5[:], F.Identity, bias=4096.0 - SHIFT + 0.5 * (order[2 * m] + order[2 * m + 1]), scale=-1.0)
+    op("a", [a, b], "act", T.p7f[:], T.sg8[:], F.Identity, bias=T.rm4[:, 0:1], scale=-4.0)
+    for m in range(2):
+        op("a", [c], "act", T.sbx[:, m:m + 1], T.sg8[:], F.Identity, bias=T.qn[:, m:m + 1], scale=0.5 * (order[2 * m + 1] - order[2 * m]))
+    a = op("a", [tr16], "act", T.wb[:], T.r16[:], F.Identity, bias=float(WHOLE), scale=-1.0)
+    tsa = op("a", [a, tsg0], "act", T.bw[:], T.io64[:], F.Identity, bias=T.wb[:, 0:1])
+    aa0 = ("a0", into)
     for qd in range(4):
         a = op("v", [aa0, tho], "ts", T.cn1[32 * qd:32 * qd + 32, :], T.hl[32 * me:32 * me + 32, 0:32:8], 1.0, None, A.min)
-    a = op("v", [a, tset, tzf], "scan", T.ce[:, 1:5], T.cn1[:], T.zf[:, 0:4], 0.0, A.add, A.add)
+    a = op("v", [a, tsg0], "scan", T.ce[:, 1:5], T.cn1[:], T.zf[:, 0:4], 0.0, A.add, A.add)
+    twq = op("v", [tw], "qmx", T.wq[:], T.ws[:], T.wt[:])
     a = op("v", [a], "tt", T.fi[:], T.cn1[:], T.ce[:, 0:4], A.is_gt)
     a = op("v", [a, tmo], "tt", T.fo[:], T.fi[:], T.mo[:], A.mult)
     a = op("v", [a], "tt", T.ov[:], T.fo[:, 0:4:2], T.fo[:, 1:4:2], A.add)
     op("v", [a], "ts", T.th0[:], T.ov[:, 0:1], 4.0 * BIG, None, A.mult)
     tov = op("v", [], "ts", T.th1[:], T.ov[:, 1:2], 4096.0, 0.5 - 256, A.mult, A.add)
 
-    aa1 = ("a1", into["c"] + into["p"])
+    aa1 = ("a1", 2 * into)
     first = {0: 0, 1: 128, 2: 192}
     tmm, tmf, tof, tdg = {}, {}, {}, {}
 
     def slots(out, b, i0, i1):
         k0 = first[b]
         return op("t", [aa1, toc, tos, tdz], "mm", out, T.l1q[:, k0:k0 + 128], T.l1s[:, k0:k0 + 128], T.l1q[:, i0:i1], T.l1s[:, i0:i1], True, True)
-    for b in (1, 2, 0):
+    for b in (2, 1, 0):
         tmm[b] = slots(T.pmm[:, 512 * b:512 * b + 128], b, first[b], first[b] + 128)
-    for b in (1, 2):
+    for b in (2, 1):
         tmf[b] = slots(T.pz[:, 512 * b + 512:512 * b + 512 + first[b]], b, 0, first[b])
-    tdb, tmb = {}, {}
+    tdb, tmb, tnt = {}, {}, {}
 
     def diagonal(b):
         tdb[b] = op("v", [tmm[b], tid], "tt", T.db[:, 128 * b:128 * b + 128], T.pmm[:, 512 * b:512 * b + 128], T.idm[:], A.mult)
 
-    def signs(b):
+    def mask(b):
         tmb[b] = op("v", [tmm[b], tng, tn0], "tt", T.mb[:, 128 * b:128 * b + 128], T.pmm[:, 512 * b:512 * b + 128], T.nega[:] if b else T.neg0[:], A.add)
-        a = op("v", [tdb[b]], "red", T.nt[:, b:b + 1], T.db[:, 128 * b:128 * b + 128], X, A.add)
-        if b == 0:
-            tdg[0] = op("v", [tmb[0]], "red", T.mx0[:], T.mb[:, 0:128], X, A.max)
-            return
-        tdg[b] = op("a", [a, tmb[b]], "act", T.jf[:, 128 * b:128 * b + 128], T.mb[:, 128 * b:128 * b + 128], F.Sign, bias=T.nt[:, b:b + 1],
+
+    def limit(b, q):
+        nt, db = T.nt[:, b:b + 1], T.db[:, 128 * b:128 * b + 128]
+        if q == "v":
+            tnt[b] = op("v", [tdb[b]], "red", nt, db, X, A.add)
+        else:
+            tnt[b] = op("a", [tdb[b]], "act", T.jf[:, 704 + 128 * b:832 + 128 * b], db, F.Copy, accum_out=nt)
+
+    def own(b):
+        tdg[b] = op("a", [tnt[b], tmb[b]], "act", T.jf[:, 128 * b:128 * b + 128], T.mb[:, 128 * b:128 * b + 128], F.Sign, bias=T.nt[:, b:b + 1],
                     accum_out=T.acc[:, b:b + 1])
+
+    def earlier(b):
         j0 = 256 + 128 * b
-        tof[b] = op("a", [a, tmf[b]], "act", T.jf[:, j0:j0 + first[b]], T.pz[:, 512 * b + 512:512 * b + 512 + first[b]], F.Sign,
+        tof[b] = op("a", [tnt[b], tmf[b]], "act", T.jf[:, j0:j0 + first[b]], T.pz[:, 512 * b + 512:512 * b + 512 + first[b]], F.Sign,
                     bias=T.nt[:, b:b + 1], accum_out=T.acc[:, 4 + b:5 + b])
-    diagonal(1)
     diagonal(2)
-    signs(1)
-    signs(2)
+    diagonal(1)
+    limit(2, "a")
+    mask(2)
+    earlier(2)
+    own(2)
+    limit(1, "v")
+    mask(1)
+    earlier(1)
+    own(1)
     diagonal(0)
-    signs(0)
+    mask(0)
+    limit(0, "v")
+    tdg[0] = op("v", [tmb[0]], "red", T.mx0[:], T.mb[:, 0:128], X, A.max)
+    c = op("v", [tof[2], tdg[2], tsa], "ts", T.bb2[:, 0:1], T.acc[:, 2:3], T.acc[:, 6:7], 0.5 - S1, A.add, A.is_le)
+    a = op("v", [tdg[0], tov, tnt[0]], "ts", T.ev[:, 0:1], T.mx0[:], T.nt[:, 0:1], T.th0[:, 0:1], A.add, A.is_lt)
     b = op("v", [tof[1], tdg[1], tov], "ts", T.ev[:, 1:2], T.acc[:, 1:2], T.acc[:, 5:6], T.th1[:, 0:1], A.add, A.is_le)
-    a = op("v", [tdg[0], tov], "ts", T.ev[:, 0:1], T.mx0[:], T.nt[:, 0:1], T.th0[:, 0:1], A.add, A.is_lt)
-    c = op("v", [tof[2], tdg[2], tset], "ts", T.bb2[:, 0:1], T.acc[:, 2:3], T.acc[:, 6:7], 0.5 - S1, A.add, A.is_le)
-    a = op("v", [a, b, tset], "ts", T.bb[:], T.km[:], T.ev[:, 0:1], T.ev[:, 1:2], A.mult, A.add)
     tb2 = op("v", [c], "tr", T.bt2[:], T.bb2[:])
+    a = op("v", [a, b], "ts", T.bb[:], T.km[:], T.ev[:, 0:1], T.ev[:, 1:2], A.mult, A.add)
     tbt = op("v", [a], "tr", T.bt[:], T.bb[:])
     for i in (2, 3):
-        tb = op("g", [tb2], "bc", T.rv[:, 64 + 32 * i:96 + 32 * i], T.bt2[32 * i:32 * i + 1, 0:32], 128)
-    for i in range(4):
+        op("g", [tb2], "bc", T.rv[:, 64 + 32 * i:96 + 32 * i], T.bt2[32 * i:32 * i + 1, 0:32], 128)
+    tb = op("g", [tbt], "bc", T.rv[:, 0:32], T.bt[0:1, 0:32], 128)
+    for i in (1, 2, 3):
         for qd in range(4):
             out, src = T.rv[32 * qd:32 * qd + 32, 32 * i:32 * i + 32], T.bt[32 * i:32 * i + 32, 0:32]
-            if qd < 2:
-                tv = op("v", [tbt], "copy", out, src)
+            if qd < 2 or (qd, i) == (2, 3):
+                tv = move("v", [tbt], out, src)
             else:
-                ta = op("a", [tbt], "act", out, src, F.Copy)
+                ta = move("a", [tbt], out, src)
     trv = [tb, tv, ta]
-    tcs = op("v", trv, "red", T.cs[:], T.rv[:], X, A.add)
-    send([tcs], "a2", "c", [(T.cs[:], T.cn2[:, 4 * me:4 * me + 1])] * 3)
-    aa2 = ("a2", into["c"])
+    tcs = op("a", trv, "act", T.rvj[:], T.rv[:], F.Copy, accum_out=T.cs[:])
+    send_all([tcs], "a2", lambda x: (T.cs[:], T.cn2[:, 4 * me:4 * me + 1]))
+    aa2 = ("a2", into)
 
-    op("a", trv, "act", T.d0[:, 0:128], T.rv[:, 0:128], F.Copy)
-    ta = op("a", [], "act", T.d0[:, 256:S1], T.rv[:, 128:192], F.Copy)
-    op("v", [], "ts", T.d1[:, 0:128], T.rv[:, 0:128], 1.0, -1.0, A.is_ge, A.mult)
-    a = op("v", [], "ts", T.d0[:, 128:256], T.rv[:, 0:128], 1.0, None, A.is_ge)
-    tc2 = op("v", [a, ta, td1], "scan", T.c2[:], T.d0[:], T.d1[:], -SHIFT, A.add, A.add)
-    for m in range(3):
-        tac = op("a", [tc2, tq2], "act", T.ja2[:, S1 * m:S1 * m + S1], T.c2[:], F.Sign, bias=T.qb2h[:, m:m + 1], scale=-1.0,
-                 accum_out=T.ac2[:, m:m + 1])
-    tcn = op("v", [tcs], "copy", T.cn2[:, 4 * me:4 * me + 1], T.cs[:])
-    j3 = op("v", [tc2, tq2], "ts", T.jv2[:, 0:S1], T.c2[:], T.qb2[:, 3:4], None, A.is_le)
-    j4 = op("v", [], "ts", T.jv2[:, S1:2 * S1], T.c2[:], T.qb2[:, 4:5], None, A.is_le)
-    op("v", [j3], "red", T.l2[:, 3:4], T.jv2[:, 0:S1], X, A.add)
-    op("v", [j4], "red", T.l2[:, 4:5], T.jv2[:, S1:2 * S1], X, A.add)
-    tl = op("v", [tac], "ts", T.l2[:, 0:3], T.ac2[:, 0:3], 0.5, S1 / 2.0, A.mult, A.add)
-    for d in range(4):
+    ta = op("a", [], "act", T.d0[:, 0:128], T.rv[:, 0:128], F.Copy)
+    tcn = op("a", [tcs], "act", T.cn2[:, 4 * me:4 * me + 1], T.cs[:], F.Copy)
+    op("v", trv, "ts", T.d1[:, 0:128], T.rv[:, 0:128], 1.0, -1.0, A.is_ge, A.mult)
+    op("v", [], "ts", T.d0[:, 128:256], T.rv[:, 0:128], 1.0, None, A.is_ge)
+    a = op("v", [], "copy", T.d0[:, 256:S1], T.rv[:, 128:192])
+    tc2 = op("v", [a, ta, tsg], "scan", T.c2[:], T.d0[:], T.d1[:], -SHIFT, A.add, A.add)
+    tl = lists(T.c2, S1, 64, T.qb2, T.qb2h, [tc2, tsv], T.jv2, T.ja2, T.ac2, T.lst)
+    for x in (1, 2, 3):
         for qd in range(4):
-            out, src = T.lst[32 * qd:32 * qd + 32, 8 * d:8 * d + 8], T.l2[32 * d:32 * d + 32, 0:8]
-            if qd < 2:
-                tv = op("v", [tl], "copy", out, src)
+            d = (qd + x) % 4
+            out, src = T.lst[32 * qd:32 * qd + 32, 8 * x:8 * x + 8], T.lst[32 * d:32 * d + 32, 0:8]
+            if qd < 2 or (qd, x) == (2, 3):
+                tv = move("v", [tl], out, src)
             else:
-                ta = op("a", [tl], "act", out, src, F.Copy)
+                ta = move("a", [tl], out, src)
     tlst = [tv, ta]
+    tnr = op("a", [tdn, tsg], "act", T.nr[0:1, 0:S1], T.nr16[0:1, 0:S1], F.Copy)
 
-    def places():
-        return op("v", [aa2, tcn], "scan", T.gs[:, 1:5], T.cn2[:, 0:16:4], T.zf[:, 0:4], 0.0, A.add, A.add)
     if me == 0:
-        a = op("v", [tsb8], "ts", T.ei[:], T.sb8[:], 0.0, 8.0, A.subtract, A.mult)
+        a = op("v", [tsa], "copy", T.ei[:], T.sbx[:])
+    elif me == 1:
+        a = op("v", [aa2, tsa], "ts", T.ei[:], T.sbx[:], T.cn2[:, 0:1], None, A.subtract)
+    elif me == 2:
+        a = op("v", [aa2, tsa], "ts", T.ei[:], T.sbx[:], T.cn2[:, 0:1], T.cn2[:, 4:5], A.subtract, A.subtract)
     else:
-        tgs = places()
-        a = op("v", [tgs, tsb8], "ts", T.ei[:], T.sb8[:], T.gs[:, me:me + 1], 8.0, A.subtract, A.mult)
-    a = op("v", [a], "ts", T.seli[:], T.ei[:], 31, None, A.bitwise_and)
-    a = op("v", [a], "copy", T.sel[:], T.seli[:])
+        a = op("v", [aa2, tsa], "ts", T.ef[:], T.sbx[:], T.cn2[:, 0:1], T.cn2[:, 4:5], A.subtract, A.subtract)
+        a = op("v", [a], "ts", T.ei[:], T.ef[:], T.cn2[:, 8:9], None, A.subtract)
+    a = op("v", [a], "ts", T.seli[:], T.ei[:], 3, None, A.bitwise_and)
+    a = op("v", [a], "ts", T.sel[:], T.seli[:], 8.0, T.p7f[:, 0:1], A.mult, A.add)
     to2 = op("v", [a] + tlst, "copy", T.off2[:], T.lst[:, 0:32].indirect(T.sel[:]))
+    tpc, tps = [], []
     for x in range(3):
-        tpc = op("v", [to2, tdz], "copy", T.s2q[:, 80 * x:80 * x + 80].bitcast(u32), T.l1q[:, 0:S1 + 2].bitcast(u32).indirect(T.off2[:, 8 * x:8 * x + C5]))
-        tps = op("a", [to2, tdz, aa1], "act", T.s2s[:, 80 * x:80 * x + 80], T.l1s[:, 0:S1 + 2].indirect(T.off2[:, 8 * x:8 * x + C5]), F.Copy)
-    send([tpc], "a3", "c", [(T.s2q[:, 80 * x:80 * x + 80].bitcast(u8), T.l2q[:, o0:o0 + CAPP].bitcast(u8)) for x in range(3)])
-    send([tps], "a3", "p", [(T.s2s[:, 80 * x:80 * x + 80], T.l2s[:, o0:o0 + CAPP]) for x in range(3)])
-    tnr = op("v", [tdn, tset], "copy", T.nr[0:1, 0:S1], T.nr16[0:1, 0:S1])
+        tpc.append(op("v", [to2, tdz], "copy", T.s2q[:, 80 * x:80 * x + 80].bitcast(u32), T.l1q[:, 0:S1 + 2].bitcast(u32).indirect(T.off2[:, 8 * x:8 * x + C5])))
+        tps.append(op("a", [to2, tdz, aa1], "act", T.s2s[:, 80 * x:80 * x + 80], T.l1s[:, 0:S1 + 2].indirect(T.off2[:, 8 * x:8 * x + C5]), F.Copy))
+
+    def codes2(x):
+        return (T.s2q[:, 80 * x:80 * x + 80].bitcast(u8), T.l2q[:, o2:o2 + CAPP].bitcast(u8))
+
+    def planes2(x):
+        return (T.s2s[:, 80 * x:80 * x + 80], T.l2s[:, o2:o2 + CAPP])
+    send(tpc[:1], "a3", [0], codes2)
+    send(tps[:1], "a3", [0], planes2)
+    send(tpc[1:], "a3", [1, 2], codes2)
+    send(tps[1:], "a3", [1, 2], planes2)
     for x in range(3):
-        tgn = op("a", [tnr], "act", T.ng[:, 96 * x:96 * x + 96], T.nr[:].indirect(T.off2[:, 8 * x:8 * x + 6]), F.Copy)
-    toc = op("v", [], "copy", T.l2q[:, o0:o0 + CAPP].bitcast(u32), T.l1q[:, 0:S1 + 2].bitcast(u32).indirect(T.off2[:, 24:24 + C5]))
-    tos = op("a", [], "act", T.l2s[:, o0:o0 + CAPP], T.l1s[:, 0:S1 + 2].indirect(T.off2[:, 24:24 + C5]), F.Copy)
-    tno = op("a", [tset], "act", T.nw[:, o0:o0 + CAPP], T.nr[:].indirect(T.off2[:, 24:24 + C5]), F.Copy)
+        tgn = op("a", [tnr], "act", T.ng[:, RUN * x:RUN * x + RUN], T.nr[:].indirect(T.off2[:, 8 * x:8 * x + 6]), F.Copy)
+    toc = op("v", [], "copy", T.l2q[:, o2:o2 + CAPP].bitcast(u32), T.l1q[:, 0:S1 + 2].bitcast(u32).indirect(T.off2[:, 24:24 + C5]))
+    tos = op("a", [], "act", T.l2s[:, o2:o2 + CAPP], T.l1s[:, 0:S1 + 2].indirect(T.off2[:, 24:24 + C5]), F.Copy)
+    tno = op("a", [tsg], "act", T.nw[:, o2:o2 + CAPP], T.nr[:].indirect(T.off2[:, 24:24 + C5]), F.Copy)
+
+    a = op("v", [aa2, tcn, tsa], "scan", T.gs[:, 1:5], T.cn2[:, 0:16:4], T.mrun[:], 1.5 - me, A.add, A.add)
+    ta5 = op("v", [a], "ts", T.a5[:, 1:5], T.gs[:, 1:5], 0.25, float(WHOLE), A.mult, A.add)
+    twe = op("v", [ta5], "tt", T.we[:], T.a5[:, 0:4], T.a5[:, 1:5], A.subtract)
     a = op("v", [tgn], "tr", T.ngt[:], T.ng[0:32, :])
     for i in range(3):
-        tv2 = op("v", [a, tset], "copy", T.v2s[32 * i:32 * i + 32, 0:3], T.ngt[0:32, 32 * i:288:96])
-    send([tv2], "m2r", "c", [(T.v2s[:, x:x + 1], T.v2l[:, 8 * me:8 * me + 1]) for x in range(3)])
-
-    if me == 0:
-        tgs = places()
-    a = op("v", [tgs], "ts", T.ai[:], T.gs[:, 1:5], 3.25 - me, None, A.add)
-    a = op("v", [a], "ts", T.aj[:], T.ai[:], 2, None, A.logical_shift_right)
-    a = op("v", [a, tset], "copy", T.a5[:, 1:5], T.aj[:])
-    a = op("v", [a], "tt", T.wd[:], T.a5[:, 0:4], T.a5[:, 1:5], A.subtract)
-    a = op("v", [a], "ts", T.we[:], T.wd[:], float(CAPP), None, A.add)
+        tv2 = op("v", [a, tsv], "copy", T.v2s[32 * i:32 * i + 32, 0:3], T.ngt[0:32, 32 * i:S2 - RUN:RUN])
+    send_all([tv2], "m2r", lambda x: (T.v2s[:, x:x + 1], T.v2l[:, 8 * me:8 * me + 1]))
     for d in range(4):
-        b = op("v", [a], "ts", T.tp[:, 16 * d:16 * d + 16], T.b16[:], T.a5[:, d + 1:d + 2], T.we[:, d:d + 1], A.is_ge, A.mult)
+        b = op("v", [twe], "ts", T.tp[:, 16 * d:16 * d + 16], T.bw[:, 16 * d:16 * d + 16], T.a5[:, d + 1:d + 2], T.we[:, d:d + 1], A.is_ge, A.mult)
     a = op("v", [b], "tt", T.ta[:, 0:32], T.tp[:, 0:32], T.tp[:, 32:64], A.add)
     b = op("v", [a], "tt", T.ta[:, 32:48], T.ta[:, 0:16], T.ta[:, 16:32], A.add)
     a = op("v", [b], "tt", T.ta[:, 48:64], T.ta[:, 32:48], T.b16[:], A.add)
-    tfin = op("v", [a], "ts", T.fin[:], T.ta[:, 48:64], float(S1), None, A.min)
+    tfin = op("v", [a], "ts", T.fin[:], T.ta[:, 48:64], float(S2), None, A.min)
 
-    aa3 = ("a3", into["c"] + into["p"])
+    aa3 = ("a3", 2 * into)
     tfc, tfs, ty = [], [], []
     for h in range(2):
-        tfc.append(op("v", [aa3, tfin, toc, tdz], "copy", T.oq[:, H * h:H * h + H].bitcast(u32), T.l2q[:, 0:S1 + 2].bitcast(u32).indirect(T.fin[:, 8 * h:8 * h + 8])))
-        tfs.append(op("a", [aa3, tfin, tos, tdz], "act", T.os_[:, H * h:H * h + H], T.l2s[:, 0:S1 + 2].indirect(T.fin[:, 8 * h:8 * h + 8]), F.Copy))
+        tfc.append(op("v", [aa3, tfin, toc, tdz], "copy", T.oq[:, H * h:H * h + H].bitcast(u32), T.l2q[:, 0:S2 + 2].bitcast(u32).indirect(T.fin[:, 8 * h:8 * h + 8])))
+        tfs.append(op("a", [aa3, tfin, tos, tdz], "act", T.os_[:, H * h:H * h + H], T.l2s[:, 0:S2 + 2].indirect(T.fin[:, 8 * h:8 * h + 8]), F.Copy))
         ty.append(op("t", [tfc[h], tfs[h], twq], "mm", T.pz[:, 512 * h:512 * h + H], T.wq[:], T.ws[:], T.oq[:, H * h:H * h + H], T.os_[:, H * h:H * h + H], True, True))
     b0 = op("a", [ty[0]], "act", T.yb[:, 0:H], T.pz[:, 0:H], F.Copy)
     b1 = op("a", [ty[1]], "act", T.yb[:, H:P], T.pz[:, 512:512 + H], F.Copy)
     for h in range(2):
         dma("s", [tfc[h]], "so", T.oc[:, 4 * H * h:4 * H * h + 4 * H], T.oq[:, H * h:H * h + H].bitcast(u8))
-    dma("s", [b0], "so", T.y[:, 0:H], T.yb[:, 0:H])
-    dma("s", [b1], "so", T.y[:, H:P], T.yb[:, H:P])
     for i in range(4):
         dma("s", tfs, "so", T.osc[4 * i:4 * i + 4, :], T.os_[32 * i:32 * i + 4, :])
-    a = op("v", [("m2r", into["c"]), tset], "copy", T.xn[:, 0:128:32], T.v2l[:, 0:32:8])
-    a = op("v", [a], "tr", T.xnt[:], T.xn[:])
-    for d in order[:3]:
-        for i in range(3):
-            w = min(32, CAPP - 32 * i)
-            out, src = T.nw[0:1, CAPP * d + 32 * i:CAPP * d + 32 * i + w], T.xnt[32 * i:32 * i + 1, 32 * d:32 * d + w]
-            if i == 1:
-                ta = op("a", [a, tset], "act", out, src, F.Copy)
-            else:
-                tv = op("v", [a, tset], "copy", out, src)
-    a = op("v", [tv, ta, tno, tfin], "copy", T.nout[:, 0:H], T.nw[:].indirect(T.fin[:, 0:8]))
-    b = op("a", [tv, ta, tno, tfin], "act", T.nout[:, H:P], T.nw[:].indirect(T.fin[:, 8:16]), F.Copy)
+    dma("s", [b0], "so", T.y[:, 0:H], T.yb[:, 0:H])
+    dma("s", [b1], "so", T.y[:, H:P], T.yb[:, H:P])
+    for i in range(3):
+        a = op("v", [("m2r", into), tsv, tsg], "copy", T.xn[:, 32 * i:S2:RUN], T.v2l[32 * i:32 * i + 32, 0:32:8])
+    for c0, c1 in ((0, o2), (o2 + RUN, S2)):
+        if c1 > c0:
+            tnw = op("v", [a], "tr", T.nw[0:32, c0:c1], T.xn[:, c0:c1])
+    a = op("v", [tnw, tno, tfin], "copy", T.nout[:, 0:H], T.nw[:].indirect(T.fin[:, 0:8]))
+    b = op("a", [tnw, tno, tfin], "act", T.nout[:, H:P], T.nw[:].indirect(T.fin[:, 8:16]), F.Copy)
     dma("s", [a, b], "so", T.num[:], T.nout[0:1, :])
 
     wait("g", [(s, v) for s, v in count.items()])
-    wait("g", [am1, aa0, aa1, aa2, aa3, ("m2r", into["c"])])
+    wait("g", [am1, aa0, aa1, aa2, aa3, ("m2r", into)])

from concourse.bass import DstId, RemoteDMATransfer
from concourse.mybir import dt, AluOpType, AxisListType, ActivationFunctionType

N, P, CAPP = 4, 256, 80
H = P // 2
S1 = N * CAPP
C5 = CAPP // 16
RUN = 96
S2 = N * RUN
BIG = 1.0e29
TINY = 1.0e-36
MARK = 1.0 - 2.0 ** -14
SHIFT = 64.0
WHOLE = 3 * 2 ** 22

CODE = "float8_e4m3fn_x4"
SCRATCH = {
    "xt": ("sbuf", [128, 4 * P + 8], "bfloat16"),
    "plt": ("sbuf", [128, 512], "bfloat16"),
    "wt": ("sbuf", [128, 512], "bfloat16"),
    "xq": ("sbuf", [128, P + 2], CODE), "xs": ("sbuf", [128, P + 2], "uint8"),
    "plq": ("sbuf", [128, 128], CODE), "pls": ("sbuf", [128, 128], "uint8"),
    "prq": ("sbuf", [128, 256], CODE), "prs": ("sbuf", [128, 256], "uint8"),
    "wq": ("sbuf", [128, 128], CODE), "ws": ("sbuf", [128, 128], "uint8"),
    "s1q": ("sbuf", [128, 272], CODE), "s1s": ("sbuf", [128, 272], "uint8"),
    "l1q": ("sbuf", [128, S1 + 8], CODE), "l1s": ("sbuf", [128, S1 + 8], "uint8"),
    "s2q": ("sbuf", [128, 240], CODE), "s2s": ("sbuf", [128, 240], "uint8"),
    "l2q": ("sbuf", [128, S2 + 8], CODE), "l2s": ("sbuf", [128, S2 + 8], "uint8"),
    "oq": ("sbuf", [128, P], CODE), "os_": ("sbuf", [128, P], "uint8"),
    "ploff": ("sbuf", [128, 16], "uint16"),
    "pn": ("sbuf", [128, 1], "int32"), "pm16": ("sbuf", [128, 1], "int32"), "ph5": ("sbuf", [128, 1], "int32"),
    "r16": ("sbuf", [128, 1], "float32"), "q5": ("sbuf", [128, 1], "float32"),
    "io16": ("sbuf", [128, 16], "float32"), "b16": ("sbuf", [128, 16], "float32"), "b16h": ("sbuf", [128, 8], "float32"),
    "qb2": ("sbuf", [128, 5], "float32"), "qb2h": ("sbuf", [128, 5], "float32"),
    "sbx": ("sbuf", [128, 2], "float32"), "qn": ("sbuf", [128, 2], "float32"), "sg8": ("sbuf", [128, 1], "float32"),
    "rm4": ("sbuf", [128, 1], "float32"), "p7f": ("sbuf", [128, 1], "float32"),
    "bd": ("sbuf", [128, 4], "float32"),
    "idm": ("sbuf", [128, 128], "float32"), "zf": ("sbuf", [128, 128], "float32"),
    "nega": ("sbuf", [128, 128], "float32"), "neg0": ("sbuf", [128, 128], "float32"),
    "one": ("sbuf", [128, 24], "float32"), "mka": ("sbuf", [128, 24], "float32"), "mk": ("sbuf", [128, 24], "float32"),
    "mo": ("sbuf", [128, 4], "float32"),
    "zb": ("sbuf", [128, P], "bfloat16"), "km": ("sbuf", [128, 32], "float32"),
    "mrun": ("sbuf", [128, 4], "float32"), "io64": ("sbuf", [128, 64], "float32"), "wb": ("sbuf", [128, 1], "float32"),
    "bw": ("sbuf", [128, 64], "float32"),
    "t0": ("sbuf", [128, P], "bfloat16"), "th": ("sbuf", [128, P], "float32"), "ind": ("sbuf", [128, P], "bfloat16"),
    "c1": ("sbuf", [128, P], "bfloat16"), "jv": ("sbuf", [128, 2 * P], "bfloat16"), "ja": ("sbuf", [128, 3 * P], "bfloat16"),
    "ac": ("sbuf", [128, 8], "float32"), "lq": ("sbuf", [128, 8], "float32"), "lw": ("sbuf", [128, 24], "float32"),
    "off1": ("sbuf", [128, 24], "uint16"),
    "tm": ("sbuf", [128, 24], "float32"), "rn": ("sbuf", [128, 4], "float32"),
    "hl": ("sbuf", [128, 32], "bfloat16"), "m1s": ("sbuf", [128, 4], "uint16"), "m1l": ("sbuf", [128, 32], "uint16"),
    "db": ("sbuf", [128, 384], "float32"), "mb": ("sbuf", [128, 384], "float32"), "mx0": ("sbuf", [128, 1], "float32"),
    "nt": ("sbuf", [128, 4], "float32"), "acc": ("sbuf", [128, 8], "float32"), "jf": ("sbuf", [128, 1088], "bfloat16"),
    "cn1": ("sbuf", [128, 4], "float32"), "ce": ("sbuf", [128, 8], "float32"), "fi": ("sbuf", [128, 4], "float32"),
    "fo": ("sbuf", [128, 4], "float32"), "ov": ("sbuf", [128, 2], "float32"), "th0": ("sbuf", [128, 1], "float32"),
    "th1": ("sbuf", [128, 1], "float32"),
    "ev": ("sbuf", [128, 4], "float32"), "bb": ("sbuf", [128, 32], "float32"), "bt": ("sbuf", [128, 32], "float32"),
    "bb2": ("sbuf", [128, 32], "float32"), "bt2": ("sbuf", [128, 32], "float32"),
    "rv": ("sbuf", [128, 192], "float32"), "rvj": ("sbuf", [128, 192], "float32"), "cs": ("sbuf", [128, 1], "float32"),
    "cn2": ("sbuf", [128, 16], "float32"),
    "d0": ("sbuf", [128, S1], "bfloat16"), "d1": ("sbuf", [128, S1], "bfloat16"), "c2": ("sbuf", [128, S1], "bfloat16"),
    "jv2": ("sbuf", [128, 2 * S1], "bfloat16"), "ja2": ("sbuf", [128, 3 * S1], "bfloat16"),
    "ac2": ("sbuf", [128, 8], "float32"), "lst": ("sbuf", [128, 32], "float32"),
    "ef": ("sbuf", [128, 2], "float32"), "ei": ("sbuf", [128, 2], "int32"),
    "seli": ("sbuf", [128, 2], "int32"), "sel": ("sbuf", [128, 2], "uint16"), "off2": ("sbuf", [128, 32], "uint16"),
    "gs": ("sbuf", [128, 8], "float32"), "a5": ("sbuf", [128, 8], "float32"),
    "we": ("sbuf", [128, 4], "float32"), "tp": ("sbuf", [128, 64], "float32"),
    "ta": ("sbuf", [128, 64], "float32"), "fin": ("sbuf", [128, 16], "uint16"),
    "yb": ("sbuf", [128, P], "float32"),
    "nr16": ("sbuf", [1, S1], "uint16"), "nr": ("sbuf", [128, S1 + 8], "float32"), "ng": ("sbuf", [128, S2 - RUN], "float32"),
    "ngt": ("sbuf", [32, S2 - RUN], "float32"), "v2s": ("sbuf", [128, 4], "uint16"), "v2l": ("sbuf", [128, 32], "uint16"),
    "xn": ("sbuf", [32, S2], "float32"), "nw": ("sbuf", [128, S2 + 8], "float32"),
    "nout": ("sbuf", [128, P], "float32"),
    "pz": ("psum", [128, 2048], "float32"), "pmm": ("psum", [128, 1536], "float32"),
}
SEMAPHORES = ["vs", "sa", "ts", "gc", "dpl", "dx0", "dx1", "dw", "dz", "dn", "so", "ls", "a0", "a1", "m1r", "a2", "a3", "m2r"]


def far(topo, src, dst):
    a, b = topo.chip(src), topo.chip(dst)
    return a != b and not topo.mates(a, b) and not topo.same_plane(a, b)


def others(topo, r, cores):
    o = [(r + 1 + x) % N for x in range(N - 1)]
    return sorted(o, key=lambda d: not far(topo, cores[r], cores[d]))


def split(topo, src, dsts):
    el = topo.engines(src, dsts[0])
    for d in dsts[1:]:
        el = [e for e in el if e in topo.engines(src, d)]
    q = len(el) // len(dsts)
    return [el[i * q:(i + 1) * q] for i in range(len(dsts))]


def bits(es):
    m = 0
    for e in es:
        m |= 1 << e
    return m


def rank_program(g, core, T, topo):
    me = T.rank_of(core)
    if me is None:
        return
    A, F, X = AluOpType, ActivationFunctionType, AxisListType.X
    u8, u32 = dt.uint8, dt.uint32
    eng = {"v": g.vector, "a": g.scalar, "t": g.tensor, "g": g, "s": g.sync}
    own_sem = {"v": "vs", "a": "sa", "t": "ts", "g": "gc"}
    calls = {"copy": g.vector.tensor_copy, "tt": g.vector.tensor_tensor, "ts": g.vector.tensor_scalar,
             "red": g.vector.tensor_reduce, "scan": g.vector.tensor_tensor_scan, "tr": g.vector.transpose,
             "set": g.vector.memset, "qmx": g.vector.quantize_mx, "act": g.scalar.activation,
             "mm": g.tensor.matmul_mx, "iota": g.iota, "aff": g.affine_select, "bc": g.partition_broadcast}
    count, seen = {}, {}

    def wait(q, deps):
        need = {}
        for s, v in deps:
            need[s] = max(v, need.get(s, 0))
        for s, v in need.items():
            if seen.get((q, s), 0) < v:
                eng[q].wait_ge(T.sem[s], v)
                seen[(q, s)] = v

    def op(q, deps, name, *args, **kw):
        wait(q, deps)
        s = own_sem[q]
        calls[name](*args, **kw).then_inc(T.sem[s], 1)
        count[s] = count.get(s, 0) + 1
        return (s, count[s])

    def dma(q, deps, s, out, in_):
        wait(q, deps)
        eng[q].dma_start(out, in_).then_inc(T.sem[s], 16)
        count[s] = count.get(s, 0) + 16
        return (s, count[s])

    def move(q, deps, out, src):
        return op(q, deps, "copy", out, src) if q == "v" else op(q, deps, "act", out, src, F.Copy)

    order = others(topo, me, T.cores) + [me]
    o0, o2 = CAPP * me, RUN * me
    into = 0
    for r in range(N):
        if r != me:
            o = others(topo, r, T.cores)
            for grp in (o[:1], o[1:]):
                if me in grp:
                    into += len(split(topo, T.cores[r], [T.cores[d] for d in grp])[grp.index(me)])

    def send(deps, sem, xs, piece):
        wait("g", deps)
        dst = [T.cores[order[x]] for x in xs]
        tr = []
        for x, d, es in zip(xs, dst, split(topo, core, dst)):
            rid, pid = topo.addr(d)[:2]
            p_src, p_dst = piece(x)
            tr.append(RemoteDMATransfer(dst_ids=[DstId(rid=rid, pnc=pid)], dma_engine_mask=bits(es),
                                        remote_sem=T.sem[sem], src=p_src, dst=p_dst))
            count["ls"] = count.get("ls", 0) + len(es)
        g.remote_dma_fused(tr, local_sem=T.sem.ls)

    def send_all(deps, sem, piece):
        send(deps, sem, [0], piece)
        send(deps, sem, [1, 2], piece)

    tpl = dma("s", [], "dpl", T.plt[:, 0:8], T.pl[:, 0:8])
    tx1 = dma("a", [], "dx1", T.xt[:, 4 * H:8 * H], T.x[:, 4 * H:8 * H])
    tx0 = dma("s", [], "dx0", T.xt[:, 0:4 * H], T.x[:, 0:4 * H])
    tw = dma("s", [], "dw", T.wt[:], T.w[:])

    fl = {"allow_small_or_imprecise_dtypes": True}
    tpn = op("g", [], "iota", T.pn[:], [[0, 1]], 0, 1)
    tio = op("g", [], "iota", T.io16[:], [[16, 16]], 0, 1, **fl)
    tzf = op("g", [], "iota", T.zf[:], [[0, 128]], 0, 0, **fl)
    ton = op("g", [], "iota", T.one[:], [[0, 24]], 1, 0, **fl)
    tz4 = op("v", [], "set", T.plt[:, 12:512], 0.0)
    tz5 = op("v", [], "set", T.xt[:, 4 * P:4 * P + 8], 0.0)
    a = op("v", [tpn], "ts", T.pm16[:], T.pn[:], 112, None, A.bitwise_and)
    tp5 = op("v", [], "ts", T.ph5[:], T.pn[:], 5, None, A.logical_shift_right)
    op("v", [], "set", T.ploff[:, 0:8], 0)
    op("v", [], "set", T.ploff[:, 8:12], 1)
    tpo = op("v", [], "set", T.ploff[:, 12:16], 2)
    tr16 = op("v", [a], "copy", T.r16[:], T.pm16[:])
    for qd in range(4):
        op("v", [], "set", T.bd[32 * qd:32 * qd + 32, 0:1], float(qd & 1))
    tb16 = op("v", [tr16, tio], "ts", T.b16[:], T.io16[:], T.r16[:, 0:1], None, A.subtract)
    op("v", [], "set", T.bd[0:64, 1:2], 0.0)
    tbd = op("v", [], "set", T.bd[64:128, 1:2], TINY)
    tzb = op("v", [], "set", T.zb[:], 0.0)
    op("a", [tzf], "act", T.km[:], T.zf[:, 0:32], F.Identity, bias=MARK)
    a = op("g", [ton], "aff", T.mka[:], T.one[:], [[0, 4], [-16, 6]], A.is_ge, 0.0, 0, 1)
    tmk = op("g", [a], "aff", T.mk[:], T.mka[:], [[0, 4], [16, 6]], A.is_ge, 0.0, 15, -1)
    op("g", [], "aff", T.mo[:, 0:2], T.one[:, 0:2], [[-CAPP, 2]], A.is_equal, 0.0, 0, 1)
    tmo = op("g", [], "aff", T.mo[:, 2:4], T.one[:, 0:2], [[-CAPP, 2]], A.is_equal, 0.0, 128 - 2 * CAPP, 1)
    tid = op("g", [tzf], "aff", T.idm[:], T.zf[:], [[-1, 128]], A.not_equal, -0.9375, 0, 1)
    tng = op("g", [tzf], "aff", T.nega[:], T.zf[:], [[-1, 128]], A.is_gt, -BIG, 0, 1)
    tn0 = op("g", [tng], "aff", T.neg0[:], T.nega[:], [[1, 128]], A.is_gt, BIG, 0, 1)

    a = op("v", [tpl], "ts", T.plt[:, 8:12], T.plt[:, 4:8], -1.0, None, A.mult)
    tplq = op("v", [a, tz4], "qmx", T.plq[:], T.pls[:], T.plt[:])

    def plane(b):
        c = op("v", [tplq, tpo], "copy", T.prq[:, 128 * b:128 * b + 128].bitcast(u32), T.plq[:].bitcast(u32).indirect(T.ploff[:, 8 * b:8 * b + 8]))
        s = op("a", [tplq, tpo], "act", T.prs[:, 128 * b:128 * b + 128], T.pls[:].indirect(T.ploff[:, 8 * b:8 * b + 8]), F.Copy)
        return [c, s]
    tpr = [plane(0)]
    tq = [op("v", [tx0], "qmx", T.xq[:, 0:H], T.xs[:, 0:H], T.xt[:, 0:4 * H]),
          op("v", [tx1, tz5], "qmx", T.xq[:, H:P + 2], T.xs[:, H:P + 2], T.xt[:, 4 * H:4 * P + 8])]
    tpr.append(plane(1))
    for d, e in (("l1", S1), ("l2", S2)):
        dma("s", tq, "dz", T[d + "q"][:, e:e + 2].bitcast(u8), T.xq[:, P:P + 2].bitcast(u8))
        tdz = dma("s", tq, "dz", T[d + "s"][:, e:e + 2], T.xs[:, P:P + 2])
    tz = []
    for b in range(2):
        for h in range(2):
            c0 = 512 * (2 * b + h)
            tz.append(op("t", tpr[b] + [tq[h]], "mm", T.pz[:, c0:c0 + H], T.prq[:, 128 * b:128 * b + 128], T.prs[:, 128 * b:128 * b + 128],
                         T.xq[:, H * h:H * h + H], T.xs[:, H * h:H * h + H], True, True))

    def heads(jv, sz, step):
        for k, m in enumerate((1, 3)):
            t = op("v", [], "set", jv[:, sz * k + sz - step * m:sz * k + sz - step * m + 1], float(step * m))
        return t

    def lists(c, sz, step, off, offh, deps, jv, ja, ac, lq):
        n = [sz - step * m for m in range(C5)]
        t, tacc = {}, {}
        for k, m in enumerate((1, 3)):
            t[m] = op("v", deps, "ts", jv[:, sz * k:sz * k + n[m]], c[:, sz - n[m]:sz], off[:, m:m + 1], None, A.is_le)
        for k, m in enumerate((0, 2, 4)):
            tacc[m] = op("a", deps, "act", ja[:, sz * k:sz * k + n[m]], c[:, sz - n[m]:sz], F.Sign, bias=offh[:, m:m + 1], scale=-1.0,
                         accum_out=ac[:, m:m + 1])
        for k, m in enumerate((1, 3)):
            op("v", [t[m]], "red", lq[:, m:m + 1], jv[:, sz * k:sz * k + n[m] + 1], X, A.add)
        for m in (0, 2, 4):
            r = op("v", [tacc[m]], "ts", lq[:, m:m + 1], ac[:, m:m + 1], 0.5, 0.5 * (n[m] + 2 * step * m), A.mult, A.add)
        return r

    e = [H * h for h in range(2)]
    a = [op("v", [tz[h], tbd], "ts", T.t0[:, e[h]:e[h] + H], T.pz[:, 512 * h:512 * h + H], 0.0, T.bd[:, 0:1], A.is_lt, A.not_equal) for h in range(2)]
    heads(T.jv, P, 16)
    op("v", [], "set", T.lq[:, 5:6], 0.0)
    tb16h = op("v", [tb16], "ts", T.b16h[:], T.b16[:, 0:8], 0.5, None, A.add)
    a = [op("a", [a[h], tbd], "act", T.th[:, e[h]:e[h] + H], T.t0[:, e[h]:e[h] + H], F.Identity, bias=T.bd[:, 1:2], scale=BIG) for h in range(2)]
    a = [op("v", [a[h], tz[2 + h]], "tt", T.ind[:, e[h]:e[h] + H], T.pz[:, 1024 + 512 * h:1024 + 512 * h + H], T.th[:, e[h]:e[h] + H], A.is_ge) for h in range(2)]
    tc = op("v", [a[1], tzb], "scan", T.c1[:], T.ind[:], T.zb[:], 0.0, A.add, A.add)
    send_all([tc], "a0", lambda x: (T.c1[:, P - 1:P], T.hl[:, 8 * me:8 * me + 1]))
    op("g", [], "iota", T.ce[:, 0:1], [[0, 1]], 0, 0, **fl)
    op("g", [], "iota", T.bb2[:], [[0, 32]], 0, 0, **fl)
    op("g", [], "iota", T.lst[:, 5:8], [[0, 3]], 0, 0, **fl)
    op("g", [], "iota", T.a5[:, 0:1], [[0, 1]], WHOLE, 0, **fl)
    op("g", [], "iota", T.mrun[:], [[0, 4]], -4 * RUN, 0, **fl)
    tsg0 = op("g", [], "iota", T.io64[:], [[-RUN, 4], [16, 16]], -RUN, 1, **fl)
    tl = lists(T.c1, P, 16, T.b16, T.b16h, [tc, tb16h], T.jv, T.ja, T.ac, T.lq)

    def spread(q, x, qd):
        d = order[x]
        return move(q, [tl], T.lw[32 * qd:32 * qd + 32, 6 * x:6 * x + 6], T.lq[32 * d:32 * d + 32, 0:6])
    for qd in range(3):
        tv = spread("v", 0, qd)
    ta = spread("a", 0, 3)
    spread("v", 1, 0)
    toff = op("v", [tv, ta], "copy", T.off1[:, 0:6], T.lw[:, 0:6])
    for x, qd in ((1, 2), (1, 3), (2, 2)):
        ta = spread("a", x, qd)
    tpc = op("v", [toff] + tq, "copy", T.s1q[:, 0:CAPP].bitcast(u32), T.xq[:, 0:P + 2].bitcast(u32).indirect(T.off1[:, 0:C5]))
    tps = op("a", [toff] + tq, "act", T.s1s[:, 0:CAPP], T.xs[:, 0:P + 2].indirect(T.off1[:, 0:C5]), F.Copy)
    for x, qd in ((1, 1), (2, 0), (2, 1), (2, 3)):
        tv = spread("v", x, qd)
    toff = op("v", [tv, ta], "copy", T.off1[:, 6:18], T.lw[:, 6:18])
    tpc2 = op("v", [toff], "copy", T.s1q[:, 96:272].bitcast(u32), T.xq[:, 0:P + 2].bitcast(u32).indirect(T.off1[:, 6:17]))
    tps2 = op("a", [toff], "act", T.s1s[:, 96:272], T.xs[:, 0:P + 2].indirect(T.off1[:, 6:17]), F.Copy)

    def codes1(x):
        return (T.s1q[:, 96 * x:96 * x + CAPP].bitcast(u8), T.l1q[:, o0:o0 + CAPP].bitcast(u8))

    def planes1(x):
        return (T.s1s[:, 96 * x:96 * x + CAPP], T.l1s[:, o0:o0 + CAPP])
    send([tpc], "a1", [0], codes1)
    send([tps], "a1", [0], planes1)
    send([tpc2], "a1", [1, 2], codes1)
    send([tps2], "a1", [1, 2], planes1)
    for qd in range(4):
        tv = spread("v", 3, qd)
    tho = op("v", [tc], "copy", T.hl[:, 8 * me:8 * me + 1], T.c1[:, P - 1:P])
    toff = op("v", [tv], "copy", T.off1[:, 18:24], T.lw[:, 18:24])
    toc = op("v", [toff], "copy", T.l1q[:, o0:o0 + CAPP].bitcast(u32), T.xq[:, 0:P + 2].bitcast(u32).indirect(T.off1[:, 18:18 + C5]))
    tos = op("a", [toff], "act", T.l1s[:, o0:o0 + CAPP], T.xs[:, 0:P + 2].indirect(T.off1[:, 18:18 + C5]), F.Copy)
    a = op("v", [tmk], "tt", T.tm[:], T.lw[:], T.mk[:], A.mult)
    for x in range(4):
        b = op("v", [a], "red", T.rn[:, x:x + 1], T.tm[:, 6 * x:6 * x + 6], X, A.add)
    tm1 = op("v", [b], "ts", T.m1s[:], T.rn[:], float(P * me), None, A.add)
    send_all([tm1], "m1r", lambda x: (T.m1s[:, x:x + 1], T.m1l[:, 8 * me:8 * me + 1]))
    tm1o = op("v", [tm1], "copy", T.m1l[:, 8 * me:8 * me + 1], T.m1s[:, 3:4])
    am1 = ("m1r", into)
    for s in range(N):
        tdn = dma("s", [am1, tm1o], "dn", T.nr16[0:1, CAPP * s:CAPP * s + CAPP], T.m1l[0:CAPP, 8 * s:8 * s + 1])

    op("g", [], "iota", T.d1[:, 128:S1], [[0, S1 - 128]], 0, 0, **fl)
    op("g", [], "iota", T.nr[:], [[0, S1 + 8]], 0, 0, **fl)
    op("g", [], "iota", T.xn[:], [[0, S2]], 0, 0, **fl)
    tsg = op("g", [], "iota", T.nw[:], [[0, S2 + 8]], -1, 0, **fl)
    a = op("v", [tp5], "ts", T.q5[:], T.ph5[:], -SHIFT, None, A.add)
    op("v", [], "set", T.v2s[:], 0)
    op("v", [], "set", T.v2l[:, 8 * me:8 * me + 8], 0)
    heads(T.jv2, S1, 64)
    a = op("v", [a], "ts", T.qb2[:], T.b16[:, 0:5], 4.0, T.q5[:, 0:1], A.mult, A.add)
    tsv = op("v", [a], "ts", T.qb2h[:], T.qb2[:], 0.5, None, A.add)
    a = op("a", [tb16], "act", T.sg8[:], T.b16[:, 0:1], F.Sign, bias=-7.5)
    b = op("a", [], "act", T.rm4[:], T.b16[:, 0:1], F.Identity, bias=-4.0)
    for m in range(2):
        c = op("a", [tsv], "act", T.qn[:, m:m + 1], T.q5[:], F.Identity, bias=4096.0 - SHIFT + 0.5 * (order[2 * m] + order[2 * m + 1]), scale=-1.0)
    op("a", [a, b], "act", T.p7f[:], T.sg8[:], F.Identity, bias=T.rm4[:, 0:1], scale=-4.0)
    for m in range(2):
        op("a", [c], "act", T.sbx[:, m:m + 1], T.sg8[:], F.Identity, bias=T.qn[:, m:m + 1], scale=0.5 * (order[2 * m + 1] - order[2 * m]))
    a = op("a", [tr16], "act", T.wb[:], T.r16[:], F.Identity, bias=float(WHOLE), scale=-1.0)
    tsa = op("a", [a, tsg0], "act", T.bw[:], T.io64[:], F.Identity, bias=T.wb[:, 0:1])
    aa0 = ("a0", into)
    for qd in range(4):
        a = op("v", [aa0, tho], "ts", T.cn1[32 * qd:32 * qd + 32, :], T.hl[32 * me:32 * me + 32, 0:32:8], 1.0, None, A.min)
    a = op("v", [a, tsg0], "scan", T.ce[:, 1:5], T.cn1[:], T.zf[:, 0:4], 0.0, A.add, A.add)
    twq = op("v", [tw], "qmx", T.wq[:], T.ws[:], T.wt[:])
    a = op("v", [a], "tt", T.fi[:], T.cn1[:], T.ce[:, 0:4], A.is_gt)
    a = op("v", [a, tmo], "tt", T.fo[:], T.fi[:], T.mo[:], A.mult)
    a = op("v", [a], "tt", T.ov[:], T.fo[:, 0:4:2], T.fo[:, 1:4:2], A.add)
    op("v", [a], "ts", T.th0[:], T.ov[:, 0:1], 4.0 * BIG, None, A.mult)
    tov = op("v", [], "ts", T.th1[:], T.ov[:, 1:2], 4096.0, 0.5 - 256, A.mult, A.add)

    aa1 = ("a1", 2 * into)
    first = {0: 0, 1: 128, 2: 192}
    tmm, tmf, tof, tdg = {}, {}, {}, {}

    def slots(out, b, i0, i1):
        k0 = first[b]
        return op("t", [aa1, toc, tos, tdz], "mm", out, T.l1q[:, k0:k0 + 128], T.l1s[:, k0:k0 + 128], T.l1q[:, i0:i1], T.l1s[:, i0:i1], True, True)
    for b in (2, 1, 0):
        tmm[b] = slots(T.pmm[:, 512 * b:512 * b + 128], b, first[b], first[b] + 128)
    for b in (2, 1):
        tmf[b] = slots(T.pz[:, 512 * b + 512:512 * b + 512 + first[b]], b, 0, first[b])
    tdb, tmb, tnt = {}, {}, {}

    def diagonal(b):
        tdb[b] = op("v", [tmm[b], tid], "tt", T.db[:, 128 * b:128 * b + 128], T.pmm[:, 512 * b:512 * b + 128], T.idm[:], A.mult)

    def mask(b):
        tmb[b] = op("v", [tmm[b], tng, tn0], "tt", T.mb[:, 128 * b:128 * b + 128], T.pmm[:, 512 * b:512 * b + 128], T.nega[:] if b else T.neg0[:], A.add)

    def limit(b, q):
        nt, db = T.nt[:, b:b + 1], T.db[:, 128 * b:128 * b + 128]
        if q == "v":
            tnt[b] = op("v", [tdb[b]], "red", nt, db, X, A.add)
        else:
            tnt[b] = op("a", [tdb[b]], "act", T.jf[:, 704 + 128 * b:832 + 128 * b], db, F.Copy, accum_out=nt)

    def own(b):
        tdg[b] = op("a", [tnt[b], tmb[b]], "act", T.jf[:, 128 * b:128 * b + 128], T.mb[:, 128 * b:128 * b + 128], F.Sign, bias=T.nt[:, b:b + 1],
                    accum_out=T.acc[:, b:b + 1])

    def earlier(b):
        j0 = 256 + 128 * b
        tof[b] = op("a", [tnt[b], tmf[b]], "act", T.jf[:, j0:j0 + first[b]], T.pz[:, 512 * b + 512:512 * b + 512 + first[b]], F.Sign,
                    bias=T.nt[:, b:b + 1], accum_out=T.acc[:, 4 + b:5 + b])
    diagonal(2)
    diagonal(1)
    limit(2, "a")
    mask(2)
    earlier(2)
    own(2)
    limit(1, "v")
    mask(1)
    earlier(1)
    own(1)
    diagonal(0)
    mask(0)
    limit(0, "v")
    tdg[0] = op("v", [tmb[0]], "red", T.mx0[:], T.mb[:, 0:128], X, A.max)
    c = op("v", [tof[2], tdg[2], tsa], "ts", T.bb2[:, 0:1], T.acc[:, 2:3], T.acc[:, 6:7], 0.5 - S1, A.add, A.is_le)
    a = op("v", [tdg[0], tov, tnt[0]], "ts", T.ev[:, 0:1], T.mx0[:], T.nt[:, 0:1], T.th0[:, 0:1], A.add, A.is_lt)
    b = op("v", [tof[1], tdg[1], tov], "ts", T.ev[:, 1:2], T.acc[:, 1:2], T.acc[:, 5:6], T.th1[:, 0:1], A.add, A.is_le)
    tb2 = op("v", [c], "tr", T.bt2[:], T.bb2[:])
    a = op("v", [a, b], "ts", T.bb[:], T.km[:], T.ev[:, 0:1], T.ev[:, 1:2], A.mult, A.add)
    tbt = op("v", [a], "tr", T.bt[:], T.bb[:])
    for i in (2, 3):
        op("g", [tb2], "bc", T.rv[:, 64 + 32 * i:96 + 32 * i], T.bt2[32 * i:32 * i + 1, 0:32], 128)
    tb = op("g", [tbt], "bc", T.rv[:, 0:32], T.bt[0:1, 0:32], 128)
    for i in (1, 2, 3):
        for qd in range(4):
            out, src = T.rv[32 * qd:32 * qd + 32, 32 * i:32 * i + 32], T.bt[32 * i:32 * i + 32, 0:32]
            if qd < 2 or (qd, i) == (2, 3):
                tv = move("v", [tbt], out, src)
            else:
                ta = move("a", [tbt], out, src)
    trv = [tb, tv, ta]
    tcs = op("a", trv, "act", T.rvj[:], T.rv[:], F.Copy, accum_out=T.cs[:])
    send_all([tcs], "a2", lambda x: (T.cs[:], T.cn2[:, 4 * me:4 * me + 1]))
    aa2 = ("a2", into)

    ta = op("a", [], "act", T.d0[:, 0:128], T.rv[:, 0:128], F.Copy)
    tcn = op("a", [tcs], "act", T.cn2[:, 4 * me:4 * me + 1], T.cs[:], F.Copy)
    op("v", trv, "ts", T.d1[:, 0:128], T.rv[:, 0:128], 1.0, -1.0, A.is_ge, A.mult)
    op("v", [], "ts", T.d0[:, 128:256], T.rv[:, 0:128], 1.0, None, A.is_ge)
    a = op("v", [], "copy", T.d0[:, 256:S1], T.rv[:, 128:192])
    tc2 = op("v", [a, ta, tsg], "scan", T.c2[:], T.d0[:], T.d1[:], -SHIFT, A.add, A.add)
    tl = lists(T.c2, S1, 64, T.qb2, T.qb2h, [tc2, tsv], T.jv2, T.ja2, T.ac2, T.lst)
    for x in (1, 2, 3):
        for qd in range(4):
            d = (qd + x) % 4
            out, src = T.lst[32 * qd:32 * qd + 32, 8 * x:8 * x + 8], T.lst[32 * d:32 * d + 32, 0:8]
            if qd < 2 or (qd, x) == (2, 3):
                tv = move("v", [tl], out, src)
            else:
                ta = move("a", [tl], out, src)
    tlst = [tv, ta]
    tnr = op("a", [tdn, tsg], "act", T.nr[0:1, 0:S1], T.nr16[0:1, 0:S1], F.Copy)

    if me == 0:
        a = op("v", [tsa], "copy", T.ei[:], T.sbx[:])
    elif me == 1:
        a = op("v", [aa2, tsa], "ts", T.ei[:], T.sbx[:], T.cn2[:, 0:1], None, A.subtract)
    elif me == 2:
        a = op("v", [aa2, tsa], "ts", T.ei[:], T.sbx[:], T.cn2[:, 0:1], T.cn2[:, 4:5], A.subtract, A.subtract)
    else:
        a = op("v", [aa2, tsa], "ts", T.ef[:], T.sbx[:], T.cn2[:, 0:1], T.cn2[:, 4:5], A.subtract, A.subtract)
        a = op("v", [a], "ts", T.ei[:], T.ef[:], T.cn2[:, 8:9], None, A.subtract)
    a = op("v", [a], "ts", T.seli[:], T.ei[:], 3, None, A.bitwise_and)
    a = op("v", [a], "ts", T.sel[:], T.seli[:], 8.0, T.p7f[:, 0:1], A.mult, A.add)
    to2 = op("v", [a] + tlst, "copy", T.off2[:], T.lst[:, 0:32].indirect(T.sel[:]))
    tpc, tps = [], []
    for x in range(3):
        tpc.append(op("v", [to2, tdz], "copy", T.s2q[:, 80 * x:80 * x + 80].bitcast(u32), T.l1q[:, 0:S1 + 2].bitcast(u32).indirect(T.off2[:, 8 * x:8 * x + C5])))
        tps.append(op("a", [to2, tdz, aa1], "act", T.s2s[:, 80 * x:80 * x + 80], T.l1s[:, 0:S1 + 2].indirect(T.off2[:, 8 * x:8 * x + C5]), F.Copy))

    def codes2(x):
        return (T.s2q[:, 80 * x:80 * x + 80].bitcast(u8), T.l2q[:, o2:o2 + CAPP].bitcast(u8))

    def planes2(x):
        return (T.s2s[:, 80 * x:80 * x + 80], T.l2s[:, o2:o2 + CAPP])
    send(tpc[:1], "a3", [0], codes2)
    send(tps[:1], "a3", [0], planes2)
    send(tpc[1:], "a3", [1, 2], codes2)
    send(tps[1:], "a3", [1, 2], planes2)
    for x in range(3):
        tgn = op("a", [tnr], "act", T.ng[:, RUN * x:RUN * x + RUN], T.nr[:].indirect(T.off2[:, 8 * x:8 * x + 6]), F.Copy)
    toc = op("v", [], "copy", T.l2q[:, o2:o2 + CAPP].bitcast(u32), T.l1q[:, 0:S1 + 2].bitcast(u32).indirect(T.off2[:, 24:24 + C5]))
    tos = op("a", [], "act", T.l2s[:, o2:o2 + CAPP], T.l1s[:, 0:S1 + 2].indirect(T.off2[:, 24:24 + C5]), F.Copy)
    tno = op("a", [tsg], "act", T.nw[:, o2:o2 + CAPP], T.nr[:].indirect(T.off2[:, 24:24 + C5]), F.Copy)

    a = op("v", [aa2, tcn, tsa], "scan", T.gs[:, 1:5], T.cn2[:, 0:16:4], T.mrun[:], 1.5 - me, A.add, A.add)
    ta5 = op("v", [a], "ts", T.a5[:, 1:5], T.gs[:, 1:5], 0.25, float(WHOLE), A.mult, A.add)
    twe = op("v", [ta5], "tt", T.we[:], T.a5[:, 0:4], T.a5[:, 1:5], A.subtract)
    a = op("v", [tgn], "tr", T.ngt[:], T.ng[0:32, :])
    for i in range(3):
        tv2 = op("v", [a, tsv], "copy", T.v2s[32 * i:32 * i + 32, 0:3], T.ngt[0:32, 32 * i:S2 - RUN:RUN])
    send_all([tv2], "m2r", lambda x: (T.v2s[:, x:x + 1], T.v2l[:, 8 * me:8 * me + 1]))
    for d in range(4):
        b = op("v", [twe], "ts", T.tp[:, 16 * d:16 * d + 16], T.bw[:, 16 * d:16 * d + 16], T.a5[:, d + 1:d + 2], T.we[:, d:d + 1], A.is_ge, A.mult)
    a = op("v", [b], "tt", T.ta[:, 0:32], T.tp[:, 0:32], T.tp[:, 32:64], A.add)
    b = op("v", [a], "tt", T.ta[:, 32:48], T.ta[:, 0:16], T.ta[:, 16:32], A.add)
    a = op("v", [b], "tt", T.ta[:, 48:64], T.ta[:, 32:48], T.b16[:], A.add)
    tfin = op("v", [a], "ts", T.fin[:], T.ta[:, 48:64], float(S2), None, A.min)

    aa3 = ("a3", 2 * into)
    tfc, tfs, ty = [], [], []
    for h in range(2):
        tfc.append(op("v", [aa3, tfin, toc, tdz], "copy", T.oq[:, H * h:H * h + H].bitcast(u32), T.l2q[:, 0:S2 + 2].bitcast(u32).indirect(T.fin[:, 8 * h:8 * h + 8])))
        tfs.append(op("a", [aa3, tfin, tos, tdz], "act", T.os_[:, H * h:H * h + H], T.l2s[:, 0:S2 + 2].indirect(T.fin[:, 8 * h:8 * h + 8]), F.Copy))
        ty.append(op("t", [tfc[h], tfs[h], twq], "mm", T.pz[:, 512 * h:512 * h + H], T.wq[:], T.ws[:], T.oq[:, H * h:H * h + H], T.os_[:, H * h:H * h + H], True, True))
    b0 = op("a", [ty[0]], "act", T.yb[:, 0:H], T.pz[:, 0:H], F.Copy)
    b1 = op("a", [ty[1]], "act", T.yb[:, H:P], T.pz[:, 512:512 + H], F.Copy)
    for h in range(2):
        dma("s", [tfc[h]], "so", T.oc[:, 4 * H * h:4 * H * h + 4 * H], T.oq[:, H * h:H * h + H].bitcast(u8))
    for i in range(4):
        dma("s", tfs, "so", T.osc[4 * i:4 * i + 4, :], T.os_[32 * i:32 * i + 4, :])
    dma("s", [b0], "so", T.y[:, 0:H], T.yb[:, 0:H])
    dma("s", [b1], "so", T.y[:, H:P], T.yb[:, H:P])
    for i in range(3):
        a = op("v", [("m2r", into), tsv, tsg], "copy", T.xn[:, 32 * i:S2:RUN], T.v2l[32 * i:32 * i + 32, 0:32:8])
    for c0, c1 in ((0, o2), (o2 + RUN, S2)):
        if c1 > c0:
            tnw = op("v", [a], "tr", T.nw[0:32, c0:c1], T.xn[:, c0:c1])
    a = op("v", [tnw, tno, tfin], "copy", T.nout[:, 0:H], T.nw[:].indirect(T.fin[:, 0:8]))
    b = op("a", [tnw, tno, tfin], "act", T.nout[:, H:P], T.nw[:].indirect(T.fin[:, 8:16]), F.Copy)
    dma("s", [a, b], "so", T.num[:], T.nout[0:1, :])

    wait("g", [(s, v) for s, v in count.items()])
    wait("g", [am1, aa0, aa1, aa2, aa3, ("m2r", into)])
